import numpy as np, ml_dtypes
CORES = [48,51,52,55]
N = 4
import mx_ref
BF = ml_dtypes.bfloat16
def tile(rs):
    return np.stack(rs, axis=2).reshape(128, -1).astype(BF)
def pick(q, e):
    c = np.concatenate([q[0].reshape(128, -1, 4), np.zeros((128, 1, 4), np.uint8)], axis=1); s = np.concatenate([q[1], np.ones((16, 1), np.uint8)], axis=1)
    return (np.ascontiguousarray(c[:, e].reshape(128, -1)), np.ascontiguousarray(s[:, e]))
def join(*qs):
    return (np.concatenate([q[0] for q in qs], axis=1), np.concatenate([q[1] for q in qs], axis=1))
def put(q, e, v):
    c, s = q[0].reshape(128, -1, 4).copy(), q[1].copy(); c[:, e] = v[0].reshape(128, -1, 4); s[:, e] = v[1]
    return (c.reshape(128, -1), s)
def pk(c, s):
    return (np.ascontiguousarray(c), mx_ref.live(s))
def emit(q):
    return q[0], q[1]
def packed(v, rng):
    q = [mx_ref.quantize(np.ascontiguousarray(v[r])) for r in range(N)]
    return np.stack([a for a, b in q]), np.stack([mx_ref.plane(b, rng) for a, b in q])
def values_of_codes():
    e, c = np.zeros((128, 128, 4), np.float32), np.zeros((128, 2, 4), np.uint8)
    e[np.arange(128), np.arange(128), 0] = 1
    c[:127, :, 0] = np.arange(256).reshape(2, 128).T[:127]
    return mx_ref.matmul(mx_ref.quantize(e.reshape(128, 512).astype(BF)), (c.reshape(128, 8), np.full((16, 2), 127, np.uint8))).T.reshape(-1).astype(np.float64)
CODE_VALUE, SCALE_VALUE = values_of_codes(), 2.0 ** (np.arange(256) - 127.0)
def decode(q):
    return (CODE_VALUE[q[0]].reshape(16, 8, -1, 4) * SCALE_VALUE[q[1]][:, None, :, None] + 0.0).reshape(128, -1).astype(np.float32)
def f(rng, *shape):
    return mx_ref.flush((rng.standard_normal(shape, dtype=np.float32) * np.exp2(rng.integers(-2, 3, shape[:-1] + (1,)))).astype(BF))
def wide(rng, *shape, cols=0):
    v = rng.standard_normal(shape, dtype=np.float32) * np.exp2(rng.integers(-12, 13, shape)).astype(np.float32)
    if cols: v *= np.repeat(np.exp2(rng.integers(-cols, cols + 1, shape[:-2] + (1, shape[-1] // 4))) * (rng.random(shape[:-2] + (1, shape[-1] // 4)) > 0.0625), 4, axis=-1).astype(np.float32)
    return mx_ref.flush(v.astype(BF))
C, H = 320, 160
MASK = [1, 2, 3]
def numbers_of(rng):
    return {"x": np.array(f(rng, N, 128, 4 * C)), "u": np.array(f(rng, N, 128, 512)), "v": np.array(f(rng, N, 128, 512))}
def weights(rng, w):
    c, s = packed(np.ascontiguousarray(w).reshape(N, 128, 2048), rng)
    return {"wc": c, "ws": s}
def layers(rng, still=[], pairs=False):
    w = np.array(f(rng, N, 128, 2048)).reshape(N, 8, 16, 4, 8, 16, 4)
    for i in still:
        w[:, :, i] = 0
        w[:, :, :, :, :, i] = 0
    if pairs:
        w[:, :, :, :, :, 8:] = 0
        for g in range(8):
            w[:, g, 8, 0, g, 8, 0] = -28.0
            for b in range(4): w[:, g, 10, b, g, 9, 0] = -2.0 ** (b - 5)
    return weights(rng, w)
def setup_inputs(rng):
    return {**numbers_of(rng), **layers(rng)}
def setup_inputs_ties(rng):
    d = numbers_of(rng)
    o = rng.permutation(N)
    k = rng.integers(0, 4, (N, 8, C))
    k[o[1]] += 1
    k[o[2], rng.permutation(8)[:4]] = 1
    for g in range(8): k[o[3], g] = 1 + (rng.permutation(C) < H + g % 3 - 1)
    x = d["x"].reshape(N, 8, 16, C, 4)
    x[:, :, 0] = 0
    x[:, :, 0, :, 0] = k.astype(np.float32).astype(BF)
    a = np.exp2(rng.integers(-3, 4, (N, 8, C)).astype(np.float32))
    x[:, :, 8:] = 0
    x[:, :, 8, :, 0] = (-1.125 * a).astype(BF)
    x[:, :, 10, :, 0] = (-0.0703125 * a).astype(BF)
    u = d["u"].reshape(N, 128, 128, 4)
    u[:, :, ::16] = 0
    for r in range(N):
        for h in range(0, 128, 16): u[r, h, h, 0] = 0.0 if r == o[0] else -1.0 if r == o[1] else 1.0
    return {"x": x.reshape(N, 128, 4 * C), "u": u.reshape(N, 128, 512), "v": d["v"], **layers(rng, [0], True)}
def setup_inputs_near(rng):
    d = numbers_of(rng)
    x = d["x"].astype(np.float32).reshape(N, 8, 16, C, 4)
    x[:, :, 0] = 0
    x[:, :, 8:] = 0
    u = d["u"].reshape(N, 128, 128, 4)
    u[:, :, ::16] = 0
    o = rng.permutation(N) % 4
    for r in range(N):
        c = rng.choice([-1.0, 1.0], (8, 1))
        s = rng.integers(0, 16, (8, C))
        digits = ((s[:, :, None] >> np.arange(4)) & 1) * np.exp2(np.arange(4) - 23.0)
        if o[r] < 2:
            x[r, :, 0, :, 0] = c
            x[r, :, 8] = digits
            x[r, :, 11, :, 0] = 2.0 ** -10
        elif o[r] == 2: x[r, :, 8] = digits * rng.choice([-1.0, 1.0], (8, C, 1))
        else:
            x[r, :, 8, :, 0] = np.where(s < 8, 1.25, 0.0) * 2.0 ** -30 * c
            x[r, :, 9, :, 0] = np.where(s < 8, 0.0, 1.125) * 2.0 ** -30 * c
            for g in rng.permutation(8)[:4]:
                e = rng.choice([-1.0, 1.0], C) * 2.0 ** -30
                x[r, g, 8, :, 0] = 1.25 * e
                x[r, g, 9, :, 0] = -1.125 * e
        at = [0, C - 1, int(rng.integers(C)), int(rng.integers(C))]
        for g, j in zip(rng.permutation(8)[:4], at): x[r, g, 0, j, 0] = 2.0 ** 29 * rng.choice([-1.0, 1.0])
        k = 1.0 if o[r] == 0 else 2.0 ** -30
        for h in range(0, 128, 16):
            u[r, h, h, 0] = k if o[r] < 2 else 1.0
            if o[r] < 2: u[r, h + 11, h, 0] = k
            if o[r] < 3: u[r, h + 8, h] = k
            else:
                u[r, h + 8, h, 0] = k
                u[r, h + 9, h, 0] = 1.125 * k
    return {"x": x.reshape(N, 128, 4 * C).astype(BF), "u": u.reshape(N, 128, 512), "v": d["v"], **layers(rng, [0, 8, 9, 10, 11, 12, 13, 14, 15])}
def setup_inputs_odd(rng):
    d = numbers_of(rng)
    o = rng.permutation(N)
    x = (1.0 + (2 * rng.integers(0, 64, (N, 16, 8, C, 4)) + 1) * 2.0 ** -7) * np.exp2(-rng.integers(0, 7, (N, 16, 8, C, 4)).astype(np.float64)) * rng.choice([-1.0, 1.0], (N, 16, 8, C, 4))
    s = rng.choice([-1.0, 1.0], (N, 8, 2, C))
    late = np.arange(C) >= H
    e = np.arange(C)[None, :] - np.where(np.arange(8)[:, None] < rng.integers(1, 8), 1, 0)
    s[o[0], :, 0] = np.where(late, 1.0, -1.0)
    s[o[1], :, 0] = np.where((e >= 0) & (e < H), 1.0, -1.0)
    s[o[2], :, 0] = np.where(late[None, :] == (rng.permutation(8)[:, None] < 4), 1.0, -1.0)
    x[:, :, 0, :, 0] = 1.96875 * 2.0 ** 8 * s.reshape(N, 16, C)
    u = d["u"].reshape(N, 16, 8, 128, 4)
    u[:, :, 0, ::16] = 0
    for r in o[:3]:
        u[r, :, :, ::16] = 0
        for g in range(8): u[r, 2 * g, 0, 16 * g, 0] = 1.0
    for i, g in enumerate(rng.permutation(8)[:4]):
        x[o[3], 2 * g, 1, :, 0] = (8 + rng.integers(0, 2, C)) * 2.0 ** (i - 8)
        u[o[3], :, :, 16 * g] = 0
        u[o[3], 2 * g, 1, 16 * g, 0] = 1.0
    return {"x": x.astype(np.float32).reshape(N, 128, 4 * C).astype(BF), "u": u.reshape(N, 128, 512), "v": d["v"], **layers(rng, [0, 8])}
def setup_inputs_ends(rng):
    d = numbers_of(rng)
    x = np.zeros((N, 8, 16, C, 4))
    u = d["u"].astype(np.float32).reshape(N, 128, 128, 4)
    v = d["v"].astype(np.float32)
    w = np.zeros((N, 128, 4, 128, 4), np.float32)
    o = rng.permutation(N) % 4
    i = np.arange(128)
    for r in range(N):
        h = rng.permutation(8)
        c = np.where(h < 2, 0.0, h % 2 * 2.0 - 1.0)[None, :, None]
        low = -(0.9 + 0.1 * rng.random((8, 16, C, 4))) * 2.0 ** 30
        if o[r] == 0: x[r] = low
        if o[r] == 1: x[r] = np.where((rng.random(C) < 0.5)[:, None], (1.0 + 0.4 * rng.random((8, 16, C, 4))) * 2.0 ** 27, low)
        if o[r] == 2: x[r] = -(1.0 + 0.125 * rng.integers(0, 8, (8, 16, C, 4))) * 2.0 ** -30
        if o[r] == 3: x[r] = d["x"][r].astype(np.float32).reshape(8, 16, C, 4)[:, :, :1]
        if o[r] < 2:
            u[r, :, ::16] = c * (0.9 + 0.1 * rng.random((128, 8, 4))) * 2.0 ** 30
            v[r] = rng.choice([-1.0, 1.0], (128, 512)) * (0.9 + 0.1 * rng.random((128, 512))) * 2.0 ** 30
        if o[r] == 2:
            u[r, :, ::16] = c * (1.0 + 0.125 * rng.integers(0, 8, (128, 8, 4))) * 2.0 ** -30
            v[r] = rng.choice([-1.0, 1.0], (128, 512)) * (1.0 + 0.125 * rng.integers(0, 8, (128, 512))) * 2.0 ** -30
        if o[r] == 3: u[r, :, ::16] *= np.abs(c).astype(np.float32)
        k = np.array([4.0, 8.0, 16.0])[rng.permutation(8) % 3]
        for b in range(4): w[r, i, b, i, b] = k[i // 16]
    return {"x": x.astype(np.float32).reshape(N, 128, 4 * C).astype(BF), "u": u.reshape(N, 128, 512).astype(BF), "v": v.astype(BF), **weights(rng, w.astype(BF))}
def setup_inputs_spread(rng):
    d = setup_inputs(rng)
    d["x"] = wide(rng, N, 128, 4 * C, cols=6)
    return d
def check_inputs(d):
    b = []
    for k in ("x", "u", "v"):
        a = np.abs(d[k].astype(np.float32))
        if not (np.isfinite(a).all() and ((a == 0) | (a >= 2.0 ** -30) & (a <= 2.0 ** 30)).all()): b.append("a value of " + k)
    none, least, most = [emit(mx_ref.quantize(np.full((128, 16), k, np.float32).astype(BF)))[1][0, 0] for k in (0.0, 2.0 ** -8, 2.0 ** 8)]
    for r in range(N):
        if ((d["wc"][r] == 0x7F) | (d["wc"][r] == 0xFF)).any(): b.append("wc: a code that is no number")
        s = mx_ref.live(d["ws"][r])
        if ((s != none) & ((s < least) | (s > most))).any(): b.append("ws: a scale out of range")
    return b
def parts(t):
    return np.ascontiguousarray(t.reshape(8, 16, -1, 4).transpose(2, 0, 1, 3)).reshape(-1, 16, 4)
def laid(p):
    return np.ascontiguousarray(p.reshape(-1, 8, 16, 4).transpose(1, 2, 0, 3)).reshape(128, -1)
def layer(w, q):
    return mx_ref.quantize(tile([np.maximum(mx_ref.matmul(pick(w, np.arange(128 * b, 128 * b + 128)), q), np.float32(0.0)) * np.float32(0.03125) for b in range(4)]))
def reference(x, u, v, wc, ws):
    qu = [mx_ref.quantize(u[r]) for r in range(N)]
    lay = [pk(wc[r], ws[r]) for r in range(N)]
    now = [x[r] for r in range(N)]
    for m in MASK:
        t, high, low, own, out = [], [], [], [], []
        for r in range(N):
            q = mx_ref.quantize(now[r])
            s = mx_ref.matmul(qu[r], q)[::16] + np.float32(0.0)
            flag = np.zeros((8, C), bool)
            np.put_along_axis(flag, np.argsort(-s, axis=1, kind="stable")[:, :H], True, axis=1)
            high.append(np.flatnonzero(flag.T))
            low.append(np.flatnonzero(~flag.T))
            t.append(decode(q))
            p = parts(t[r].astype(BF))
            own.append(mx_ref.quantize(laid(p[high[r]])))
            out.append(mx_ref.quantize(laid(p[low[r]])))
        home = [layer(lay[r], own[r]) for r in range(N)]
        guest = [layer(lay[r], out[r ^ m]) for r in range(N)]
        for r in range(N):
            a = np.zeros((8 * C, 16, 4), np.float32)
            a[high[r]] = parts(decode(home[r]))
            a[low[r]] = parts(decode(guest[r ^ m]))
            now[r] = (t[r] + laid(a)).astype(BF)
    y, op = np.zeros((N, 128, C), np.float32), np.zeros((N, 8, C), np.float32)
    oc, osc = np.zeros((N, 128, 4 * C), np.uint8), np.zeros((N, 16, C), np.uint8)
    for r in range(N):
        q = mx_ref.quantize(now[r])
        y[r] = mx_ref.matmul(mx_ref.quantize(v[r]), q)
        n = np.zeros(8 * C, np.int64)
        n[high[r]] = np.arange(4 * C)
        n[low[r]] = 4 * C + np.arange(4 * C)
        op[r] = n.reshape(C, 8).T
        oc[r], osc[r] = emit(q)
    return {"y": y, "op": op, "oc": oc, "osc": osc}

@@ -1,0 +1,559 @@
+import math
+from concourse.mybir import dt, AluOpType as Op, ActivationFunctionType as Fn
+
+C, H, ROUNDS = 320, 160, 3
+MASK = [1, 2, 3]
+U8, F8, BF, F32, I32, U16 = "uint8", "float8_e4m3fn_x4", "bfloat16", "float32", "int32", "uint16"
+T_PRODUCTS, A_PRODUCTS = 4, 4
+BY_SCALAR = [8, 9]
+
+SCRATCH = {}
+
+
+def _sb(name, cols, dtype):
+    SCRATCH[name] = ("sbuf", [128, cols], dtype)
+
+
+def _mx(name, cols):
+    _sb(name, cols, F8)
+    _sb(name + "s", cols, U8)
+
+
+for _k in range(8):
+    SCRATCH["ps%d" % _k] = ("psum", [128, 512], F32)
+for _n, _w in (("xin", 1280), ("xn", 1280), ("ut", 512), ("vt", 512), ("ones", 1024), ("zt", 1280), ("hb", 320), ("eqt", 640), ("zs", 1280),
+               ("fs", 528), ("dat", 320), ("wn", 2560), ("wt", 10240), ("wv", 10240), ("gt", 640), ("ft", 640), ("at", 640),
+               ("bt", 640), ("vb", 640), ("m16", 320), ("m32", 320), ("est", 2048), ("cst", 4096), ("cc1", 1024), ("cci", 640), ("two", 8)):
+    _sb(_n, _w, BF)
+for _k in range(6):
+    _sb("ct%d" % _k, 1280, BF)
+    _mx("cq%d" % _k, 320)
+for _n, _w in (("tr", 320), ("ob", 640), ("su", 80), ("sg", 80), ("st", 96), ("r1", 80), ("r0", 80), ("dg", 80), ("n2f", 32),
+               ("vf", 32), ("vtr", 32), ("om", 512), ("jj", 640), ("sc", 32), ("pl", 20), ("s2", 20), ("sz", 20), ("it", 20),
+               ("smk", 80), ("z80", 80), ("yo", 320), ("lf", 200)):
+    _sb(_n, _w, F32)
+for _n, _w in (("pi", 8), ("lui", 64), ("li", 480)):
+    _sb(_n, _w, I32)
+for _n, _w in (("lu", 64), ("pos", 32), ("off", 32), ("wl", 32)):
+    _sb(_n, _w, U16)
+for _n, _w in (("xq", 320), ("uq", 128), ("us", 384), ("vq", 128), ("wq", 512), ("e0", 512), ("er", 1024), ("kc", 1024), ("k1", 256),
+               ("ki", 160), ("fq", 132), ("nq", 640), ("gq", 160), ("fqq", 160), ("aq", 160), ("bq", 160)):
+    _mx(_n, _w)
+for _k in range(ROUNDS):
+    _mx("gl%d" % _k, 160)
+    _mx("bl%d" % _k, 160)
+
+SEMAPHORES = ["ev", "ea", "et", "ep"] + ["d%d" % _k for _k in range(120)]
+for _k in range(ROUNDS):
+    SEMAPHORES += ["ga%d" % _k, "ba%d" % _k, "gs%d" % _k, "bs%d" % _k]
+
+
+def rank_program(g, core, T, topo):
+    rank = T.rank_of(core)
+    if rank is None:
+        return
+    queue = {"v": g.vector, "a": g.scalar, "t": g.tensor, "p": g, "s": g.sync}
+    known = {q: {} for q in queue}
+    count, snaps, log, ndma, final = {}, {}, {}, [0], {}
+
+    def A(name, a, b, step=1):
+        return (name, a, b, step)
+
+    def ap(s):
+        return T[s[0]][:, s[1]:s[2]] if s[3] == 1 else T[s[0]][:, s[1]:s[2]:s[3]]
+
+    def hit(x, y):
+        return x[1] < y[2] and y[1] < x[2] and (x[1] - y[1]) % math.gcd(x[3], y[3]) == 0
+
+    def need(q, tokens):
+        for tok in sorted(set(tokens), key=lambda k: (k[0], -k[1])):
+            if known[q].get(tok[0], 0) < tok[1]:
+                queue[q].wait_ge(T.sem[tok[0]], tok[1])
+                known[q][tok[0]] = tok[1]
+                for s, n in snaps[tok].items():
+                    known[q][s] = max(known[q].get(s, 0), n)
+
+    def note(s, w, q, token, loose=False):
+        keep = []
+        for r in log.get(s[0], []):
+            x = r[0]
+            inside = s[1] <= x[1] and x[2] <= s[2] and (s[3] == 1 or (s[3] == x[3] and (s[1] - x[1]) % s[3] == 0))
+            if loose or not (inside and (w or (r[2] == q and not r[1]))):
+                keep.append(r)
+        keep.append((s, w, q, token, loose))
+        log[s[0]] = keep
+
+    def emit(q, fn, outs, ins, token=None, acc=False, loose=False):
+        tokens = []
+        for lst, w in ((ins, False), (outs, True)):
+            for s in lst:
+                bank = s[0][:2] == "ps"
+                for r in log.get(s[0], ()):
+                    if bank:
+                        if not (r[2] == q and (acc or not (w or r[1]))):
+                            tokens.append(r[3])
+                    elif loose and w and r[1] and r[2] == q and r[4]:
+                        continue
+                    elif (w or r[1]) and hit(s, r[0]):
+                        tokens.append(r[3])
+        need(q, tokens)
+        inst = fn()
+        if token is None:
+            name = "e" + q
+            count[name] = count.get(name, 0) + 1
+            token = (name, count[name])
+            inst.then_inc(T.sem[name], 1)
+        final[token[0]] = token[1]
+        snaps[token] = dict(known[q])
+        for s in ins:
+            note(s, False, q, token, q == "s")
+        for s in outs:
+            note(s, True, q, token, loose)
+
+    def dma(q, out_ap, in_ap, outs, ins, loose=False):
+        tok = ("d%d" % ndma[0], 16)
+        ndma[0] += 1
+        emit(q, lambda: queue[q].dma_start(out_ap, in_ap).then_inc(T.sem[tok[0]], 16), outs, ins, tok, loose=loose)
+
+    def memset(s, c):
+        emit("v", lambda: g.vector.memset(ap(s), c), [s], [])
+
+    def copy(o, i):
+        emit("v", lambda: g.vector.tensor_copy(ap(o), ap(i)), [o], [i])
+
+    def tt(o, a, b, op):
+        emit("v", lambda: g.vector.tensor_tensor(ap(o), ap(a), ap(b), op), [o], [a, b])
+
+    def ts(o, a, c1, c2, op0, op1=None):
+        ins = [a] + [c for c in (c1, c2) if isinstance(c, tuple)]
+        x1 = ap(c1) if isinstance(c1, tuple) else c1
+        x2 = ap(c2) if isinstance(c2, tuple) else c2
+        if op1 is None:
+            emit("v", lambda: g.vector.tensor_scalar(ap(o), ap(a), x1, None, op0), [o], ins)
+        else:
+            emit("v", lambda: g.vector.tensor_scalar(ap(o), ap(a), x1, x2, op0, op1), [o], ins)
+
+    def scan(o, a, b, init, op0, op1):
+        emit("v", lambda: g.vector.tensor_tensor_scan(ap(o), ap(a), ap(b), init, op0, op1), [o], [a, b])
+
+    def act(o, i, fn, bias=None, scale=1.0):
+        if bias is None:
+            emit("a", lambda: g.scalar.activation(ap(o), ap(i), fn, scale=scale), [o], [i])
+        elif isinstance(bias, tuple):
+            emit("a", lambda: g.scalar.activation(ap(o), ap(i), fn, bias=ap(bias), scale=scale), [o], [i, bias])
+        else:
+            emit("a", lambda: g.scalar.activation(ap(o), ap(i), fn, bias=bias, scale=scale), [o], [i])
+
+    def quant(o, c, n, i, c2):
+        src = A(i, c2, c2 + 4 * n)
+        emit("v", lambda: g.vector.quantize_mx(T[o][:, c:c + n], T[o + "s"][:, c:c + n], ap(src)), [A(o, c, c + n), A(o + "s", c, c + n)], [src])
+
+    def mm(bank, w, wc, x, xc, n, start=True, stop=True):
+        o = A("ps%d" % bank, 0, 512)
+        emit("t", lambda: g.tensor.matmul_mx(T["ps%d" % bank][:, 0:n], T[w][:, wc:wc + 128], T[w + "s"][:, wc:wc + 128],
+                                             T[x][:, xc:xc + n], T[x + "s"][:, xc:xc + n], start, stop),
+             [o], [A(w, wc, wc + 128), A(w + "s", wc, wc + 128), A(x, xc, xc + n), A(x + "s", xc, xc + n)], acc=not start)
+
+    def P(bank, n, a=0):
+        return A("ps%d" % bank, a, n)
+
+    def gather(q, o, win, lst):
+        if q == "v":
+            emit("v", lambda: g.vector.tensor_copy(ap(o), ap(win).indirect(ap(lst))), [o], [win, lst])
+        else:
+            emit("a", lambda: g.scalar.activation(ap(o), ap(win).indirect(ap(lst)), Fn.Copy), [o], [win, lst])
+
+    def send(dst, src, land, sem, done):
+        rid, pid, _ = topo.addr(dst)
+        eng = topo.engines(core, dst)
+        ec, es = eng[0::2], eng[1::4]
+        total = len(ec) + len(es)
+        need("p", [r[3] for nm in (src, src + "s") for r in log[nm] if r[1]])
+        g.remote_dma(T[land][:, 0:H].bitcast(dt.uint8), T[src][:, 0:H].bitcast(dt.uint8), T.sem[sem], T.sem[done], pid, rid, sum(1 << e for e in ec))
+        g.remote_dma(T[land + "s"][:, 0:H], T[src + "s"][:, 0:H], T.sem[sem], T.sem[done], pid, rid, sum(1 << e for e in es))
+        tok, arr = (done, total), (sem, total)
+        snaps[tok], snaps[arr] = dict(known["p"]), {}
+        final[done], final[sem] = total, total
+        for nm in (src, src + "s"):
+            note(A(nm, 0, H), False, "p", tok)
+        for nm in (land, land + "s"):
+            log[nm] = [(A(nm, 0, H), True, "r", arr, False)]
+
+    def iota(o, pattern, base, cm):
+        if o[0] in ("pi", "lui"):
+            emit("p", lambda: g.iota(ap(o), pattern, base, cm), [o], [])
+        else:
+            emit("p", lambda: g.iota(ap(o), pattern, base, cm, allow_small_or_imprecise_dtypes=True), [o], [])
+
+    def select(o, i, pattern, cmp, base, cm):
+        emit("p", lambda: g.affine_select(ap(o), ap(i), pattern, cmp, 0.0, base, cm), [o], [i])
+
+    def pcol(k):
+        return A("pi", k, k + 1)
+
+    def col(k):
+        return A("sc", k, k + 1)
+
+    def fill(s, c):
+        act(s, A("ones", 0, len(range(s[1], s[2], s[3]))), Fn.Copy, scale=c)
+
+    dma("a", T.ut[:, :], T.u[:, :], [A("ut", 0, 512)], [])
+    dma("s", T.xin[:, :], T.x[:, :], [A("xin", 0, 1280)], [])
+    dma("s", T.wq[:, :].bitcast(dt.uint8), T.wc[:, :], [A("wq", 0, 512)], [])
+    dma("s", T.wqs[:, :], T.ws[:, :], [A("wqs", 0, 512)], [])
+    dma("s", T.vt[:, :], T.v[:, :], [A("vt", 0, 512)], [])
+
+    memset(A("ones", 0, 512), 1.0)
+    iota(A("pi", 0, 1), [[0, 1]], 0, 1)
+    iota(A("lui", 0, 8), [[16, 8]], 0, 0)
+    iota(A("lui", 8, 16), [[32, 4], [0, 2]], 0, 0)
+    iota(A("lui", 16, 24), [[32, 4], [0, 2]], 16, 0)
+    for b in range(4):
+        select(A("est", 512 * b, 512 * b + 512), A("ones", 0, 512), [[-1, 128], [1000, 4]], Op.is_equal, -1000 * b, 1)
+        if b == 0:
+            iota(A("lui", 24, 44), [[32, 10], [0, 2]], 0, 0)
+            iota(A("lui", 44, 64), [[32, 10], [0, 2]], 16, 0)
+    iota(A("om", 0, 512), [[1, 8], [8, 16], [0, 4]], 0, 0)
+    iota(A("jj", 320, 640), [[0, 10], [1, 32]], 0, 0)
+    iota(A("jj", 0, 320), [[0, 20], [1, 16]], 0, 0)
+    iota(A("smk", 0, 80), [[0, 20], [1, 4]], 0, 0)
+    iota(A("pl", 0, 20), [[128, 20]], 0, 0)
+    iota(A("s2", 0, 20), [[0, 2], [512, 5], [16, 2]], 0, 0)
+
+    memset(A("ones", 512, 1024), 1.0)
+    fill(A("zt", 0, 1024), 0.0)
+    fill(A("zt", 1024, 1280), 0.0)
+    ts(pcol(1), pcol(0), 15, None, Op.bitwise_and)
+    ts(pcol(2), pcol(0), 31, None, Op.bitwise_and)
+    ts(pcol(3), pcol(0), 4, None, Op.arith_shift_right)
+    memset(A("cc1", 0, 512), 0.0)
+    for a in range(4):
+        for gg in range(2):
+            m = 32 * a + 16 * gg
+            s = A("cc1", 4 * m + gg, 4 * (m + 16), 2)
+            emit("v", lambda: g.vector.memset(T.cc1[32 * a:32 * a + 32, s[1]:s[2]:2], 1.0), [s], [], loose=True)
+    copy(A("sc", 0, 3), A("pi", 1, 4))
+    memset(A("two", 0, 8), 2.0)
+    ts(A("cc1", 512, 1024), A("cc1", 0, 512), 0.5, None, Op.mult)
+    copy(A("lu", 0, 24), A("lui", 0, 24))
+    quant("uq", 0, 128, "ut", 0)
+    lst = A("lu", 0, 24)
+    emit("a", lambda: g.scalar.activation(T.uss[:, 0:384], T.uqs[:, 0:128].indirect(ap(lst)), Fn.Copy), [A("uss", 0, 384)], [A("uqs", 0, 128), lst])
+    emit("v", lambda: g.vector.tensor_copy(T.us[:, 0:384].bitcast(dt.uint32), T.uq[:, 0:128].bitcast(dt.uint32).indirect(ap(lst))),
+         [A("us", 0, 384)], [A("uq", 0, 128), lst])
+
+    def consts_early():
+        copy(A("lu", 24, 64), A("lui", 24, 64))
+        quant("k1", 0, 256, "cc1", 0)
+
+    def consts_a():
+        fill(A("cst", 2048, 3072), 0.0)
+        fill(A("cst", 3072, 4096), 0.0)
+        for b in range(4):
+            for e in range(b + 1):
+                s = A("cst", 2048 + 512 * b + 4 * (3 + e // 2) + e, 2048 + 512 * b + 512, 64)
+                if e < b:
+                    iota(s, [[0, 8]], 2, 0)
+                else:
+                    select(s, A("two", 0, 8), [[16, 8]], Op.is_gt, 0, -1)
+        fill(A("ct5", 0, 1024), 0.0)
+        fill(A("ct5", 1024, 1280), 0.0)
+
+    def consts_a2():
+        fill(A("fs", 0, 528), 0.0)
+        fill(A("cst", 1536, 2048), 2.0)
+        fill(A("cci", 0, 640), 0.0)
+        for e, c in ((80, -1.0), (86, -1.0), (121, 1.0), (127, 1.0)):
+            fill(A("cci", e, e + 1), c)
+        act(A("smk", 0, 80), A("smk", 0, 80), Fn.Sign)
+        fill(A("z80", 0, 80), 0.0)
+        fill(A("st", 0, 8), 0.0)
+        fill(A("vf", 0, 32), 0.0)
+
+    def consts_v():
+        ts(col(3), col(0), 8.0, col(2), Op.mult, Op.add)
+        none, big, small = 1.5 * 2.0 ** 35, 1.5 * 2.0 ** 30, 1.5 * 2.0 ** 26
+        ts(col(8), col(0), 3.0, none, Op.is_ge, Op.mult)
+        for k, v in ((9, big), (10, small)):
+            ts(col(k), col(0), float(k - 9), v, Op.is_equal, Op.mult)
+        for k, v in ((11, none), (12, big), (13, small)):
+            ts(col(k), col(0), float(k - 11), v, Op.is_equal, Op.mult)
+        ts(col(14), col(2), 2.0, None, Op.mult)
+        ts(A("cst", 0, 512), A("om", 0, 512), col(3), 2.0, Op.is_gt, Op.mult)
+        tt(col(19), col(8), col(9), Op.add)
+        tt(col(20), col(8), col(11), Op.add)
+        tt(col(21), col(12), col(13), Op.add)
+        ts(A("cst", 512, 1024), A("om", 0, 512), col(3), 2.0, Op.is_le, Op.mult)
+        ts(col(15), col(0), 32.0, col(14), Op.mult, Op.add)
+        ts(col(16), col(2), -1.0, 8.0, Op.mult, Op.add)
+        tt(col(6), col(19), col(10), Op.add)
+        tt(col(7), col(20), col(21), Op.add)
+        ts(A("cst", 1024, 1536), A("om", 0, 512), col(3), 2.0, Op.is_equal, Op.mult)
+        ts(A("s2", 0, 20), A("s2", 0, 20), col(15), None, Op.add)
+        ts(col(17), col(2), -2.0, 16.0, Op.mult, Op.add)
+        ts(A("pl", 0, 20), A("pl", 0, 20), col(3), 0.5, Op.add, Op.add)
+        ts(A("m16", 0, 320), A("jj", 0, 320), col(0), None, Op.is_equal)
+        ts(A("sz", 0, 20), A("s2", 0, 20), col(16), None, Op.add)
+        quant("kc", 0, 512, "cst", 0)
+        quant("kc", 512, 512, "cst", 2048)
+        quant("ki", 0, 160, "cci", 0)
+
+    flip = [0]
+
+    def other():
+        flip[0] += 1
+        return "vavav"[flip[0] % 5]
+
+    def unpack(pair, b, d, bank, q, i):
+        mm(bank, "er", 256 * b + 16 * d, pair, 0, H)
+        k = 5120 * i + 640 * d + 160 * b
+        if q == "v":
+            copy(A("wv", k, k + H), P(bank, H))
+        else:
+            act(A("wv", k, k + H), P(bank, H), Fn.Copy)
+
+    def by_dma(name, w, d):
+        o, i, k = A(name, w * d, w * d + w), A(name, 0, w), 128 - 16 * d
+        dma("s", T[name][0:k, o[1]:o[2]], T[name][16 * d:128, 0:w], [o], [i], loose=True)
+        dma("s", T[name][k:128, o[1]:o[2]], T[name][0:16 * d, 0:w], [o], [i], loose=True)
+
+    def layer(pair, tile, out):
+        for b in range(4):
+            mm(b, "wq", 128 * b, pair, 0, H)
+        for b in range(4):
+            o = A(tile, b, 4 * H, 4)
+            if b % 2 == 0:
+                ts(o, P(b, H), 0.0, 0.03125, Op.max, Op.mult)
+            else:
+                act(o, P(b, H), Fn.Relu, scale=0.03125)
+        quant(out, 0, H, tile, 0)
+
+    def L(k):
+        return A("li", 20 * k, 20 * k + 20)
+
+    def LF(k):
+        return A("lf", 20 * k, 20 * k + 20)
+
+    def TW(b):
+        return A("wt", 320 * b, 320 * b + 9280)
+
+    def WV(b):
+        return A("wv", 160 * b, 160 * b + 9760)
+
+    def own(gg, b):
+        return A("tr", 32 * b + 16 * gg, 32 * b + 16 * gg + 1)
+
+    def t_number(b, d):
+        bank = 6 + b % 2
+        if d == 0:
+            mm(bank, "e0", 128 * b, "xq", 0, C)
+        else:
+            mm(bank, "er", 256 * b + 16 * d, "xq", 0, C)
+        act(A("wt", 1280 * d + 320 * b, 1280 * d + 320 * b + 320), P(bank, C), Fn.Copy)
+
+    def compare(b):
+        for gg in range(2):
+            t, e, lo = "ct%d" % (b // 2), 2 * (b % 2) + gg, 32 * b + 32
+            ts(A(t, e, 4 * lo, 4), P(1 + gg, lo), own(gg, b), None, Op.is_lt)
+            if lo < C:
+                ts(A(t, 4 * lo + e, 1280, 4), P(1 + gg, C, lo), own(gg, b), None, Op.is_le)
+
+    def compare_a(b):
+        for gg in range(2):
+            t, e, lo, z = "ct%d" % (b // 2), 2 * (b % 2) + gg, 32 * b + 32, 320 * ((2 * b + gg) % 4)
+            act(A("zs", z, z + C), P(4 + gg, C), Fn.Sign, bias=own(gg, b), scale=-1.0)
+            act(A(t, e, 4 * lo, 4), A("zs", z, z + lo), Fn.Sign, bias=-0.5)
+            if lo < C:
+                act(A(t, 4 * lo + e, 1280, 4), A("zs", z + lo, z + C), Fn.Sign, bias=0.5)
+
+    def add_ranks(t, w, start, stop):
+        quant("cq%d" % t, 0, C, "ct%d" % t, 0)
+        mm(3, "k1", 128 * w, "cq%d" % t, 0, C, start=start, stop=stop)
+
+    def tie_rows():
+        for k in range(2):
+            gather("a", A("ob", 320 * k, 320 * k + 320), A("tr", 0, 320), A("lu", 24 + 20 * k, 44 + 20 * k))
+
+    for rd in range(ROUNDS):
+        dst = T.cores[rank ^ MASK[rd]]
+        dma("s", T.wn[:, 0:1280], T.zt[:, :], [A("wn", 0, 1280)], [A("zt", 0, 1280)])
+        dma("s", T.wn[:, 1280:2560], T.zt[:, :], [A("wn", 1280, 2560)], [A("zt", 0, 1280)])
+        quant("xq", 0, C, "xin" if rd == 0 else "xn", 0)
+        for bank, k in ((0, 0), (1, 1), (2, 2)):
+            mm(bank, "us", 128 * k, "xq", 0, C)
+        emit("v", lambda: g.vector.transpose(T.tr[:, 0:320], T.ps0[:, 0:320]), [A("tr", 0, 320)], [P(0, 320)])
+        if rd == 0:
+            mm(4, "us", 128, "xq", 0, C)
+            mm(5, "us", 256, "xq", 0, C)
+            consts_early()
+            compare(0)
+            consts_a()
+            tie_rows()
+            compare(1)
+            add_ranks(0, 0, True, False)
+            quant("e0", 0, 512, "est", 0)
+            for b in range(4):
+                for k in range(2):
+                    to = 256 * b + 128 * k
+                    dma("s", T.er[:, to:to + 128].bitcast(dt.uint8), T.e0[:, 128 * b:128 * b + 128].bitcast(dt.uint8), [A("er", to, to + 128)], [A("e0", 128 * b, 128 * b + 128)])
+                    dma("s", T.ers[:, to:to + 128], T.e0s[:, 128 * b:128 * b + 128], [A("ers", to, to + 128)], [A("e0s", 128 * b, 128 * b + 128)])
+        for b in range(4):
+            t_number(b, 0)
+        for d in range(T_PRODUCTS, 8):
+            by_dma("wt", 1280, d)
+        if rd > 0:
+            mm(4, "us", 128, "xq", 0, C)
+            mm(5, "us", 256, "xq", 0, C)
+            tie_rows()
+            compare(0)
+            compare(1)
+            add_ranks(0, 0, True, False)
+        for b in BY_SCALAR:
+            compare_a(b)
+        if rd == 0:
+            consts_a2()
+        compare(2)
+        compare(3)
+        add_ranks(1, 0, False, False)
+        compare(4)
+        compare(5)
+        add_ranks(2, 0, False, False)
+        if rd == 0:
+            ts(A("m32", 0, 320), A("jj", 320, 640), col(1), None, Op.is_gt)
+        for gg in range(2):
+            o = A("eqt", 320 * gg, 320 * gg + 320)
+            tt(o, P(1 + gg, C), A("ob", 320 * gg, 320 * gg + 320), Op.is_equal)
+            tt(A("ct5", gg, 1280, 4), o, A("m32", 0, 320), Op.mult)
+        add_ranks(5, 0, False, False)
+        for b in range(4):
+            t_number(b, 1)
+        compare(6)
+        compare(7)
+        add_ranks(4, 1, False, False)
+        if rd == 0:
+            consts_v()
+        add_ranks(3, 0, False, True)
+        ts(A("hb", 0, 320), P(3, C), 160.0 - 16 * len(BY_SCALAR), 0.5, Op.is_lt, Op.subtract)
+        tt(A("fs", 16, 336), A("hb", 0, 320), A("m16", 0, 320), Op.mult)
+        quant("fq", 0, 132, "fs", 0)
+        mm(0, "kc", 0, "fq", 4, 128, True, False)
+        mm(0, "kc", 128, "fq", 0, 128, False, True)
+        mm(1, "kc", 256, "fq", 4, 128)
+        mm(2, "kc", 384, "fq", 4, 128)
+        mm(4, "kc", 512, "fq", 4, 128)
+        mm(5, "kc", 640, "fq", 4, 128)
+        mm(3, "kc", 768, "fq", 4, 128)
+        scan(A("su", 0, 80), P(0, 80), A("z80", 0, 80), -0.5, Op.add, Op.add)
+        mm(0, "kc", 896, "fq", 4, 128)
+        for d in range(2, T_PRODUCTS):
+            for b in range(4):
+                t_number(b, d)
+        scan(A("sg", 0, 80), A("smk", 0, 80), P(1, 80), 0.0, Op.mult, Op.add)
+        scan(A("st", 8, 88), P(2, 80), A("z80", 0, 80), 0.0, Op.add, Op.add)
+        n2, y, h2 = L(0), L(1), L(2)
+        tt(A("n2f", 0, 20), A("su", 3, 80, 4), A("sg", 3, 80, 4), Op.mult)
+        ts(A("r1", 0, 80), A("st", 7, 87), col(6), col(6), Op.add, Op.subtract)
+        tt(n2, A("n2f", 0, 20), A("pl", 0, 20), Op.add)
+        ts(A("r0", 0, 80), A("st", 7, 87), col(7), col(7), Op.add, Op.subtract)
+        ts(y, n2, 4, 31, Op.arith_shift_right, Op.bitwise_and)
+        ts(h2, n2, 14, None, Op.bitwise_and)
+        tt(A("dg", 0, 80), A("r1", 0, 80), A("r0", 0, 80), Op.subtract)
+        ts(L(3), y, -14, None, Op.mult)
+        ts(L(4), h2, 31, None, Op.mult)
+        for b, bank in ((0, 4), (1, 5)):
+            tt(A("dat", b, 320, 4), P(bank, 80), A("dg", 0, 80), Op.add)
+        tt(L(5), L(3), n2, Op.add)
+        tt(A("dat", 2, 320, 4), P(3, 80), A("dg", 0, 80), Op.add)
+        tt(L(6), L(5), L(4), Op.add)
+        tt(A("dat", 3, 320, 4), P(0, 80), A("dg", 0, 80), Op.add)
+        copy(A("pos", 0, 20), L(6))
+        slots, lst = A("wn", 0, 2560), A("pos", 0, 20)
+        emit("v", lambda: g.vector.tensor_copy(ap(slots).indirect(ap(lst)), T.dat[:, 0:320]), [slots], [lst, A("dat", 0, 320)])
+        quant("nq", 0, 320, "wn", 0)
+        quant("nq", 320, 320, "wn", 1280)
+        for s in range(5):
+            mm(1, "nq", 128 * s, "ki", 20 - 2 * s, 128, s == 0, s == 4)
+        tt(L(7), P(1, 20), A("sz", 0, 20), Op.add)
+        tt(L(8), P(1, 20), A("s2", 0, 20), Op.add)
+        ts(L(9), L(7), 7, None, Op.bitwise_and)
+        ts(L(10), L(8), 3, None, Op.arith_shift_right)
+        ts(L(11), L(9), 1280, None, Op.mult)
+        tt(L(12), L(11), L(10), Op.add)
+        copy(A("off", 0, 20), L(12))
+        for b in range(4):
+            gather("va"[b % 2], A("gt", b, 640, 4), TW(b), A("off", 10, 20))
+        quant("gq", 0, H, "gt", 0)
+        send(dst, "gq", "gl%d" % rd, "ga%d" % rd, "gs%d" % rd)
+        for b in range(4):
+            gather("va"[b % 2], A("ft", b, 640, 4), TW(b), A("off", 0, 10))
+        quant("fqq", 0, H, "ft", 0)
+        layer("fqq", "at", "aq")
+        for b in range(4):
+            unpack("aq", b, 0, 4 + b, "va"[b % 2], 0)
+        for d in range(A_PRODUCTS, 8):
+            by_dma("wv", 640, d)
+        layer("gl%d" % rd, "bt", "bq")
+        send(dst, "bq", "bl%d" % rd, "ba%d" % rd, "bs%d" % rd)
+        for k in range(4 * (A_PRODUCTS - 1)):
+            unpack("aq", k % 4, 1 + k // 4, 4 + k % 4, other(), 0)
+        ts(L(13), n2, 4, None, Op.arith_shift_right)
+        ts(L(14), n2, 16, None, Op.bitwise_and)
+        ts(L(15), n2, 1, None, Op.bitwise_and)
+        ts(L(16), n2, col(17), None, Op.add)
+        ts(LF(0), y, -0.5, None, Op.mult)
+        ts(LF(1), L(14), 0.96875, None, Op.mult)
+        ts(LF(2), L(15), 5120.0, None, Op.mult)
+        ts(L(17), L(16), 14, None, Op.bitwise_and)
+        tt(LF(3), LF(0), L(13), Op.add)
+        tt(LF(4), LF(1), LF(2), Op.add)
+        ts(LF(5), L(17), 320.0, None, Op.mult)
+        tt(LF(6), LF(3), LF(4), Op.add)
+        tt(LF(7), LF(6), LF(5), Op.add)
+        copy(A("wl", 0, 20), LF(7))
+        if rd == 0:
+            quant("vq", 0, 128, "vt", 0)
+        if rd == ROUNDS - 1:
+            ts(A("r0", 0, 20), A("sg", 3, 80, 4), -639.75, None, Op.mult)
+            ts(A("r1", 0, 20), A("n2f", 0, 20), 0.5, 639.75, Op.mult, Op.add)
+            ts(A("it", 0, 20), A("pl", 0, 20), 0.5, None, Op.mult)
+            tt(A("dg", 0, 20), A("r0", 0, 20), A("r1", 0, 20), Op.add)
+            tt(A("vf", 0, 20), A("dg", 0, 20), A("it", 0, 20), Op.add)
+            emit("v", lambda: g.vector.transpose(T.vtr[:, 0:32], T.vf[:, 0:32]), [A("vtr", 0, 32)], [A("vf", 0, 32)])
+            for k in range(8):
+                a, o = k // 2, 16 * (k % 2)
+                dma("s", T.op[k:k + 1, :], T.vtr[32 * a:32 * a + 20, o:o + 16], [], [A("vtr", 0, 32)])
+
+        def add_gathered(b, a, n):
+            o, win, t2 = A("xn", 4 * a + b, 4 * (a + n), 4), WV(b), A("wt", 320 * b + a, 320 * b + a + n)
+            li = A("wl", a // 16, (a + n) // 16)
+            emit("v", lambda: g.vector.tensor_tensor(ap(o), ap(win).indirect(ap(li)), ap(t2), Op.add), [o], [win, li, t2])
+
+        def gather_v(b, slot, a, n):
+            gather("a", A("vb", 320 * slot + a, 320 * slot + a + n), WV(b), A("wl", a // 16, (a + n) // 16))
+
+        def add_v(b, slot, a, n):
+            tt(A("xn", 4 * a + b, 4 * (a + n), 4), A("vb", 320 * slot + a, 320 * slot + a + n), A("wt", 320 * b + a, 320 * b + a + n), Op.add)
+
+        land = "bl%d" % rd
+        for b in range(4):
+            for d in range(8):
+                unpack(land, b, d, d, other(), 1)
+        gather_v(1, 0, 0, 320)
+        add_gathered(0, 0, 320)
+        gather_v(2, 1, 0, 320)
+        add_v(1, 0, 0, 320)
+        add_gathered(3, 0, 160)
+        gather_v(3, 0, 160, 160)
+        add_v(2, 1, 0, 320)
+        add_v(3, 0, 160, 160)
+
+    quant("xq", 0, C, "xn", 0)
+    dma("s", T.oc[:, :], T.xq[:, 0:C].bitcast(dt.uint8), [], [A("xq", 0, C)])
+    mm(0, "vq", 0, "xq", 0, C)
+    for k in range(4):
+        dma("a", T.osc[4 * k:4 * k + 4, :], T.xqs[32 * k:32 * k + 4, 0:C], [], [A("xqs", 0, C)])
+    copy(A("yo", 0, C), P(0, C))
+    dma("s", T.y[:, :], T.yo[:, 0:C], [], [A("yo", 0, C)])
+    for s in sorted(final):
+        if known["p"].get(s, 0) < final[s]:
+            g.wait_ge(T.sem[s], final[s])

@@ -4,8 +4,15 @@ from concourse.mybir import dt, AluOpType as Op, ActivationFunctionType as Fn
 C, H, ROUNDS = 320, 160, 3
 MASK = [1, 2, 3]
 U8, F8, BF, F32, I32, U16 = "uint8", "float8_e4m3fn_x4", "bfloat16", "float32", "int32", "uint16"
-T_PRODUCTS, A_PRODUCTS = 4, 4
-BY_SCALAR = [8, 9]
+T_PRODUCTS = 4
+NV = 5
+TURN = 2048
+FAR = 2.0 ** 90
+A_EARLY = 8
+B_BY_VECTOR = [4, 3, 2, 2]
+
+PAIRS = [("a", b, 32 * b) for b in range(9, NV - 1, -1)] + [("v", k, 32 * NV) for k in range(NV - 1)]
+TILES = [PAIRS[k:k + 2] for k in range(0, len(PAIRS), 2)]
 
 SCRATCH = {}
 
@@ -21,29 +28,31 @@ def _mx(name, cols):
 
 for _k in range(8):
     SCRATCH["ps%d" % _k] = ("psum", [128, 512], F32)
-for _n, _w in (("xin", 1280), ("xn", 1280), ("ut", 512), ("vt", 512), ("ones", 1024), ("zt", 1280), ("hb", 320), ("eqt", 640), ("zs", 1280),
-               ("fs", 528), ("dat", 320), ("wn", 2560), ("wt", 10240), ("wv", 10240), ("gt", 640), ("ft", 640), ("at", 640),
-               ("bt", 640), ("vb", 640), ("m16", 320), ("m32", 320), ("est", 2048), ("cst", 4096), ("cc1", 1024), ("cci", 640), ("two", 8)):
+for _n, _w in (("xin", 1280), ("xn", 1280), ("ut", 512), ("vt", 512), ("ones", 512), ("zt", 1280), ("zs", 1152), ("cd", 1280),
+               ("fs", 528), ("dat", 320), ("wn", 2560), ("wt", 7 * TURN + 1280), ("wv", 10240), ("gt", 640), ("ft", 640), ("at", 640),
+               ("bt", 640), ("tri", 320), ("row", 320), ("est", 1936), ("cst", 4096), ("cc1", 1024), ("cci", 640), ("om", 512), ("oa", 512),
+               ("j32", 320), ("jq", 320), ("j128", 128), ("jg", 64), ("jh", 16)):
     _sb(_n, _w, BF)
-for _k in range(6):
-    _sb("ct%d" % _k, 1280, BF)
-    _mx("cq%d" % _k, 320)
-for _n, _w in (("tr", 320), ("ob", 640), ("su", 80), ("sg", 80), ("st", 96), ("r1", 80), ("r0", 80), ("dg", 80), ("n2f", 32),
-               ("vf", 32), ("vtr", 32), ("om", 512), ("jj", 640), ("sc", 32), ("pl", 20), ("s2", 20), ("sz", 20), ("it", 20),
+_mx("cdq", 320)
+for _k, _t in enumerate(TILES):
+    _sb("ct%d" % _k, 4 * _t[0][2], BF)
+    _mx("cq%d" % _k, _t[0][2])
+for _n, _w in (("pm", 640), ("pt", 640), ("acc", 24), ("aw", 40), ("sp", 320), ("thr", 320), ("su", 80), ("sg", 80), ("st", 96), ("r1", 80),
+               ("r0", 80), ("dg", 80), ("n2f", 32), ("vf", 32), ("vtr", 32), ("sc", 40), ("pl", 20), ("s2", 20), ("it", 20),
                ("smk", 80), ("z80", 80), ("yo", 320), ("lf", 200)):
     _sb(_n, _w, F32)
-for _n, _w in (("pi", 8), ("lui", 64), ("li", 480)):
+for _n, _w in (("pi", 16), ("lui", 40), ("li", 400)):
     _sb(_n, _w, I32)
-for _n, _w in (("lu", 64), ("pos", 32), ("off", 32), ("wl", 32)):
+for _n, _w in (("lu", 16), ("lt", 20), ("pos", 32), ("off", 32), ("wl", 32)):
     _sb(_n, _w, U16)
-for _n, _w in (("xq", 320), ("uq", 128), ("us", 384), ("vq", 128), ("wq", 512), ("e0", 512), ("er", 1024), ("kc", 1024), ("k1", 256),
+for _n, _w in (("xq", 320), ("uq", 128), ("us", 256), ("vq", 128), ("wq", 512), ("er", 960), ("kc", 1024), ("k1", 256),
                ("ki", 160), ("fq", 132), ("nq", 640), ("gq", 160), ("fqq", 160), ("aq", 160), ("bq", 160)):
     _mx(_n, _w)
 for _k in range(ROUNDS):
     _mx("gl%d" % _k, 160)
     _mx("bl%d" % _k, 160)
 
-SEMAPHORES = ["ev", "ea", "et", "ep"] + ["d%d" % _k for _k in range(120)]
+SEMAPHORES = ["ev", "ea", "et", "ep"] + ["d%d" % _k for _k in range(100)]
 for _k in range(ROUNDS):
     SEMAPHORES += ["ga%d" % _k, "ba%d" % _k, "gs%d" % _k, "bs%d" % _k]
 
@@ -121,6 +130,9 @@ def rank_program(g, core, T, topo):
     def copy(o, i):
         emit("v", lambda: g.vector.tensor_copy(ap(o), ap(i)), [o], [i])
 
+    def turn32(o, i):
+        emit("v", lambda: g.vector.transpose(ap(o), ap(i)), [o], [i])
+
     def tt(o, a, b, op):
         emit("v", lambda: g.vector.tensor_tensor(ap(o), ap(a), ap(b), op), [o], [a, b])
 
@@ -136,13 +148,14 @@ def rank_program(g, core, T, topo):
     def scan(o, a, b, init, op0, op1):
         emit("v", lambda: g.vector.tensor_tensor_scan(ap(o), ap(a), ap(b), init, op0, op1), [o], [a, b])
 
-    def act(o, i, fn, bias=None, scale=1.0):
-        if bias is None:
-            emit("a", lambda: g.scalar.activation(ap(o), ap(i), fn, scale=scale), [o], [i])
-        elif isinstance(bias, tuple):
-            emit("a", lambda: g.scalar.activation(ap(o), ap(i), fn, bias=ap(bias), scale=scale), [o], [i, bias])
-        else:
-            emit("a", lambda: g.scalar.activation(ap(o), ap(i), fn, bias=bias, scale=scale), [o], [i])
+    def act(o, i, fn, bias=None, scale=1.0, total=None):
+        kw = {"scale": ap(scale) if isinstance(scale, tuple) else scale}
+        if bias is not None:
+            kw["bias"] = ap(bias) if isinstance(bias, tuple) else bias
+        if total is not None:
+            kw["accum_out"] = ap(total)
+        emit("a", lambda: g.scalar.activation(ap(o), ap(i), fn, **kw), [o] + ([total] if total else []),
+             [i] + [c for c in (bias, scale) if isinstance(c, tuple)])
 
     def quant(o, c, n, i, c2):
         src = A(i, c2, c2 + 4 * n)
@@ -162,6 +175,9 @@ def rank_program(g, core, T, topo):
             emit("v", lambda: g.vector.tensor_copy(ap(o), ap(win).indirect(ap(lst))), [o], [win, lst])
         else:
             emit("a", lambda: g.scalar.activation(ap(o), ap(win).indirect(ap(lst)), Fn.Copy), [o], [win, lst])
+
+    def gather_add(o, win, lst, more):
+        emit("v", lambda: g.vector.tensor_tensor(ap(o), ap(win).indirect(ap(lst)), ap(more), Op.add), [o], [win, lst, more])
 
     def send(dst, src, land, sem, done):
         rid, pid, _ = topo.addr(dst)
@@ -185,9 +201,6 @@ def rank_program(g, core, T, topo):
         else:
             emit("p", lambda: g.iota(ap(o), pattern, base, cm, allow_small_or_imprecise_dtypes=True), [o], [])
 
-    def select(o, i, pattern, cmp, base, cm):
-        emit("p", lambda: g.affine_select(ap(o), ap(i), pattern, cmp, 0.0, base, cm), [o], [i])
-
     def pcol(k):
         return A("pi", k, k + 1)
 
@@ -199,123 +212,143 @@ def rank_program(g, core, T, topo):
 
     dma("a", T.ut[:, :], T.u[:, :], [A("ut", 0, 512)], [])
     dma("s", T.xin[:, :], T.x[:, :], [A("xin", 0, 1280)], [])
-    dma("s", T.wq[:, :].bitcast(dt.uint8), T.wc[:, :], [A("wq", 0, 512)], [])
-    dma("s", T.wqs[:, :], T.ws[:, :], [A("wqs", 0, 512)], [])
-    dma("s", T.vt[:, :], T.v[:, :], [A("vt", 0, 512)], [])
 
-    memset(A("ones", 0, 512), 1.0)
     iota(A("pi", 0, 1), [[0, 1]], 0, 1)
-    iota(A("lui", 0, 8), [[16, 8]], 0, 0)
-    iota(A("lui", 8, 16), [[32, 4], [0, 2]], 0, 0)
-    iota(A("lui", 16, 24), [[32, 4], [0, 2]], 16, 0)
-    for b in range(4):
-        select(A("est", 512 * b, 512 * b + 512), A("ones", 0, 512), [[-1, 128], [1000, 4]], Op.is_equal, -1000 * b, 1)
-        if b == 0:
-            iota(A("lui", 24, 44), [[32, 10], [0, 2]], 0, 0)
-            iota(A("lui", 44, 64), [[32, 10], [0, 2]], 16, 0)
-    iota(A("om", 0, 512), [[1, 8], [8, 16], [0, 4]], 0, 0)
-    iota(A("jj", 320, 640), [[0, 10], [1, 32]], 0, 0)
-    iota(A("jj", 0, 320), [[0, 20], [1, 16]], 0, 0)
+    iota(A("j128", 0, 128), [[1, 128]], 0, 0)
+    iota(A("lui", 0, 8), [[32, 4], [0, 2]], 0, 0)
+    iota(A("lui", 8, 16), [[32, 4], [0, 2]], 16, 0)
+    iota(A("j32", 0, 320), [[0, 10], [1, 32]], 0, 0)
+    iota(A("jg", 0, 64), [[1, 8], [0, 8]], 0, 0)
+    iota(A("om", 0, 512), [[1, 8], [8, 16], [-8, 4]], 0, 0)
+    iota(A("jq", 0, 320), [[0, 40], [1, 4], [0, 2]], 0, 0)
+    iota(A("lui", 16, 36), [[1, 20]], 0, 0)
+    iota(A("jh", 0, 16), [[1, 8], [0, 2]], 0, 0)
     iota(A("smk", 0, 80), [[0, 20], [1, 4]], 0, 0)
     iota(A("pl", 0, 20), [[128, 20]], 0, 0)
     iota(A("s2", 0, 20), [[0, 2], [512, 5], [16, 2]], 0, 0)
 
-    memset(A("ones", 512, 1024), 1.0)
-    fill(A("zt", 0, 1024), 0.0)
-    fill(A("zt", 1024, 1280), 0.0)
-    ts(pcol(1), pcol(0), 15, None, Op.bitwise_and)
-    ts(pcol(2), pcol(0), 31, None, Op.bitwise_and)
-    ts(pcol(3), pcol(0), 4, None, Op.arith_shift_right)
-    memset(A("cc1", 0, 512), 0.0)
-    for a in range(4):
-        for gg in range(2):
-            m = 32 * a + 16 * gg
-            s = A("cc1", 4 * m + gg, 4 * (m + 16), 2)
-            emit("v", lambda: g.vector.memset(T.cc1[32 * a:32 * a + 32, s[1]:s[2]:2], 1.0), [s], [], loose=True)
-    copy(A("sc", 0, 3), A("pi", 1, 4))
-    memset(A("two", 0, 8), 2.0)
-    ts(A("cc1", 512, 1024), A("cc1", 0, 512), 0.5, None, Op.mult)
-    copy(A("lu", 0, 24), A("lui", 0, 24))
-    quant("uq", 0, 128, "ut", 0)
-    lst = A("lu", 0, 24)
-    emit("a", lambda: g.scalar.activation(T.uss[:, 0:384], T.uqs[:, 0:128].indirect(ap(lst)), Fn.Copy), [A("uss", 0, 384)], [A("uqs", 0, 128), lst])
-    emit("v", lambda: g.vector.tensor_copy(T.us[:, 0:384].bitcast(dt.uint32), T.uq[:, 0:128].bitcast(dt.uint32).indirect(ap(lst))),
-         [A("us", 0, 384)], [A("uq", 0, 128), lst])
+    memset(A("ones", 0, 512), 1.0)
+    memset(A("zt", 0, 1280), 0.0)
+    memset(A("est", 0, 1936), 0.0)
+    for k, (shift, keep) in enumerate(((0, 15), (0, 31), (4, 7), (4, 6), (0, 1), (1, 3), (3, 1), (2, 3))):
+        ts(pcol(k + 1), pcol(0), shift, keep, Op.arith_shift_right, Op.bitwise_and)
+    copy(A("sc", 0, 9), A("pi", 0, 9))
+    for k in range(2):
+        ts(A("est", 969 * k + 2, 969 * k + 514, 4), A("j128", 0, 128), col(0), None, Op.is_equal)
+        ts(A("est", 969 * k + 514, 969 * k + 962, 4), A("j128", 0, 112), col(0), None, Op.is_equal)
+    ts(col(9), col(2), 0.5, None, Op.add)
+    ts(col(10), col(4), 1.0, None, Op.add)
+    copy(A("lu", 0, 16), A("lui", 0, 16))
+    for b, at in enumerate((2, 970, 0, 968)):
+        quant("er", 240 * b, 240, "est", at)
+    ts(A("tri", 0, 320), A("j32", 0, 320), col(9), -FAR, Op.subtract, Op.mult)
 
-    def consts_early():
-        copy(A("lu", 24, 64), A("lui", 24, 64))
+    for q, o, w in (("s", "wn", 0), ("s", "wn", 1280)):
+        dma(q, T[o][:, w:w + 1280], T.zt[:, :], [A(o, w, w + 1280)], [A("zt", 0, 1280)])
+    for w in (2048, 3072):
+        dma("s", T.cst[:, w:w + 1024], T.zt[:, 0:1024], [A("cst", w, w + 1024)], [A("zt", 0, 1024)])
+    dma("s", T.wq[:, :].bitcast(dt.uint8), T.wc[:, :], [A("wq", 0, 512)], [])
+    dma("s", T.wqs[:, :], T.ws[:, :], [A("wqs", 0, 512)], [])
+    dma("s", T.vt[:, :], T.v[:, :], [A("vt", 0, 512)], [])
+
+    for k, t in enumerate(TILES):
+        wide = t[0][2]
+        for e in (2, 3):
+            a = t[1][2] if len(t) > 1 else 0
+            if a < wide:
+                fill(A("ct%d" % k, 4 * a + e, 4 * wide, 4), 0.0)
+    fill(A("fs", 0, 16), 0.0)
+    fill(A("fs", 336, 528), 0.0)
+    fill(A("cci", 0, 512), 0.0)
+    fill(A("cci", 512, 640), 0.0)
+    fill(A("z80", 0, 80), 0.0)
+    fill(A("st", 0, 8), 0.0)
+    fill(A("vf", 0, 32), 0.0)
+
+    quant("uq", 0, 128, "ut", 0)
+    lst = A("lu", 0, 16)
+    emit("a", lambda: g.scalar.activation(T.uss[:, 0:256], T.uqs[:, 0:128].indirect(ap(lst)), Fn.Copy), [A("uss", 0, 256)], [A("uqs", 0, 128), lst])
+    emit("v", lambda: g.vector.tensor_copy(T.us[:, 0:256].bitcast(dt.uint32), T.uq[:, 0:128].bitcast(dt.uint32).indirect(ap(lst))),
+         [A("us", 0, 256)], [A("uq", 0, 128), lst])
+
+    def consts_rank():
+        for s in range(2):
+            for e in range(4):
+                ts(A("cc1", 4 * s + e, 512, 8), A("jg", 0, 64), col((4, 10)[e % 2]), 1.0 - 2 * s, Op.is_equal, Op.mult)
+        for e in range(4):
+            ts(A("cc1", 512 + e, 1024, 4), A("cc1", e, 512, 4), (2.0, 2.0, -2.0, -2.0)[e], None, Op.mult)
         quant("k1", 0, 256, "cc1", 0)
 
-    def consts_a():
-        fill(A("cst", 2048, 3072), 0.0)
-        fill(A("cst", 3072, 4096), 0.0)
-        for b in range(4):
-            for e in range(b + 1):
-                s = A("cst", 2048 + 512 * b + 4 * (3 + e // 2) + e, 2048 + 512 * b + 512, 64)
-                if e < b:
-                    iota(s, [[0, 8]], 2, 0)
-                else:
-                    select(s, A("two", 0, 8), [[16, 8]], Op.is_gt, 0, -1)
-        fill(A("ct5", 0, 1024), 0.0)
-        fill(A("ct5", 1024, 1280), 0.0)
+    def consts_flags():
+        ts(col(11), col(5), -2.0, 1.0, Op.mult, Op.add)
+        ts(col(12), col(7), -1.0, 1.0, Op.mult, Op.add)
+        ts(col(13), col(6), 32.0, col(3), Op.mult, Op.add)
+        ts(col(14), col(2), 2.0, -31.0, Op.mult, Op.add)
+        ts(col(15), col(2), 2.0, 257.0 - 32 * (10 - NV), Op.mult, Op.add)
+        ts(col(16), col(5), 20.0, None, Op.mult)
+        tt(col(17), col(11), col(12), Op.mult)
+        ts(col(18), col(13), -1.0, -0.5, Op.mult, Op.add)
+        ts(A("aw", 0, 2 * NV), A("ones", 0, 2 * NV), col(15), None, Op.mult)
+        ts(A("aw", 20, 20 + 2 * NV), A("ones", 0, 2 * NV), col(15), -1.0, Op.mult, Op.mult)
+        ts(col(19), col(17), 0.5, None, Op.mult)
+        ts(col(20), col(17), -0.5, None, Op.mult)
+        ts(A("lt", 0, 20), A("lui", 16, 36), col(16), None, Op.add)
+        ts(A("row", 0, 320), A("jq", 0, 320), col(8), -FAR, Op.not_equal, Op.mult)
 
-    def consts_a2():
-        fill(A("fs", 0, 528), 0.0)
-        fill(A("cst", 1536, 2048), 2.0)
-        fill(A("cci", 0, 640), 0.0)
-        for e, c in ((80, -1.0), (86, -1.0), (121, 1.0), (127, 1.0)):
-            fill(A("cci", e, e + 1), c)
+    def consts_order_a():
+        act(A("oa", 0, 512), A("om", 0, 512), Fn.Sign, bias=col(18))
+        act(A("cst", 0, 512), A("oa", 0, 512), Fn.Identity, bias=col(19), scale=col(19))
+        act(A("cst", 512, 1024), A("oa", 0, 512), Fn.Identity, bias=col(19), scale=col(20))
+        fill(A("cst", 1536, 2048), col(17))
         act(A("smk", 0, 80), A("smk", 0, 80), Fn.Sign)
-        fill(A("z80", 0, 80), 0.0)
-        fill(A("st", 0, 8), 0.0)
-        fill(A("vf", 0, 32), 0.0)
 
-    def consts_v():
-        ts(col(3), col(0), 8.0, col(2), Op.mult, Op.add)
+    def within(b, e):
+        return A("cst", 2048 + 512 * b + 4 * (3 + e // 2) + e, 2048 + 512 * b + 512, 32)
+
+    def consts_order_v():
+        ts(A("cst", 1024, 1536), A("om", 0, 512), col(13), col(17), Op.is_equal, Op.mult)
+        for b in range(4):
+            ts(within(b, b), A("jh", 0, 16), col(3), col(17), Op.is_gt, Op.mult)
+            for e in range(b):
+                fill(within(b, e), col(17))
         none, big, small = 1.5 * 2.0 ** 35, 1.5 * 2.0 ** 30, 1.5 * 2.0 ** 26
-        ts(col(8), col(0), 3.0, none, Op.is_ge, Op.mult)
-        for k, v in ((9, big), (10, small)):
-            ts(col(k), col(0), float(k - 9), v, Op.is_equal, Op.mult)
-        for k, v in ((11, none), (12, big), (13, small)):
-            ts(col(k), col(0), float(k - 11), v, Op.is_equal, Op.mult)
-        ts(col(14), col(2), 2.0, None, Op.mult)
-        ts(A("cst", 0, 512), A("om", 0, 512), col(3), 2.0, Op.is_gt, Op.mult)
-        tt(col(19), col(8), col(9), Op.add)
-        tt(col(20), col(8), col(11), Op.add)
-        tt(col(21), col(12), col(13), Op.add)
-        ts(A("cst", 512, 1024), A("om", 0, 512), col(3), 2.0, Op.is_le, Op.mult)
-        ts(col(15), col(0), 32.0, col(14), Op.mult, Op.add)
-        ts(col(16), col(2), -1.0, 8.0, Op.mult, Op.add)
-        tt(col(6), col(19), col(10), Op.add)
-        tt(col(7), col(20), col(21), Op.add)
-        ts(A("cst", 1024, 1536), A("om", 0, 512), col(3), 2.0, Op.is_equal, Op.mult)
-        ts(A("s2", 0, 20), A("s2", 0, 20), col(15), None, Op.add)
-        ts(col(17), col(2), -2.0, 16.0, Op.mult, Op.add)
-        ts(A("pl", 0, 20), A("pl", 0, 20), col(3), 0.5, Op.add, Op.add)
-        ts(A("m16", 0, 320), A("jj", 0, 320), col(0), None, Op.is_equal)
-        ts(A("sz", 0, 20), A("s2", 0, 20), col(16), None, Op.add)
+        ts(col(21), col(1), 10.0, -8.0, Op.is_equal, Op.mult)
+        ts(col(22), col(7), 16383.0, 1.0, Op.mult, Op.add)
+        ts(col(23), col(1), 8.0, col(3), Op.mult, Op.add)
+        tt(col(24), col(21), col(1), Op.add)
+        ts(col(25), col(3), 64.0, 16384.0, Op.add, Op.mult)
+        ts(col(26), col(1), 16.0, col(3), Op.mult, Op.add)
+        ts(col(27), col(3), -2.0, 16.0, Op.mult, Op.add)
+        ts(col(28), col(24), 3.0, none, Op.is_ge, Op.mult)
+        for k, (r, v) in enumerate(((0, big), (1, small), (0, none), (1, big), (2, small))):
+            ts(col(29 + k), col(24), float(r), v, Op.is_equal, Op.mult)
+        ts(col(34), col(22), -1.0, None, Op.mult)
+        ts(col(35), col(26), 2.0, col(25), Op.mult, Op.add)
+        ts(A("pl", 0, 20), A("pl", 0, 20), col(23), 0.5, Op.add, Op.add)
+        ts(col(36), col(28), col(29), col(30), Op.add, Op.add)
+        ts(col(37), col(28), col(31), col(32), Op.add, Op.add)
+        ts(A("s2", 0, 20), A("s2", 0, 20), col(35), None, Op.add)
+        tt(col(38), col(37), col(33), Op.add)
+        for e, c in ((80, 34), (86, 34), (121, 22), (127, 22)):
+            fill(A("cci", e, e + 1), col(c))
+
+    def consts_order_q():
         quant("kc", 0, 512, "cst", 0)
         quant("kc", 512, 512, "cst", 2048)
         quant("ki", 0, 160, "cci", 0)
 
-    flip = [0]
-
-    def other():
-        flip[0] += 1
-        return "vavav"[flip[0] % 5]
-
     def unpack(pair, b, d, bank, q, i):
-        mm(bank, "er", 256 * b + 16 * d, pair, 0, H)
-        k = 5120 * i + 640 * d + 160 * b
+        mm(bank, "er", 240 * b + 16 * d, pair, 0, H)
+        k = 2560 * b + 1280 * i + 160 * d
         if q == "v":
             copy(A("wv", k, k + H), P(bank, H))
         else:
             act(A("wv", k, k + H), P(bank, H), Fn.Copy)
 
-    def by_dma(name, w, d):
-        o, i, k = A(name, w * d, w * d + w), A(name, 0, w), 128 - 16 * d
-        dma("s", T[name][0:k, o[1]:o[2]], T[name][16 * d:128, 0:w], [o], [i], loose=True)
-        dma("s", T[name][k:128, o[1]:o[2]], T[name][0:16 * d, 0:w], [o], [i], loose=True)
+    def by_dma(d):
+        o, i, k = A("wt", TURN * d, TURN * d + 1280), A("wt", 0, 1280), 128 - 16 * d
+        dma("s", T.wt[0:k, o[1]:o[2]], T.wt[16 * d:128, 0:1280], [o], [i], loose=True)
+        dma("s", T.wt[k:128, o[1]:o[2]], T.wt[0:16 * d, 0:1280], [o], [i], loose=True)
 
     def layer(pair, tile, out):
         for b in range(4):
@@ -335,106 +368,107 @@ def rank_program(g, core, T, topo):
         return A("lf", 20 * k, 20 * k + 20)
 
     def TW(b):
-        return A("wt", 320 * b, 320 * b + 9280)
-
-    def WV(b):
-        return A("wv", 160 * b, 160 * b + 9760)
+        return A("wt", 320 * b, 320 * b + 7 * TURN + 320)
 
     def own(gg, b):
-        return A("tr", 32 * b + 16 * gg, 32 * b + 16 * gg + 1)
+        return A("pt", 320 * gg + 32 * b + 31, 320 * gg + 32 * b + 32)
 
-    def t_number(b, d):
-        bank = 6 + b % 2
-        if d == 0:
-            mm(bank, "e0", 128 * b, "xq", 0, C)
-        else:
-            mm(bank, "er", 256 * b + 16 * d, "xq", 0, C)
-        act(A("wt", 1280 * d + 320 * b, 1280 * d + 320 * b + 320), P(bank, C), Fn.Copy)
+    def t_product(b, d, bank):
+        mm(bank, "er", 240 * b + 16 * d, "xq", 0, C)
 
-    def compare(b):
+    def t_out(b, d, bank):
+        act(A("wt", TURN * d + 320 * b, TURN * d + 320 * b + 320), P(bank, C), Fn.Copy)
+
+    def where(kind, k, gg):
+        i = [p[:2] for p in PAIRS].index((kind, k))
+        return "ct%d" % (i // 2), 2 * (i % 2) + gg
+
+    def compare_v(b):
         for gg in range(2):
-            t, e, lo = "ct%d" % (b // 2), 2 * (b % 2) + gg, 32 * b + 32
-            ts(A(t, e, 4 * lo, 4), P(1 + gg, lo), own(gg, b), None, Op.is_lt)
-            if lo < C:
-                ts(A(t, 4 * lo + e, 1280, 4), P(1 + gg, C, lo), own(gg, b), None, Op.is_le)
+            if b > 0:
+                t, e = where("v", b - 1, gg)
+                ts(A(t, e, 128 * b, 4), P(1 + gg, 32 * b), own(gg, b), 2.0, Op.is_lt, Op.mult)
+            if b < NV - 1:
+                t, e = where("v", b, gg)
+                ts(A(t, 128 * b + 128 + e, 128 * NV, 4), P(1 + gg, 32 * NV, 32 * b + 32), own(gg, b), 2.0, Op.is_le, Op.mult)
 
     def compare_a(b):
+        z = [A("zs", 288 * (2 * (b % 2) + gg), 288 * (2 * (b % 2) + gg) + 32 * b) for gg in range(2)]
         for gg in range(2):
-            t, e, lo, z = "ct%d" % (b // 2), 2 * (b % 2) + gg, 32 * b + 32, 320 * ((2 * b + gg) % 4)
-            act(A("zs", z, z + C), P(4 + gg, C), Fn.Sign, bias=own(gg, b), scale=-1.0)
-            act(A(t, e, 4 * lo, 4), A("zs", z, z + lo), Fn.Sign, bias=-0.5)
-            if lo < C:
-                act(A(t, 4 * lo + e, 1280, 4), A("zs", z + lo, z + C), Fn.Sign, bias=0.5)
+            act(z[gg], P(4 + gg, 32 * b), Fn.Sign, bias=own(gg, b), scale=-1.0)
+        for gg in range(2):
+            t, e = where("a", b, gg)
+            act(A(t, e, 128 * b, 4), z[gg], Fn.Sign, bias=-0.5, total=A("acc", 2 * b + gg, 2 * b + gg + 1))
 
-    def add_ranks(t, w, start, stop):
-        quant("cq%d" % t, 0, C, "ct%d" % t, 0)
-        mm(3, "k1", 128 * w, "cq%d" % t, 0, C, start=start, stop=stop)
+    def add_ranks(k, stop=False):
+        n = TILES[k][0][2]
+        quant("cq%d" % k, 0, n, "ct%d" % k, 0)
+        mm(3, "k1", 0, "cq%d" % k, 0, n, start=False, stop=stop)
 
-    def tie_rows():
-        for k in range(2):
-            gather("a", A("ob", 320 * k, 320 * k + 320), A("tr", 0, 320), A("lu", 24 + 20 * k, 44 + 20 * k))
+    def bounds(a, b, summed=True):
+        if summed:
+            ts(A("aw", 2 * a, 2 * b), A("acc", 2 * a, 2 * b), col(14), None, Op.add)
+            ts(A("aw", 20 + 2 * a, 20 + 2 * b), A("acc", 2 * a, 2 * b), col(14), -1.0, Op.add, Op.mult)
+        gather_add(A("sp", 32 * a, 32 * b), A("aw", 0, 40), A("lt", 2 * a, 2 * b), A("row", 32 * a, 32 * b))
+        turn32(A("thr", 32 * a, 32 * b), A("sp", 32 * a, 32 * b))
 
     for rd in range(ROUNDS):
         dst = T.cores[rank ^ MASK[rd]]
-        dma("s", T.wn[:, 0:1280], T.zt[:, :], [A("wn", 0, 1280)], [A("zt", 0, 1280)])
-        dma("s", T.wn[:, 1280:2560], T.zt[:, :], [A("wn", 1280, 2560)], [A("zt", 0, 1280)])
         quant("xq", 0, C, "xin" if rd == 0 else "xn", 0)
-        for bank, k in ((0, 0), (1, 1), (2, 2)):
-            mm(bank, "us", 128 * k, "xq", 0, C)
-        emit("v", lambda: g.vector.transpose(T.tr[:, 0:320], T.ps0[:, 0:320]), [A("tr", 0, 320)], [P(0, 320)])
-        if rd == 0:
-            mm(4, "us", 128, "xq", 0, C)
-            mm(5, "us", 256, "xq", 0, C)
-            consts_early()
-            compare(0)
-            consts_a()
-            tie_rows()
-            compare(1)
-            add_ranks(0, 0, True, False)
-            quant("e0", 0, 512, "est", 0)
-            for b in range(4):
-                for k in range(2):
-                    to = 256 * b + 128 * k
-                    dma("s", T.er[:, to:to + 128].bitcast(dt.uint8), T.e0[:, 128 * b:128 * b + 128].bitcast(dt.uint8), [A("er", to, to + 128)], [A("e0", 128 * b, 128 * b + 128)])
-                    dma("s", T.ers[:, to:to + 128], T.e0s[:, 128 * b:128 * b + 128], [A("ers", to, to + 128)], [A("e0s", 128 * b, 128 * b + 128)])
-        for b in range(4):
-            t_number(b, 0)
+        mm(1, "us", 0, "xq", 0, C)
+        t_product(0, 0, 6)
+        mm(2, "us", 128, "xq", 0, C)
+        t_product(1, 0, 7)
+        t_product(2, 0, 0)
+        mm(4, "us", 0, "xq", 0, C)
+        t_out(0, 0, 6)
+        t_product(3, 0, 6)
+        mm(5, "us", 128, "xq", 0, C)
+        for b, bank in ((1, 7), (2, 0), (3, 6)):
+            t_out(b, 0, bank)
         for d in range(T_PRODUCTS, 8):
-            by_dma("wt", 1280, d)
-        if rd > 0:
-            mm(4, "us", 128, "xq", 0, C)
-            mm(5, "us", 256, "xq", 0, C)
-            tie_rows()
-            compare(0)
-            compare(1)
-            add_ranks(0, 0, True, False)
-        for b in BY_SCALAR:
+            by_dma(d)
+        if rd == 0:
+            consts_rank()
+        for gg in range(2):
+            tt(A("pm", 320 * gg, 320 * gg + 320), P(1 + gg, C), A("tri", 0, 320), Op.min)
+            turn32(A("pt", 320 * gg, 320 * gg + 320), A("pm", 320 * gg, 320 * gg + 320))
+        for gg in range(2):
+            tt(A("cd", gg, 1280, 4), P(1 + gg, C), A("pt", 320 * gg, 320 * gg + 320), Op.is_le)
+        for gg in range(2):
+            turn32(A("cd", 2 + gg, 1280, 4), A("cd", gg, 1280, 4))
+        quant("cdq", 0, C, "cd", 0)
+        mm(3, "k1", 128, "cdq", 0, C, start=True, stop=False)
+        for b in range(9, NV - 1, -1):
             compare_a(b)
         if rd == 0:
-            consts_a2()
-        compare(2)
-        compare(3)
-        add_ranks(1, 0, False, False)
-        compare(4)
-        compare(5)
-        add_ranks(2, 0, False, False)
+            consts_flags()
+            consts_order_a()
+            bounds(0, NV, False)
+        for b in range(NV):
+            compare_v(b)
         if rd == 0:
-            ts(A("m32", 0, 320), A("jj", 320, 640), col(1), None, Op.is_gt)
-        for gg in range(2):
-            o = A("eqt", 320 * gg, 320 * gg + 320)
-            tt(o, P(1 + gg, C), A("ob", 320 * gg, 320 * gg + 320), Op.is_equal)
-            tt(A("ct5", gg, 1280, 4), o, A("m32", 0, 320), Op.mult)
-        add_ranks(5, 0, False, False)
-        for b in range(4):
-            t_number(b, 1)
-        compare(6)
-        compare(7)
-        add_ranks(4, 1, False, False)
+            consts_order_v()
+        last = (9 - NV) // 2
+        add_ranks(0)
+        for k in range(last + 1, len(TILES)):
+            add_ranks(k)
+        for k in range(1, last):
+            add_ranks(k)
         if rd == 0:
-            consts_v()
-        add_ranks(3, 0, False, True)
-        ts(A("hb", 0, 320), P(3, C), 160.0 - 16 * len(BY_SCALAR), 0.5, Op.is_lt, Op.subtract)
-        tt(A("fs", 16, 336), A("hb", 0, 320), A("m16", 0, 320), Op.mult)
+            consts_order_q()
+        later = [(b, d) for d in range(1, T_PRODUCTS) for b in range(4)]
+        t_product(*later[0], 6)
+        t_product(*later[1], 7)
+        bounds(NV + 1, 10)
+        add_ranks(last, True)
+        bounds(NV, NV + 1)
+        tt(A("fs", 16, 336), P(3, C), A("thr", 0, 320), Op.is_lt)
+        t_out(*later[0], 6)
+        t_out(*later[1], 7)
+        for k in (2, 3):
+            t_product(*later[k], 4 + k)
+            t_out(*later[k], 4 + k)
         quant("fq", 0, 132, "fs", 0)
         mm(0, "kc", 0, "fq", 4, 128, True, False)
         mm(0, "kc", 128, "fq", 0, 128, False, True)
@@ -445,16 +479,16 @@ def rank_program(g, core, T, topo):
         mm(3, "kc", 768, "fq", 4, 128)
         scan(A("su", 0, 80), P(0, 80), A("z80", 0, 80), -0.5, Op.add, Op.add)
         mm(0, "kc", 896, "fq", 4, 128)
-        for d in range(2, T_PRODUCTS):
-            for b in range(4):
-                t_number(b, d)
+        for k in range(4, len(later)):
+            t_product(*later[k], 6 + k % 2)
+            t_out(*later[k], 6 + k % 2)
         scan(A("sg", 0, 80), A("smk", 0, 80), P(1, 80), 0.0, Op.mult, Op.add)
         scan(A("st", 8, 88), P(2, 80), A("z80", 0, 80), 0.0, Op.add, Op.add)
         n2, y, h2 = L(0), L(1), L(2)
         tt(A("n2f", 0, 20), A("su", 3, 80, 4), A("sg", 3, 80, 4), Op.mult)
-        ts(A("r1", 0, 80), A("st", 7, 87), col(6), col(6), Op.add, Op.subtract)
+        ts(A("r1", 0, 80), A("st", 7, 87), col(36), col(36), Op.add, Op.subtract)
         tt(n2, A("n2f", 0, 20), A("pl", 0, 20), Op.add)
-        ts(A("r0", 0, 80), A("st", 7, 87), col(7), col(7), Op.add, Op.subtract)
+        ts(A("r0", 0, 80), A("st", 7, 87), col(38), col(38), Op.add, Op.subtract)
         ts(y, n2, 4, 31, Op.arith_shift_right, Op.bitwise_and)
         ts(h2, n2, 14, None, Op.bitwise_and)
         tt(A("dg", 0, 80), A("r1", 0, 80), A("r0", 0, 80), Op.subtract)
@@ -469,17 +503,13 @@ def rank_program(g, core, T, topo):
         copy(A("pos", 0, 20), L(6))
         slots, lst = A("wn", 0, 2560), A("pos", 0, 20)
         emit("v", lambda: g.vector.tensor_copy(ap(slots).indirect(ap(lst)), T.dat[:, 0:320]), [slots], [lst, A("dat", 0, 320)])
-        quant("nq", 0, 320, "wn", 0)
-        quant("nq", 320, 320, "wn", 1280)
-        for s in range(5):
-            mm(1, "nq", 128 * s, "ki", 20 - 2 * s, 128, s == 0, s == 4)
-        tt(L(7), P(1, 20), A("sz", 0, 20), Op.add)
-        tt(L(8), P(1, 20), A("s2", 0, 20), Op.add)
-        ts(L(9), L(7), 7, None, Op.bitwise_and)
-        ts(L(10), L(8), 3, None, Op.arith_shift_right)
-        ts(L(11), L(9), 1280, None, Op.mult)
-        tt(L(12), L(11), L(10), Op.add)
-        copy(A("off", 0, 20), L(12))
+        for a, n in ((0, 256), (256, 256), (512, 128)):
+            quant("nq", a, n, "wn", 4 * a)
+            for s in range(a // 128, (a + n) // 128):
+                mm(1, "nq", 128 * s, "ki", 20 - 2 * s, 128, s == 0, s == 4)
+        tt(L(7), P(1, 20), A("s2", 0, 20), Op.add)
+        ts(L(8), L(7), 3, 7 * TURN + 511, Op.arith_shift_right, Op.bitwise_and)
+        copy(A("off", 0, 20), L(8))
         for b in range(4):
             gather("va"[b % 2], A("gt", b, 640, 4), TW(b), A("off", 10, 20))
         quant("gq", 0, H, "gt", 0)
@@ -488,28 +518,32 @@ def rank_program(g, core, T, topo):
             gather("va"[b % 2], A("ft", b, 640, 4), TW(b), A("off", 0, 10))
         quant("fqq", 0, H, "ft", 0)
         layer("fqq", "at", "aq")
-        for b in range(4):
-            unpack("aq", b, 0, 4 + b, "va"[b % 2], 0)
-        for d in range(A_PRODUCTS, 8):
-            by_dma("wv", 640, d)
+        for k in range(A_EARLY):
+            unpack("aq", k // 8, k % 8, 4 + k % 4, "va"[k % 2], 0)
         layer("gl%d" % rd, "bt", "bq")
         send(dst, "bq", "bl%d" % rd, "ba%d" % rd, "bs%d" % rd)
-        for k in range(4 * (A_PRODUCTS - 1)):
-            unpack("aq", k % 4, 1 + k // 4, 4 + k % 4, other(), 0)
-        ts(L(13), n2, 4, None, Op.arith_shift_right)
-        ts(L(14), n2, 16, None, Op.bitwise_and)
-        ts(L(15), n2, 1, None, Op.bitwise_and)
-        ts(L(16), n2, col(17), None, Op.add)
-        ts(LF(0), y, -0.5, None, Op.mult)
-        ts(LF(1), L(14), 0.96875, None, Op.mult)
-        ts(LF(2), L(15), 5120.0, None, Op.mult)
-        ts(L(17), L(16), 14, None, Op.bitwise_and)
-        tt(LF(3), LF(0), L(13), Op.add)
-        tt(LF(4), LF(1), LF(2), Op.add)
-        ts(LF(5), L(17), 320.0, None, Op.mult)
-        tt(LF(6), LF(3), LF(4), Op.add)
-        tt(LF(7), LF(6), LF(5), Op.add)
-        copy(A("wl", 0, 20), LF(7))
+        if rd < ROUNDS - 1:
+            iota(A("wn", 0, 2560), [[0, 2560]], 0, 0)
+        steps = [lambda: ts(L(13), n2, 4, None, Op.arith_shift_right),
+                 lambda: ts(L(14), n2, 16, None, Op.bitwise_and),
+                 lambda: ts(L(15), n2, 1, None, Op.bitwise_and),
+                 lambda: ts(L(16), n2, col(27), None, Op.add),
+                 lambda: ts(LF(0), y, -0.5, None, Op.mult),
+                 lambda: ts(LF(1), L(14), 0.96875, None, Op.mult),
+                 lambda: ts(LF(2), L(15), 1280.0, None, Op.mult),
+                 lambda: ts(L(17), L(16), 14, None, Op.bitwise_and),
+                 lambda: tt(LF(3), LF(0), L(13), Op.add),
+                 lambda: tt(LF(4), LF(1), LF(2), Op.add),
+                 lambda: ts(LF(5), L(17), 80.0, None, Op.mult),
+                 lambda: tt(LF(6), LF(3), LF(4), Op.add),
+                 lambda: tt(LF(7), LF(6), LF(5), Op.add),
+                 lambda: copy(A("wl", 0, 20), LF(7))]
+        for k in range(A_EARLY, 32):
+            unpack("aq", k // 8, k % 8, k % 8, "aav"[k % 3], 0)
+            if steps:
+                steps.pop(0)()
+        for step in steps:
+            step()
         if rd == 0:
             quant("vq", 0, 128, "vt", 0)
         if rd == ROUNDS - 1:
@@ -518,34 +552,18 @@ def rank_program(g, core, T, topo):
             ts(A("it", 0, 20), A("pl", 0, 20), 0.5, None, Op.mult)
             tt(A("dg", 0, 20), A("r0", 0, 20), A("r1", 0, 20), Op.add)
             tt(A("vf", 0, 20), A("dg", 0, 20), A("it", 0, 20), Op.add)
-            emit("v", lambda: g.vector.transpose(T.vtr[:, 0:32], T.vf[:, 0:32]), [A("vtr", 0, 32)], [A("vf", 0, 32)])
+            turn32(A("vtr", 0, 32), A("vf", 0, 32))
             for k in range(8):
                 a, o = k // 2, 16 * (k % 2)
                 dma("s", T.op[k:k + 1, :], T.vtr[32 * a:32 * a + 20, o:o + 16], [], [A("vtr", 0, 32)])
 
-        def add_gathered(b, a, n):
-            o, win, t2 = A("xn", 4 * a + b, 4 * (a + n), 4), WV(b), A("wt", 320 * b + a, 320 * b + a + n)
-            li = A("wl", a // 16, (a + n) // 16)
-            emit("v", lambda: g.vector.tensor_tensor(ap(o), ap(win).indirect(ap(li)), ap(t2), Op.add), [o], [win, li, t2])
-
-        def gather_v(b, slot, a, n):
-            gather("a", A("vb", 320 * slot + a, 320 * slot + a + n), WV(b), A("wl", a // 16, (a + n) // 16))
-
-        def add_v(b, slot, a, n):
-            tt(A("xn", 4 * a + b, 4 * (a + n), 4), A("vb", 320 * slot + a, 320 * slot + a + n), A("wt", 320 * b + a, 320 * b + a + n), Op.add)
-
         land = "bl%d" % rd
         for b in range(4):
+            nv = B_BY_VECTOR[b]
             for d in range(8):
-                unpack(land, b, d, d, other(), 1)
-        gather_v(1, 0, 0, 320)
-        add_gathered(0, 0, 320)
-        gather_v(2, 1, 0, 320)
-        add_v(1, 0, 0, 320)
-        add_gathered(3, 0, 160)
-        gather_v(3, 0, 160, 160)
-        add_v(2, 1, 0, 320)
-        add_v(3, 0, 160, 160)
+                by_v = d % 2 == 0 and d // 2 < nv if b == 0 else d >= 8 - nv
+                unpack(land, b, d, d, "v" if by_v else "a", 1)
+            gather_add(A("xn", b, 1280, 4), A("wv", 2560 * b, 2560 * b + 2560), A("wl", 0, 20), A("wt", 320 * b, 320 * b + 320))
 
     quant("xq", 0, C, "xn", 0)
     dma("s", T.oc[:, :], T.xq[:, 0:C].bitcast(dt.uint8), [], [A("xq", 0, C)])

@@ -8,11 +8,15 @@ T_PRODUCTS = 4
 NV = 5
 TURN = 2048
 FAR = 2.0 ** 90
-A_EARLY = 8
-B_BY_VECTOR = [4, 3, 2, 2]
+A_EARLY = 12
+B_OUT = ["vavavava", "avvvvava", "avvvvava", "avvvvava"]
+FUSED = ["vavavava", "aaaaavvv", "aaaaaavv", "aaaaaavv"]
+B_GATHER, B_ADD = 1, 6
 
 PAIRS = [("a", b, 32 * b) for b in range(9, NV - 1, -1)] + [("v", k, 32 * NV) for k in range(NV - 1)]
 TILES = [PAIRS[k:k + 2] for k in range(0, len(PAIRS), 2)]
+LAST = (9 - NV) // 2
+CUT = 10 - 2 * LAST
 
 SCRATCH = {}
 
@@ -28,7 +32,7 @@ def _mx(name, cols):
 
 for _k in range(8):
     SCRATCH["ps%d" % _k] = ("psum", [128, 512], F32)
-for _n, _w in (("xin", 1280), ("xn", 1280), ("ut", 512), ("vt", 512), ("ones", 512), ("zt", 1280), ("zs", 1152), ("cd", 1280),
+for _n, _w in (("xin", 1280), ("xn", 1280), ("ut", 512), ("vt", 512), ("ones", 512), ("zt", 512), ("vb", 1280), ("zs", 1152), ("cd", 1280),
                ("fs", 528), ("dat", 320), ("wn", 2560), ("wt", 7 * TURN + 1280), ("wv", 10240), ("gt", 640), ("ft", 640), ("at", 640),
                ("bt", 640), ("tri", 320), ("row", 320), ("est", 1936), ("cst", 4096), ("cc1", 1024), ("cci", 640), ("om", 512), ("oa", 512),
                ("j32", 320), ("jq", 320), ("j128", 128), ("jg", 64), ("jh", 16)):
@@ -37,8 +41,8 @@ _mx("cdq", 320)
 for _k, _t in enumerate(TILES):
     _sb("ct%d" % _k, 4 * _t[0][2], BF)
     _mx("cq%d" % _k, _t[0][2])
-for _n, _w in (("pm", 640), ("pt", 640), ("acc", 24), ("aw", 40), ("sp", 320), ("thr", 320), ("su", 80), ("sg", 80), ("st", 96), ("r1", 80),
-               ("r0", 80), ("dg", 80), ("n2f", 32), ("vf", 32), ("vtr", 32), ("sc", 40), ("pl", 20), ("s2", 20), ("it", 20),
+for _n, _w in (("pm", 640), ("pt", 640), ("acc", 24), ("aw", 48), ("sp", 320), ("thr", 320), ("su", 80), ("sg", 80), ("st", 96), ("r1", 160),
+               ("r0", 160), ("dg", 80), ("n2f", 32), ("vf", 32), ("vtr", 32), ("sc", 40), ("pl", 20), ("s2", 20),
                ("smk", 80), ("z80", 80), ("yo", 320), ("lf", 200)):
     _sb(_n, _w, F32)
 for _n, _w in (("pi", 16), ("lui", 40), ("li", 400)):
@@ -182,7 +186,7 @@ def rank_program(g, core, T, topo):
     def send(dst, src, land, sem, done):
         rid, pid, _ = topo.addr(dst)
         eng = topo.engines(core, dst)
-        ec, es = eng[0::2], eng[1::4]
+        ec, es = eng, eng
         total = len(ec) + len(es)
         need("p", [r[3] for nm in (src, src + "s") for r in log[nm] if r[1]])
         g.remote_dma(T[land][:, 0:H].bitcast(dt.uint8), T[src][:, 0:H].bitcast(dt.uint8), T.sem[sem], T.sem[done], pid, rid, sum(1 << e for e in ec))
@@ -215,61 +219,72 @@ def rank_program(g, core, T, topo):
 
     iota(A("pi", 0, 1), [[0, 1]], 0, 1)
     iota(A("j128", 0, 128), [[1, 128]], 0, 0)
-    iota(A("lui", 0, 8), [[32, 4], [0, 2]], 0, 0)
-    iota(A("lui", 8, 16), [[32, 4], [0, 2]], 16, 0)
+    iota(A("lui", 0, 16), [[16, 2], [32, 4], [0, 2]], 0, 0)
+    iota(A("om", 0, 512), [[1, 8], [8, 16], [-8, 4]], 0, 0)
     iota(A("j32", 0, 320), [[0, 10], [1, 32]], 0, 0)
     iota(A("jg", 0, 64), [[1, 8], [0, 8]], 0, 0)
-    iota(A("om", 0, 512), [[1, 8], [8, 16], [-8, 4]], 0, 0)
     iota(A("jq", 0, 320), [[0, 40], [1, 4], [0, 2]], 0, 0)
-    iota(A("lui", 16, 36), [[1, 20]], 0, 0)
+    for a, b in ((0, NV), (NV, CUT), (CUT, 10)):
+        iota(A("lui", 16 + 2 * a, 16 + 2 * b), [[2, 2 * (b - a)]], 4 * a % 8, 0)
     iota(A("jh", 0, 16), [[1, 8], [0, 2]], 0, 0)
+    blank = [A("fs", 0, 16), A("fs", 336, 528), A("z80", 0, 80), A("st", 0, 8), A("vf", 0, 32)]
+    for k, t in enumerate(TILES):
+        a = t[1][2] if len(t) > 1 else 0
+        if a < t[0][2]:
+            blank = [A("ct%d" % k, 4 * a + e, 4 * t[0][2], 4) for e in (2, 3)] + blank
+    for s in blank:
+        iota(s, [[0, len(range(s[1], s[2], s[3]))]], 0, 0)
     iota(A("smk", 0, 80), [[0, 20], [1, 4]], 0, 0)
-    iota(A("pl", 0, 20), [[128, 20]], 0, 0)
-    iota(A("s2", 0, 20), [[0, 2], [512, 5], [16, 2]], 0, 0)
+    iota(A("pl", 0, 20), [[128, 20]], 0, 8)
+    iota(A("s2", 0, 20), [[0, 2], [512, 5], [16, 2]], 64 * 16384, 32)
+    iota(A("wn", 0, 2560), [[0, 2560]], 0, 0)
+
+    def affine(o, i, scale, bias):
+        act(o, i, Fn.Identity, bias=bias, scale=scale)
 
     memset(A("ones", 0, 512), 1.0)
-    memset(A("zt", 0, 1280), 0.0)
-    memset(A("est", 0, 1936), 0.0)
-    for k, (shift, keep) in enumerate(((0, 15), (0, 31), (4, 7), (4, 6), (0, 1), (1, 3), (3, 1), (2, 3))):
+    memset(A("zt", 0, 512), 0.0)
+    for k, (shift, keep) in enumerate(((0, 15), (0, 31), (4, 7), (4, 6), (0, 1), (1, 3), (3, 1), (2, 3), (0, 7))):
         ts(pcol(k + 1), pcol(0), shift, keep, Op.arith_shift_right, Op.bitwise_and)
-    copy(A("sc", 0, 9), A("pi", 0, 9))
+    memset(A("est", 0, 968), 0.0)
+    copy(A("sc", 0, 10), A("pi", 0, 10))
+    fill(A("est", 968, 1480), 0.0)
+    fill(A("est", 1480, 1936), 0.0)
+    copy(A("lu", 0, 16), A("lui", 0, 16))
     for k in range(2):
         ts(A("est", 969 * k + 2, 969 * k + 514, 4), A("j128", 0, 128), col(0), None, Op.is_equal)
         ts(A("est", 969 * k + 514, 969 * k + 962, 4), A("j128", 0, 112), col(0), None, Op.is_equal)
-    ts(col(9), col(2), 0.5, None, Op.add)
-    ts(col(10), col(4), 1.0, None, Op.add)
-    copy(A("lu", 0, 16), A("lui", 0, 16))
-    for b, at in enumerate((2, 970, 0, 968)):
-        quant("er", 240 * b, 240, "est", at)
-    ts(A("tri", 0, 320), A("j32", 0, 320), col(9), -FAR, Op.subtract, Op.mult)
+    affine(col(11), col(5), -2.0, 1.0)
+    affine(col(12), col(7), -1.0, 1.0)
+    affine(col(13), col(6), 32.0, col(3))
+    affine(col(21), col(2), 1.0, 0.5)
+    affine(col(17), col(11), col(12), 0.0)
+    affine(col(18), col(13), -1.0, -0.5)
+    affine(col(10), col(4), 1.0, 1.0)
+    affine(col(19), col(17), 0.5, 0.0)
+    affine(col(20), col(17), -0.5, 0.0)
+    quant("er", 0, 240, "est", 2)
+    quant("er", 480, 240, "est", 0)
 
-    for q, o, w in (("s", "wn", 0), ("s", "wn", 1280)):
-        dma(q, T[o][:, w:w + 1280], T.zt[:, :], [A(o, w, w + 1280)], [A("zt", 0, 1280)])
-    for w in (2048, 3072):
-        dma("s", T.cst[:, w:w + 1024], T.zt[:, 0:1024], [A("cst", w, w + 1024)], [A("zt", 0, 1024)])
+    for o, w, n in [("cst", w, 512) for w in range(2048, 4096, 512)] + [("cci", 0, 512), ("cci", 512, 128)]:
+        dma("s", T[o][:, w:w + n], T.zt[:, 0:n], [A(o, w, w + n)], [A("zt", 0, n)])
     dma("s", T.wq[:, :].bitcast(dt.uint8), T.wc[:, :], [A("wq", 0, 512)], [])
     dma("s", T.wqs[:, :], T.ws[:, :], [A("wqs", 0, 512)], [])
     dma("s", T.vt[:, :], T.v[:, :], [A("vt", 0, 512)], [])
-
-    for k, t in enumerate(TILES):
-        wide = t[0][2]
-        for e in (2, 3):
-            a = t[1][2] if len(t) > 1 else 0
-            if a < wide:
-                fill(A("ct%d" % k, 4 * a + e, 4 * wide, 4), 0.0)
-    fill(A("fs", 0, 16), 0.0)
-    fill(A("fs", 336, 528), 0.0)
-    fill(A("cci", 0, 512), 0.0)
-    fill(A("cci", 512, 640), 0.0)
-    fill(A("z80", 0, 80), 0.0)
-    fill(A("st", 0, 8), 0.0)
-    fill(A("vf", 0, 32), 0.0)
 
     quant("uq", 0, 128, "ut", 0)
     lst = A("lu", 0, 16)
     emit("a", lambda: g.scalar.activation(T.uss[:, 0:256], T.uqs[:, 0:128].indirect(ap(lst)), Fn.Copy), [A("uss", 0, 256)], [A("uqs", 0, 128), lst])
     emit("v", lambda: g.vector.tensor_copy(T.us[:, 0:256].bitcast(dt.uint32), T.uq[:, 0:128].bitcast(dt.uint32).indirect(ap(lst))),
          [A("us", 0, 256)], [A("uq", 0, 128), lst])
+    quant("er", 240, 240, "est", 970)
+    quant("er", 720, 240, "est", 968)
+    ts(A("tri", 0, 320), A("j32", 0, 320), col(21), -FAR, Op.subtract, Op.mult)
+
+    act(A("oa", 0, 512), A("om", 0, 512), Fn.Sign, bias=col(18))
+    fill(A("cst", 1536, 2048), col(17))
+    affine(A("cst", 0, 512), A("oa", 0, 512), col(19), col(19))
+    affine(A("cst", 512, 1024), A("oa", 0, 512), col(20), col(19))
 
     def consts_rank():
         for s in range(2):
@@ -280,27 +295,13 @@ def rank_program(g, core, T, topo):
         quant("k1", 0, 256, "cc1", 0)
 
     def consts_flags():
-        ts(col(11), col(5), -2.0, 1.0, Op.mult, Op.add)
-        ts(col(12), col(7), -1.0, 1.0, Op.mult, Op.add)
-        ts(col(13), col(6), 32.0, col(3), Op.mult, Op.add)
         ts(col(14), col(2), 2.0, -31.0, Op.mult, Op.add)
         ts(col(15), col(2), 2.0, 257.0 - 32 * (10 - NV), Op.mult, Op.add)
-        ts(col(16), col(5), 20.0, None, Op.mult)
-        tt(col(17), col(11), col(12), Op.mult)
-        ts(col(18), col(13), -1.0, -0.5, Op.mult, Op.add)
-        ts(A("aw", 0, 2 * NV), A("ones", 0, 2 * NV), col(15), None, Op.mult)
-        ts(A("aw", 20, 20 + 2 * NV), A("ones", 0, 2 * NV), col(15), -1.0, Op.mult, Op.mult)
-        ts(col(19), col(17), 0.5, None, Op.mult)
-        ts(col(20), col(17), -0.5, None, Op.mult)
-        ts(A("lt", 0, 20), A("lui", 16, 36), col(16), None, Op.add)
+        ts(col(24), col(2), -2.0, 31.0, Op.mult, Op.add)
         ts(A("row", 0, 320), A("jq", 0, 320), col(8), -FAR, Op.not_equal, Op.mult)
-
-    def consts_order_a():
-        act(A("oa", 0, 512), A("om", 0, 512), Fn.Sign, bias=col(18))
-        act(A("cst", 0, 512), A("oa", 0, 512), Fn.Identity, bias=col(19), scale=col(19))
-        act(A("cst", 512, 1024), A("oa", 0, 512), Fn.Identity, bias=col(19), scale=col(20))
-        fill(A("cst", 1536, 2048), col(17))
-        act(A("smk", 0, 80), A("smk", 0, 80), Fn.Sign)
+        ts(A("aw", 0, 4 * NV, 2), A("ones", 0, 2 * NV), col(15), None, Op.mult)
+        ts(A("aw", 1, 4 * NV, 2), A("ones", 0, 2 * NV), col(15), -1.0, Op.mult, Op.mult)
+        ts(A("lt", 0, 20), A("lui", 16, 36), col(5), None, Op.add)
 
     def within(b, e):
         return A("cst", 2048 + 512 * b + 4 * (3 + e // 2) + e, 2048 + 512 * b + 512, 32)
@@ -310,32 +311,32 @@ def rank_program(g, core, T, topo):
         for b in range(4):
             ts(within(b, b), A("jh", 0, 16), col(3), col(17), Op.is_gt, Op.mult)
             for e in range(b):
-                fill(within(b, e), col(17))
-        none, big, small = 1.5 * 2.0 ** 35, 1.5 * 2.0 ** 30, 1.5 * 2.0 ** 26
-        ts(col(21), col(1), 10.0, -8.0, Op.is_equal, Op.mult)
-        ts(col(22), col(7), 16383.0, 1.0, Op.mult, Op.add)
-        ts(col(23), col(1), 8.0, col(3), Op.mult, Op.add)
-        tt(col(24), col(21), col(1), Op.add)
-        ts(col(25), col(3), 64.0, 16384.0, Op.add, Op.mult)
-        ts(col(26), col(1), 16.0, col(3), Op.mult, Op.add)
-        ts(col(27), col(3), -2.0, 16.0, Op.mult, Op.add)
-        ts(col(28), col(24), 3.0, none, Op.is_ge, Op.mult)
-        for k, (r, v) in enumerate(((0, big), (1, small), (0, none), (1, big), (2, small))):
-            ts(col(29 + k), col(24), float(r), v, Op.is_equal, Op.mult)
-        ts(col(34), col(22), -1.0, None, Op.mult)
-        ts(col(35), col(26), 2.0, col(25), Op.mult, Op.add)
-        ts(A("pl", 0, 20), A("pl", 0, 20), col(23), 0.5, Op.add, Op.add)
-        ts(col(36), col(28), col(29), col(30), Op.add, Op.add)
-        ts(col(37), col(28), col(31), col(32), Op.add, Op.add)
-        ts(A("s2", 0, 20), A("s2", 0, 20), col(35), None, Op.add)
-        tt(col(38), col(37), col(33), Op.add)
-        for e, c in ((80, 34), (86, 34), (121, 22), (127, 22)):
-            fill(A("cci", e, e + 1), col(c))
-
-    def consts_order_q():
+                ts(within(b, e), A("ones", 0, 16), col(17), None, Op.mult)
         quant("kc", 0, 512, "cst", 0)
         quant("kc", 512, 512, "cst", 2048)
+
+    def consts_lists_a():
+        act(A("smk", 0, 80), A("smk", 0, 80), Fn.Sign)
+        affine(col(23), col(3), -127.0, 0.5)
+        affine(col(22), col(7), 16383.0, 1.0)
+        affine(col(34), col(7), -16383.0, -1.0)
+        affine(col(25), col(3), 16386.0 - 512, 0.0)
+        affine(A("pl", 0, 20), A("pl", 0, 20), 1.0, col(23))
+        for e, c in ((80, 34), (86, 34), (121, 22), (127, 22)):
+            fill(A("cci", e, e + 1), col(c))
+        affine(A("s2", 0, 20), A("s2", 0, 20), 1.0, col(25))
+        affine(col(27), col(3), -2.0, 16.0)
+
+    def consts_digits():
+        ts(col(29), col(1), 0.0, 1.5 * 2.0 ** 30, Op.is_equal, Op.mult)
+        ts(col(30), col(1), 1.0, 1.5 * 2.0 ** 26, Op.is_equal, Op.mult)
+        ts(col(31), col(9), 2.0, 1.5 * 2.0 ** 26, Op.is_equal, Op.mult)
         quant("ki", 0, 160, "cci", 0)
+        tt(col(36), col(29), col(30), Op.add)
+        ts(col(32), col(29), 32.0, col(31), Op.mult, Op.add)
+        ts(col(38), col(30), 16.0, col(32), Op.mult, Op.add)
+        affine(col(37), col(36), -1.0, 0.0)
+        affine(col(39), col(38), -1.0, 0.0)
 
     def unpack(pair, b, d, bank, q, i):
         mm(bank, "er", 240 * b + 16 * d, pair, 0, H)
@@ -344,6 +345,16 @@ def rank_program(g, core, T, topo):
             copy(A("wv", k, k + H), P(bank, H))
         else:
             act(A("wv", k, k + H), P(bank, H), Fn.Copy)
+
+    def halves(q, b, i):
+        k = 2560 * b + 1280 * i
+        o, src = A("wv", k + 640, k + 1280), A("wv", k, k + 640)
+        for to, fr in ((0, 64), (64, 0)):
+            x, w = T.wv[to:to + 64, k + 640:k + 1280], T.wv[fr:fr + 64, k:k + 640]
+            if q == "s":
+                dma("s", x, w, [o], [src], loose=True)
+            else:
+                emit("v", lambda: g.vector.tensor_copy(x, w), [o], [src], loose=True)
 
     def by_dma(d):
         o, i, k = A("wt", TURN * d, TURN * d + 1280), A("wt", 0, 1280), 128 - 16 * d
@@ -392,25 +403,39 @@ def rank_program(g, core, T, topo):
                 t, e = where("v", b, gg)
                 ts(A(t, 128 * b + 128 + e, 128 * NV, 4), P(1 + gg, 32 * NV, 32 * b + 32), own(gg, b), 2.0, Op.is_le, Op.mult)
 
+    def zs(b, gg):
+        return A("zs", 288 * (2 * (b % 2) + gg), 288 * (2 * (b % 2) + gg) + 32 * b)
+
+    def signs(b, gg):
+        act(zs(b, gg), P(4 + gg, 32 * b), Fn.Sign, bias=own(gg, b), scale=-1.0)
+
+    def sums(b, gg):
+        t, e = where("a", b, gg)
+        act(A(t, e, 128 * b, 4), zs(b, gg), Fn.Sign, bias=-0.5, total=A("acc", 2 * b + gg, 2 * b + gg + 1))
+
     def compare_a(b):
-        z = [A("zs", 288 * (2 * (b % 2) + gg), 288 * (2 * (b % 2) + gg) + 32 * b) for gg in range(2)]
-        for gg in range(2):
-            act(z[gg], P(4 + gg, 32 * b), Fn.Sign, bias=own(gg, b), scale=-1.0)
-        for gg in range(2):
-            t, e = where("a", b, gg)
-            act(A(t, e, 128 * b, 4), z[gg], Fn.Sign, bias=-0.5, total=A("acc", 2 * b + gg, 2 * b + gg + 1))
+        for step in (signs, sums):
+            for gg in range(2):
+                step(b, gg)
 
     def add_ranks(k, stop=False):
         n = TILES[k][0][2]
         quant("cq%d" % k, 0, n, "ct%d" % k, 0)
         mm(3, "k1", 0, "cq%d" % k, 0, n, start=False, stop=stop)
 
-    def bounds(a, b, summed=True):
-        if summed:
-            ts(A("aw", 2 * a, 2 * b), A("acc", 2 * a, 2 * b), col(14), None, Op.add)
-            ts(A("aw", 20 + 2 * a, 20 + 2 * b), A("acc", 2 * a, 2 * b), col(14), -1.0, Op.add, Op.mult)
-        gather_add(A("sp", 32 * a, 32 * b), A("aw", 0, 40), A("lt", 2 * a, 2 * b), A("row", 32 * a, 32 * b))
+    def signed(a, b):
+        affine(A("aw", 4 * a, 4 * b, 2), A("acc", 2 * a, 2 * b), 1.0, col(14))
+        affine(A("aw", 4 * a + 1, 4 * b, 2), A("acc", 2 * a, 2 * b), -1.0, col(24))
+
+    def spread(a, b):
+        gather_add(A("sp", 32 * a, 32 * b), A("aw", 4 * a // 8 * 8, 4 * b), A("lt", 2 * a, 2 * b), A("row", 32 * a, 32 * b))
+
+    def mirror(a, b):
         turn32(A("thr", 32 * a, 32 * b), A("sp", 32 * a, 32 * b))
+
+    def bounds(a, b):
+        spread(a, b)
+        mirror(a, b)
 
     for rd in range(ROUNDS):
         dst = T.cores[rank ^ MASK[rd]]
@@ -420,49 +445,56 @@ def rank_program(g, core, T, topo):
         mm(2, "us", 128, "xq", 0, C)
         t_product(1, 0, 7)
         t_product(2, 0, 0)
+        t_product(3, 0, 3)
         mm(4, "us", 0, "xq", 0, C)
-        t_out(0, 0, 6)
-        t_product(3, 0, 6)
         mm(5, "us", 128, "xq", 0, C)
-        for b, bank in ((1, 7), (2, 0), (3, 6)):
+        for b, bank in ((0, 6), (1, 7), (2, 0), (3, 3)):
             t_out(b, 0, bank)
         for d in range(T_PRODUCTS, 8):
             by_dma(d)
         if rd == 0:
             consts_rank()
-        for gg in range(2):
-            tt(A("pm", 320 * gg, 320 * gg + 320), P(1 + gg, C), A("tri", 0, 320), Op.min)
-            turn32(A("pt", 320 * gg, 320 * gg + 320), A("pm", 320 * gg, 320 * gg + 320))
-        for gg in range(2):
-            tt(A("cd", gg, 1280, 4), P(1 + gg, C), A("pt", 320 * gg, 320 * gg + 320), Op.is_le)
-        for gg in range(2):
-            turn32(A("cd", 2 + gg, 1280, 4), A("cd", gg, 1280, 4))
+        steps = (lambda gg: tt(A("pm", 320 * gg, 320 * gg + 320), P(1 + gg, C), A("tri", 0, 320), Op.min),
+                 lambda gg: turn32(A("pt", 320 * gg, 320 * gg + 320), A("pm", 320 * gg, 320 * gg + 320)),
+                 lambda gg: tt(A("cd", gg, 1280, 4), P(1 + gg, C), A("pt", 320 * gg, 320 * gg + 320), Op.is_le),
+                 lambda gg: turn32(A("cd", 2 + gg, 1280, 4), A("cd", gg, 1280, 4)))
+        for k, gg in ((0, 0), (1, 0), (0, 1), (2, 0), (1, 1), (3, 0), (2, 1)):
+            steps[k](gg)
+        compare_v(0)
+        steps[3](1)
+        compare_v(1)
         quant("cdq", 0, C, "cd", 0)
         mm(3, "k1", 128, "cdq", 0, C, start=True, stop=False)
-        for b in range(9, NV - 1, -1):
-            compare_a(b)
+        last, cut = LAST, CUT
         if rd == 0:
             consts_flags()
-            consts_order_a()
-            bounds(0, NV, False)
-        for b in range(NV):
+        for gg in range(2):
+            for b in (9, 8):
+                signs(b, gg)
+            for b in (9, 8):
+                sums(b, gg)
+        for b in range(7, NV - 1, -1):
+            compare_a(b)
+            if b in (cut, NV):
+                signed(b, 10 if b == cut else cut)
+        if rd == 0:
+            consts_lists_a()
+        for b in range(2, NV):
             compare_v(b)
-        if rd == 0:
-            consts_order_v()
-        last = (9 - NV) // 2
-        add_ranks(0)
-        for k in range(last + 1, len(TILES)):
-            add_ranks(k)
-        for k in range(1, last):
-            add_ranks(k)
-        if rd == 0:
-            consts_order_q()
         later = [(b, d) for d in range(1, T_PRODUCTS) for b in range(4)]
+        for k in [0] + list(range(last + 1, len(TILES))):
+            add_ranks(k)
         t_product(*later[0], 6)
         t_product(*later[1], 7)
-        bounds(NV + 1, 10)
+        if rd == 0:
+            consts_order_v()
+            bounds(0, NV)
+        for k in range(1, last):
+            add_ranks(k)
+        bounds(cut, 10)
         add_ranks(last, True)
-        bounds(NV, NV + 1)
+        spread(NV, cut)
+        mirror(NV, cut)
         tt(A("fs", 16, 336), P(3, C), A("thr", 0, 320), Op.is_lt)
         t_out(*later[0], 6)
         t_out(*later[1], 7)
@@ -470,32 +502,36 @@ def rank_program(g, core, T, topo):
             t_product(*later[k], 4 + k)
             t_out(*later[k], 4 + k)
         quant("fq", 0, 132, "fs", 0)
+        mm(2, "kc", 384, "fq", 4, 128)
         mm(0, "kc", 0, "fq", 4, 128, True, False)
         mm(0, "kc", 128, "fq", 0, 128, False, True)
         mm(1, "kc", 256, "fq", 4, 128)
-        mm(2, "kc", 384, "fq", 4, 128)
         mm(4, "kc", 512, "fq", 4, 128)
         mm(5, "kc", 640, "fq", 4, 128)
         mm(3, "kc", 768, "fq", 4, 128)
+        if rd == 0:
+            consts_digits()
+        scan(A("st", 8, 88), P(2, 80), A("z80", 0, 80), 0.0, Op.add, Op.add)
         scan(A("su", 0, 80), P(0, 80), A("z80", 0, 80), -0.5, Op.add, Op.add)
         mm(0, "kc", 896, "fq", 4, 128)
+        scan(A("sg", 0, 80), A("smk", 0, 80), P(1, 80), 0.0, Op.mult, Op.add)
+        for k in (0, 1):
+            affine(A("r%d" % k, 80, 160), A("st", 7, 87), 1.0, col((38, 36)[k]))
+        for k in (0, 1):
+            affine(A("r%d" % k, 0, 80), A("r%d" % k, 80, 160), 1.0, col((39, 37)[k]))
         for k in range(4, len(later)):
             t_product(*later[k], 6 + k % 2)
             t_out(*later[k], 6 + k % 2)
-        scan(A("sg", 0, 80), A("smk", 0, 80), P(1, 80), 0.0, Op.mult, Op.add)
-        scan(A("st", 8, 88), P(2, 80), A("z80", 0, 80), 0.0, Op.add, Op.add)
         n2, y, h2 = L(0), L(1), L(2)
         tt(A("n2f", 0, 20), A("su", 3, 80, 4), A("sg", 3, 80, 4), Op.mult)
-        ts(A("r1", 0, 80), A("st", 7, 87), col(36), col(36), Op.add, Op.subtract)
         tt(n2, A("n2f", 0, 20), A("pl", 0, 20), Op.add)
-        ts(A("r0", 0, 80), A("st", 7, 87), col(38), col(38), Op.add, Op.subtract)
+        tt(A("dg", 0, 80), A("r1", 0, 80), A("r0", 0, 80), Op.subtract)
         ts(y, n2, 4, 31, Op.arith_shift_right, Op.bitwise_and)
         ts(h2, n2, 14, None, Op.bitwise_and)
-        tt(A("dg", 0, 80), A("r1", 0, 80), A("r0", 0, 80), Op.subtract)
+        tt(A("dat", 0, 320, 4), P(4, 80), A("dg", 0, 80), Op.add)
         ts(L(3), y, -14, None, Op.mult)
         ts(L(4), h2, 31, None, Op.mult)
-        for b, bank in ((0, 4), (1, 5)):
-            tt(A("dat", b, 320, 4), P(bank, 80), A("dg", 0, 80), Op.add)
+        tt(A("dat", 1, 320, 4), P(5, 80), A("dg", 0, 80), Op.add)
         tt(L(5), L(3), n2, Op.add)
         tt(A("dat", 2, 320, 4), P(3, 80), A("dg", 0, 80), Op.add)
         tt(L(6), L(5), L(4), Op.add)
@@ -549,21 +585,42 @@ def rank_program(g, core, T, topo):
         if rd == ROUNDS - 1:
             ts(A("r0", 0, 20), A("sg", 3, 80, 4), -639.75, None, Op.mult)
             ts(A("r1", 0, 20), A("n2f", 0, 20), 0.5, 639.75, Op.mult, Op.add)
-            ts(A("it", 0, 20), A("pl", 0, 20), 0.5, None, Op.mult)
+            ts(LF(8), A("pl", 0, 20), 0.5, None, Op.mult)
             tt(A("dg", 0, 20), A("r0", 0, 20), A("r1", 0, 20), Op.add)
-            tt(A("vf", 0, 20), A("dg", 0, 20), A("it", 0, 20), Op.add)
+            tt(A("vf", 0, 20), A("dg", 0, 20), LF(8), Op.add)
             turn32(A("vtr", 0, 32), A("vf", 0, 32))
             for k in range(8):
                 a, o = k // 2, 16 * (k % 2)
                 dma("s", T.op[k:k + 1, :], T.vtr[32 * a:32 * a + 20, o:o + 16], [], [A("vtr", 0, 32)])
 
         land = "bl%d" % rd
+        def spliced(q, b, a, n):
+            gather(q, A("vb", 320 * b + a, 320 * b + a + n), A("wv", 2560 * b, 2560 * b + 2560), A("wl", a // 16, (a + n) // 16))
+
+        def add(b, a, n):
+            tt(A("xn", 4 * a + b, 4 * (a + n), 4), A("vb", 320 * b + a, 320 * b + a + n), P(6 + b % 2, a + n, a), Op.add)
+
+        if FUSED:
+            for b in range(4):
+                for d, q in enumerate(FUSED[b]):
+                    unpack(land, b, d, d, q, 1)
+                gather_add(A("xn", b, 1280, 4), A("wv", 2560 * b, 2560 * b + 2560), A("wl", 0, 20), A("wt", 320 * b, 320 * b + 320))
+            continue
+        t_product(0, 0, 6)
+        t_product(1, 0, 7)
         for b in range(4):
-            nv = B_BY_VECTOR[b]
-            for d in range(8):
-                by_v = d % 2 == 0 and d // 2 < nv if b == 0 else d >= 8 - nv
-                unpack(land, b, d, d, "v" if by_v else "a", 1)
-            gather_add(A("xn", b, 1280, 4), A("wv", 2560 * b, 2560 * b + 2560), A("wl", 0, 20), A("wt", 320 * b, 320 * b + 320))
+            for d, q in enumerate(B_OUT[b]):
+                unpack(land, b, d, (8 * b + d) % 6, q, 1)
+                if b > 0 and d == B_GATHER:
+                    spliced("a", b - 1, 0, C)
+                if b > 0 and d == B_ADD:
+                    add(b - 1, 0, C)
+            if b > 1:
+                t_product(b, 0, 6 + b % 2)
+        spliced("v", 3, 0, H)
+        spliced("a", 3, H, H)
+        add(3, 0, H)
+        add(3, H, H)
 
     quant("xq", 0, C, "xn", 0)
     dma("s", T.oc[:, :], T.xq[:, 0:C].bitcast(dt.uint8), [], [A("xq", 0, C)])

@@ -1,4 +1,5 @@
 import math
+from concourse.bass import DstId, RemoteDMATransfer
 from concourse.mybir import dt, AluOpType as Op, ActivationFunctionType as Fn
 
 C, H, ROUNDS = 320, 160, 3
@@ -6,12 +7,11 @@ MASK = [1, 2, 3]
 U8, F8, BF, F32, I32, U16 = "uint8", "float8_e4m3fn_x4", "bfloat16", "float32", "int32", "uint16"
 T_PRODUCTS = 4
 NV = 5
+WIDE = H
 TURN = 2048
 FAR = 2.0 ** 90
-A_EARLY = 12
-B_OUT = ["vavavava", "avvvvava", "avvvvava", "avvvvava"]
-FUSED = ["vavavava", "aaaaavvv", "aaaaaavv", "aaaaaavv"]
-B_GATHER, B_ADD = 1, 6
+A_OUT = "aavaavav" + "avavavav"
+B_PLAN = "vavavava" + "av0aaaava" + "av1aaaava" + "av2aaaava" + "3"
 
 PAIRS = [("a", b, 32 * b) for b in range(9, NV - 1, -1)] + [("v", k, 32 * NV) for k in range(NV - 1)]
 TILES = [PAIRS[k:k + 2] for k in range(0, len(PAIRS), 2)]
@@ -32,7 +32,7 @@ def _mx(name, cols):
 
 for _k in range(8):
     SCRATCH["ps%d" % _k] = ("psum", [128, 512], F32)
-for _n, _w in (("xin", 1280), ("xn", 1280), ("ut", 512), ("vt", 512), ("ones", 512), ("zt", 512), ("vb", 1280), ("zs", 1152), ("cd", 1280),
+for _n, _w in (("xin", 1280), ("xn", 1280), ("ut", 512), ("vt", 512), ("ones", 512), ("zt", 512), ("zs", 1152), ("cd", 1280),
                ("fs", 528), ("dat", 320), ("wn", 2560), ("wt", 7 * TURN + 1280), ("wv", 10240), ("gt", 640), ("ft", 640), ("at", 640),
                ("bt", 640), ("tri", 320), ("row", 320), ("est", 1936), ("cst", 4096), ("cc1", 1024), ("cci", 640), ("om", 512), ("oa", 512),
                ("j32", 320), ("jq", 320), ("j128", 128), ("jg", 64), ("jh", 16)):
@@ -50,11 +50,11 @@ for _n, _w in (("pi", 16), ("lui", 40), ("li", 400)):
 for _n, _w in (("lu", 16), ("lt", 20), ("pos", 32), ("off", 32), ("wl", 32)):
     _sb(_n, _w, U16)
 for _n, _w in (("xq", 320), ("uq", 128), ("us", 256), ("vq", 128), ("wq", 512), ("er", 960), ("kc", 1024), ("k1", 256),
-               ("ki", 160), ("fq", 132), ("nq", 640), ("gq", 160), ("fqq", 160), ("aq", 160), ("bq", 160)):
+               ("ki", 160), ("fq", 132), ("nq", 640), ("gq", WIDE), ("fqq", 160), ("aq", 160), ("bq", WIDE)):
     _mx(_n, _w)
 for _k in range(ROUNDS):
-    _mx("gl%d" % _k, 160)
-    _mx("bl%d" % _k, 160)
+    _mx("gl%d" % _k, WIDE)
+    _mx("bl%d" % _k, WIDE)
 
 SEMAPHORES = ["ev", "ea", "et", "ep"] + ["d%d" % _k for _k in range(100)]
 for _k in range(ROUNDS):
@@ -186,7 +186,7 @@ def rank_program(g, core, T, topo):
     def send(dst, src, land, sem, done):
         rid, pid, _ = topo.addr(dst)
         eng = topo.engines(core, dst)
-        ec, es = eng, eng
+        ec, es = eng[0::2], eng[1::2]
         total = len(ec) + len(es)
         need("p", [r[3] for nm in (src, src + "s") for r in log[nm] if r[1]])
         g.remote_dma(T[land][:, 0:H].bitcast(dt.uint8), T[src][:, 0:H].bitcast(dt.uint8), T.sem[sem], T.sem[done], pid, rid, sum(1 << e for e in ec))
@@ -195,9 +195,9 @@ def rank_program(g, core, T, topo):
         snaps[tok], snaps[arr] = dict(known["p"]), {}
         final[done], final[sem] = total, total
         for nm in (src, src + "s"):
-            note(A(nm, 0, H), False, "p", tok)
+            note(A(nm, 0, WIDE), False, "p", tok)
         for nm in (land, land + "s"):
-            log[nm] = [(A(nm, 0, H), True, "r", arr, False)]
+            log[nm] = [(A(nm, 0, WIDE), True, "r", arr, False)]
 
     def iota(o, pattern, base, cm):
         if o[0] in ("pi", "lui"):
@@ -361,16 +361,17 @@ def rank_program(g, core, T, topo):
         dma("s", T.wt[0:k, o[1]:o[2]], T.wt[16 * d:128, 0:1280], [o], [i], loose=True)
         dma("s", T.wt[k:128, o[1]:o[2]], T.wt[0:16 * d, 0:1280], [o], [i], loose=True)
 
-    def layer(pair, tile, out):
+    def layer(pair, tile, bank, first=None):
         for b in range(4):
-            mm(b, "wq", 128 * b, pair, 0, H)
+            mm(bank + b, "wq", 128 * b, pair, 0, H)
+        if first:
+            first()
         for b in range(4):
             o = A(tile, b, 4 * H, 4)
-            if b % 2 == 0:
-                ts(o, P(b, H), 0.0, 0.03125, Op.max, Op.mult)
+            if b % 2 == 1:
+                ts(o, P(bank + b, H), 0.0, 0.03125, Op.max, Op.mult)
             else:
-                act(o, P(b, H), Fn.Relu, scale=0.03125)
-        quant(out, 0, H, tile, 0)
+                act(o, P(bank + b, H), Fn.Relu, scale=0.03125)
 
     def L(k):
         return A("li", 20 * k, 20 * k + 20)
@@ -543,23 +544,6 @@ def rank_program(g, core, T, topo):
             quant("nq", a, n, "wn", 4 * a)
             for s in range(a // 128, (a + n) // 128):
                 mm(1, "nq", 128 * s, "ki", 20 - 2 * s, 128, s == 0, s == 4)
-        tt(L(7), P(1, 20), A("s2", 0, 20), Op.add)
-        ts(L(8), L(7), 3, 7 * TURN + 511, Op.arith_shift_right, Op.bitwise_and)
-        copy(A("off", 0, 20), L(8))
-        for b in range(4):
-            gather("va"[b % 2], A("gt", b, 640, 4), TW(b), A("off", 10, 20))
-        quant("gq", 0, H, "gt", 0)
-        send(dst, "gq", "gl%d" % rd, "ga%d" % rd, "gs%d" % rd)
-        for b in range(4):
-            gather("va"[b % 2], A("ft", b, 640, 4), TW(b), A("off", 0, 10))
-        quant("fqq", 0, H, "ft", 0)
-        layer("fqq", "at", "aq")
-        for k in range(A_EARLY):
-            unpack("aq", k // 8, k % 8, 4 + k % 4, "va"[k % 2], 0)
-        layer("gl%d" % rd, "bt", "bq")
-        send(dst, "bq", "bl%d" % rd, "ba%d" % rd, "bs%d" % rd)
-        if rd < ROUNDS - 1:
-            iota(A("wn", 0, 2560), [[0, 2560]], 0, 0)
         steps = [lambda: ts(L(13), n2, 4, None, Op.arith_shift_right),
                  lambda: ts(L(14), n2, 16, None, Op.bitwise_and),
                  lambda: ts(L(15), n2, 1, None, Op.bitwise_and),
@@ -574,53 +558,58 @@ def rank_program(g, core, T, topo):
                  lambda: tt(LF(6), LF(3), LF(4), Op.add),
                  lambda: tt(LF(7), LF(6), LF(5), Op.add),
                  lambda: copy(A("wl", 0, 20), LF(7))]
-        for k in range(A_EARLY, 32):
-            unpack("aq", k // 8, k % 8, k % 8, "aav"[k % 3], 0)
-            if steps:
-                steps.pop(0)()
-        for step in steps:
-            step()
         if rd == 0:
-            quant("vq", 0, 128, "vt", 0)
+            steps.append(lambda: quant("vq", 0, 128, "vt", 0))
         if rd == ROUNDS - 1:
-            ts(A("r0", 0, 20), A("sg", 3, 80, 4), -639.75, None, Op.mult)
-            ts(A("r1", 0, 20), A("n2f", 0, 20), 0.5, 639.75, Op.mult, Op.add)
-            ts(LF(8), A("pl", 0, 20), 0.5, None, Op.mult)
-            tt(A("dg", 0, 20), A("r0", 0, 20), A("r1", 0, 20), Op.add)
-            tt(A("vf", 0, 20), A("dg", 0, 20), LF(8), Op.add)
-            turn32(A("vtr", 0, 32), A("vf", 0, 32))
+            steps += [lambda: ts(L(18), n2, 1, None, Op.arith_shift_right),
+                      lambda: tt(A("vf", 0, 20), L(18), LF(2), Op.add),
+                      lambda: turn32(A("vtr", 0, 32), A("vf", 0, 32))]
+
+        def meanwhile(k):
+            for step in steps[:k]:
+                step()
+            del steps[:k]
+
+        meanwhile(4)
+        tt(L(7), P(1, 20), A("s2", 0, 20), Op.add)
+        meanwhile(1)
+        ts(L(8), L(7), 3, 7 * TURN + 511, Op.arith_shift_right, Op.bitwise_and)
+        meanwhile(1)
+        copy(A("off", 0, 20), L(8))
+        meanwhile(1)
+        for b in range(4):
+            gather("va"[b % 2], A("gt", b, 640, 4), TW(b), A("off", 10, 20))
+        meanwhile(1)
+        quant("gq", 0, H, "gt", 0)
+        send(dst, "gq", "gl%d" % rd, "ga%d" % rd, "gs%d" % rd)
+        for b in range(4):
+            gather("aava"[b], A("ft", b, 640, 4), TW(b), A("off", 0, 10))
+        meanwhile(3)
+        quant("fqq", 0, H, "ft", 0)
+        meanwhile(3)
+        layer("fqq", "at", 0)
+        layer("gl%d" % rd, "bt", 4, lambda: quant("aq", 0, H, "at", 0))
+        quant("bq", 0, H, "bt", 0)
+        send(dst, "bq", "bl%d" % rd, "ba%d" % rd, "bs%d" % rd)
+        if rd < ROUNDS - 1:
+            iota(A("wn", 0, 2560), [[0, 2560]], 0, 0)
+        meanwhile(len(steps))
+        for k, q in enumerate(A_OUT):
+            unpack("aq", k // 4, k % 4, k % 8, q, 0)
+            if k % 4 == 3:
+                halves("s", k // 4, 0)
+        if rd == ROUNDS - 1:
             for k in range(8):
                 a, o = k // 2, 16 * (k % 2)
                 dma("s", T.op[k:k + 1, :], T.vtr[32 * a:32 * a + 20, o:o + 16], [], [A("vtr", 0, 32)])
-
-        land = "bl%d" % rd
-        def spliced(q, b, a, n):
-            gather(q, A("vb", 320 * b + a, 320 * b + a + n), A("wv", 2560 * b, 2560 * b + 2560), A("wl", a // 16, (a + n) // 16))
-
-        def add(b, a, n):
-            tt(A("xn", 4 * a + b, 4 * (a + n), 4), A("vb", 320 * b + a, 320 * b + a + n), P(6 + b % 2, a + n, a), Op.add)
-
-        if FUSED:
-            for b in range(4):
-                for d, q in enumerate(FUSED[b]):
-                    unpack(land, b, d, d, q, 1)
-                gather_add(A("xn", b, 1280, 4), A("wv", 2560 * b, 2560 * b + 2560), A("wl", 0, 20), A("wt", 320 * b, 320 * b + 320))
-            continue
-        t_product(0, 0, 6)
-        t_product(1, 0, 7)
-        for b in range(4):
-            for d, q in enumerate(B_OUT[b]):
-                unpack(land, b, d, (8 * b + d) % 6, q, 1)
-                if b > 0 and d == B_GATHER:
-                    spliced("a", b - 1, 0, C)
-                if b > 0 and d == B_ADD:
-                    add(b - 1, 0, C)
-            if b > 1:
-                t_product(b, 0, 6 + b % 2)
-        spliced("v", 3, 0, H)
-        spliced("a", 3, H, H)
-        add(3, 0, H)
-        add(3, H, H)
+        k = 0
+        for q in B_PLAN:
+            if q in "va":
+                unpack("bl%d" % rd, k // 8, k % 8, k % 8, q, 1)
+                k += 1
+            else:
+                e = int(q)
+                gather_add(A("xn", e, 1280, 4), A("wv", 2560 * e, 2560 * e + 2560), A("wl", 0, 20), A("wt", 320 * e, 320 * e + 320))
 
     quant("xq", 0, C, "xn", 0)
     dma("s", T.oc[:, :], T.xq[:, 0:C].bitcast(dt.uint8), [], [A("xq", 0, C)])

@@ -11,7 +11,7 @@ WIDE = H
 TURN = 2048
 FAR = 2.0 ** 90
 A_OUT = "aavaavav" + "avavavav"
-B_PLAN = "vavavava" + "av0aaaava" + "av1aaaava" + "av2aaaava" + "3"
+B_PLAN = "vava>" + "vavavava" + "av1aaaava" + "av2aaaava" + "03"
 
 PAIRS = [("a", b, 32 * b) for b in range(9, NV - 1, -1)] + [("v", k, 32 * NV) for k in range(NV - 1)]
 TILES = [PAIRS[k:k + 2] for k in range(0, len(PAIRS), 2)]
@@ -34,8 +34,8 @@ for _k in range(8):
     SCRATCH["ps%d" % _k] = ("psum", [128, 512], F32)
 for _n, _w in (("xin", 1280), ("xn", 1280), ("ut", 512), ("vt", 512), ("ones", 512), ("zt", 512), ("zs", 1152), ("cd", 1280),
                ("fs", 528), ("dat", 320), ("wn", 2560), ("wt", 7 * TURN + 1280), ("wv", 10240), ("gt", 640), ("ft", 640), ("at", 640),
-               ("bt", 640), ("tri", 320), ("row", 320), ("est", 1936), ("cst", 4096), ("cc1", 1024), ("cci", 640), ("om", 512), ("oa", 512),
-               ("j32", 320), ("jq", 320), ("j128", 128), ("jg", 64), ("jh", 16)):
+               ("bt", 640), ("tri", 320), ("row", 320), ("est", 520), ("cst", 4096), ("cc1", 1024), ("cci", 640), ("om", 512), ("oa", 512),
+               ("j32", 320), ("jq", 320), ("sgn", 16), ("jg", 64)):
     _sb(_n, _w, BF)
 _mx("cdq", 320)
 for _k, _t in enumerate(TILES):
@@ -56,7 +56,7 @@ for _k in range(ROUNDS):
     _mx("gl%d" % _k, WIDE)
     _mx("bl%d" % _k, WIDE)
 
-SEMAPHORES = ["ev", "ea", "et", "ep"] + ["d%d" % _k for _k in range(100)]
+SEMAPHORES = ["ev", "ea", "et", "ep"] + ["d%d" % _k for _k in range(130)]
 for _k in range(ROUNDS):
     SEMAPHORES += ["ga%d" % _k, "ba%d" % _k, "gs%d" % _k, "bs%d" % _k]
 
@@ -123,10 +123,13 @@ def rank_program(g, core, T, topo):
         for s in outs:
             note(s, True, q, token, loose)
 
-    def dma(q, out_ap, in_ap, outs, ins, loose=False):
-        tok = ("d%d" % ndma[0], 16)
+    def dmas(q, sides, outs, ins):
+        tok = ("d%d" % ndma[0], 16 * len(sides))
         ndma[0] += 1
-        emit(q, lambda: queue[q].dma_start(out_ap, in_ap).then_inc(T.sem[tok[0]], 16), outs, ins, tok, loose=loose)
+        emit(q, lambda: [queue[q].dma_start(o, i).then_inc(T.sem[tok[0]], 16) for o, i in sides], outs, ins, tok)
+
+    def dma(q, out_ap, in_ap, outs, ins):
+        dmas(q, [(out_ap, in_ap)], outs, ins)
 
     def memset(s, c):
         emit("v", lambda: g.vector.memset(ap(s), c), [s], [])
@@ -186,7 +189,7 @@ def rank_program(g, core, T, topo):
     def send(dst, src, land, sem, done):
         rid, pid, _ = topo.addr(dst)
         eng = topo.engines(core, dst)
-        ec, es = eng[0::2], eng[1::2]
+        ec = es = eng
         total = len(ec) + len(es)
         need("p", [r[3] for nm in (src, src + "s") for r in log[nm] if r[1]])
         g.remote_dma(T[land][:, 0:H].bitcast(dt.uint8), T[src][:, 0:H].bitcast(dt.uint8), T.sem[sem], T.sem[done], pid, rid, sum(1 << e for e in ec))
@@ -205,6 +208,9 @@ def rank_program(g, core, T, topo):
         else:
             emit("p", lambda: g.iota(ap(o), pattern, base, cm, allow_small_or_imprecise_dtypes=True), [o], [])
 
+    def select(o, i, pattern, cmp, base, cm):
+        emit("p", lambda: g.affine_select(ap(o), ap(i), pattern, cmp, 0.0, base, cm), [o], [i])
+
     def pcol(k):
         return A("pi", k, k + 1)
 
@@ -218,55 +224,59 @@ def rank_program(g, core, T, topo):
     dma("s", T.xin[:, :], T.x[:, :], [A("xin", 0, 1280)], [])
 
     iota(A("pi", 0, 1), [[0, 1]], 0, 1)
-    iota(A("j128", 0, 128), [[1, 128]], 0, 0)
-    iota(A("lui", 0, 16), [[16, 2], [32, 4], [0, 2]], 0, 0)
-    iota(A("om", 0, 512), [[1, 8], [8, 16], [-8, 4]], 0, 0)
-    iota(A("j32", 0, 320), [[0, 10], [1, 32]], 0, 0)
+    memset(A("ones", 0, 512), 1.0)
     iota(A("jg", 0, 64), [[1, 8], [0, 8]], 0, 0)
+    iota(A("lui", 0, 16), [[16, 2], [32, 4], [0, 2]], 0, 0)
+    iota(A("j32", 0, 320), [[0, 10], [1, 32]], 0, 0)
+    iota(A("est", 0, 520), [[0, 520]], 0, 0)
+    select(A("est", 3, 515, 4), A("ones", 0, 128), [[-1, 128]], Op.is_equal, 0, 1)
     iota(A("jq", 0, 320), [[0, 40], [1, 4], [0, 2]], 0, 0)
     for a, b in ((0, NV), (NV, CUT), (CUT, 10)):
         iota(A("lui", 16 + 2 * a, 16 + 2 * b), [[2, 2 * (b - a)]], 4 * a % 8, 0)
-    iota(A("jh", 0, 16), [[1, 8], [0, 2]], 0, 0)
     blank = [A("fs", 0, 16), A("fs", 336, 528), A("z80", 0, 80), A("st", 0, 8), A("vf", 0, 32)]
     for k, t in enumerate(TILES):
         a = t[1][2] if len(t) > 1 else 0
         if a < t[0][2]:
             blank = [A("ct%d" % k, 4 * a + e, 4 * t[0][2], 4) for e in (2, 3)] + blank
-    for s in blank:
-        iota(s, [[0, len(range(s[1], s[2], s[3]))]], 0, 0)
+    for s in blank[:-5] + [None] + blank[-5:]:
+        if s is None:
+            iota(A("om", 0, 512), [[1, 8], [8, 16], [-8, 4]], 0, 0)
+        else:
+            iota(s, [[0, len(range(s[1], s[2], s[3]))]], 0, 0)
     iota(A("smk", 0, 80), [[0, 20], [1, 4]], 0, 0)
     iota(A("pl", 0, 20), [[128, 20]], 0, 8)
     iota(A("s2", 0, 20), [[0, 2], [512, 5], [16, 2]], 64 * 16384, 32)
-    iota(A("wn", 0, 2560), [[0, 2560]], 0, 0)
 
     def affine(o, i, scale, bias):
         act(o, i, Fn.Identity, bias=bias, scale=scale)
 
-    memset(A("ones", 0, 512), 1.0)
-    memset(A("zt", 0, 512), 0.0)
+    fill(A("zt", 0, 512), 0.0)
     for k, (shift, keep) in enumerate(((0, 15), (0, 31), (4, 7), (4, 6), (0, 1), (1, 3), (3, 1), (2, 3), (0, 7))):
         ts(pcol(k + 1), pcol(0), shift, keep, Op.arith_shift_right, Op.bitwise_and)
-    memset(A("est", 0, 968), 0.0)
     copy(A("sc", 0, 10), A("pi", 0, 10))
-    fill(A("est", 968, 1480), 0.0)
-    fill(A("est", 1480, 1936), 0.0)
     copy(A("lu", 0, 16), A("lui", 0, 16))
-    for k in range(2):
-        ts(A("est", 969 * k + 2, 969 * k + 514, 4), A("j128", 0, 128), col(0), None, Op.is_equal)
-        ts(A("est", 969 * k + 514, 969 * k + 962, 4), A("j128", 0, 112), col(0), None, Op.is_equal)
+    ts(col(10), col(4), 1.0, None, Op.add)
+    affine(col(21), col(2), FAR, 0.5 * FAR)
     affine(col(11), col(5), -2.0, 1.0)
     affine(col(12), col(7), -1.0, 1.0)
+    affine(A("tri", 0, 320), A("j32", 0, 320), -FAR, col(21))
     affine(col(13), col(6), 32.0, col(3))
-    affine(col(21), col(2), 1.0, 0.5)
     affine(col(17), col(11), col(12), 0.0)
     affine(col(18), col(13), -1.0, -0.5)
-    affine(col(10), col(4), 1.0, 1.0)
+    affine(col(15), col(2), 2.0, 257.0 - 32 * (10 - NV))
     affine(col(19), col(17), 0.5, 0.0)
     affine(col(20), col(17), -0.5, 0.0)
-    quant("er", 0, 240, "est", 2)
-    quant("er", 480, 240, "est", 0)
+    affine(col(14), col(2), 2.0, -31.0)
+    affine(col(24), col(2), -2.0, 31.0)
+    affine(A("aw", 0, 4 * NV, 2), A("ones", 0, 2 * NV), col(15), 0.0)
+    fill(A("sgn", 0, 16), col(17))
+    affine(A("aw", 1, 4 * NV, 2), A("aw", 0, 4 * NV, 2), -1.0, 0.0)
+    for e in (0, 2, 1, 3):
+        for s in range(2):
+            ts(A("cc1", 4 * s + e, 512, 8), A("jg", 0, 64), col((4, 10)[e % 2]), 1.0 - 2 * s, Op.is_equal, Op.mult)
 
-    for o, w, n in [("cst", w, 512) for w in range(2048, 4096, 512)] + [("cci", 0, 512), ("cci", 512, 128)]:
+    zeros = [("cst", w, 512) for w in range(2048, 4096, 512)] + [("cci", 0, 512), ("cci", 512, 128)] + [("wn", w, 512) for w in range(0, 2560, 512)]
+    for o, w, n in zeros:
         dma("s", T[o][:, w:w + n], T.zt[:, 0:n], [A(o, w, w + n)], [A("zt", 0, n)])
     dma("s", T.wq[:, :].bitcast(dt.uint8), T.wc[:, :], [A("wq", 0, 512)], [])
     dma("s", T.wqs[:, :], T.ws[:, :], [A("wqs", 0, 512)], [])
@@ -277,43 +287,27 @@ def rank_program(g, core, T, topo):
     emit("a", lambda: g.scalar.activation(T.uss[:, 0:256], T.uqs[:, 0:128].indirect(ap(lst)), Fn.Copy), [A("uss", 0, 256)], [A("uqs", 0, 128), lst])
     emit("v", lambda: g.vector.tensor_copy(T.us[:, 0:256].bitcast(dt.uint32), T.uq[:, 0:128].bitcast(dt.uint32).indirect(ap(lst))),
          [A("us", 0, 256)], [A("uq", 0, 128), lst])
-    quant("er", 240, 240, "est", 970)
-    quant("er", 720, 240, "est", 968)
-    ts(A("tri", 0, 320), A("j32", 0, 320), col(21), -FAR, Op.subtract, Op.mult)
-
-    act(A("oa", 0, 512), A("om", 0, 512), Fn.Sign, bias=col(18))
+    for e in range(4):
+        act(A("cc1", 512 + e, 1024, 4), A("cc1", e, 512, 4), Fn.Copy, scale=(2.0, 2.0, -2.0, -2.0)[e])
     fill(A("cst", 1536, 2048), col(17))
-    affine(A("cst", 0, 512), A("oa", 0, 512), col(19), col(19))
-    affine(A("cst", 512, 1024), A("oa", 0, 512), col(20), col(19))
+    for b in range(4):
+        for e in range(b + 1):
+            select(A("cst", 2048 + 512 * b + 4 * (3 + e // 2) + e, 2048 + 512 * b + 512, 32), A("sgn", 0, 16), [[16, 8], [0, 2]], Op.is_gt,
+                   0 if e == b else 128, -1)
 
-    def consts_rank():
-        for s in range(2):
-            for e in range(4):
-                ts(A("cc1", 4 * s + e, 512, 8), A("jg", 0, 64), col((4, 10)[e % 2]), 1.0 - 2 * s, Op.is_equal, Op.mult)
-        for e in range(4):
-            ts(A("cc1", 512 + e, 1024, 4), A("cc1", e, 512, 4), (2.0, 2.0, -2.0, -2.0)[e], None, Op.mult)
-        quant("k1", 0, 256, "cc1", 0)
+    def consts_order_a():
+        act(A("oa", 0, 512), A("om", 0, 512), Fn.Sign, bias=col(18))
+        affine(A("cst", 0, 512), A("oa", 0, 512), col(19), col(19))
+        affine(A("cst", 512, 1024), A("oa", 0, 512), col(20), col(19))
 
     def consts_flags():
-        ts(col(14), col(2), 2.0, -31.0, Op.mult, Op.add)
-        ts(col(15), col(2), 2.0, 257.0 - 32 * (10 - NV), Op.mult, Op.add)
-        ts(col(24), col(2), -2.0, 31.0, Op.mult, Op.add)
         ts(A("row", 0, 320), A("jq", 0, 320), col(8), -FAR, Op.not_equal, Op.mult)
-        ts(A("aw", 0, 4 * NV, 2), A("ones", 0, 2 * NV), col(15), None, Op.mult)
-        ts(A("aw", 1, 4 * NV, 2), A("ones", 0, 2 * NV), col(15), -1.0, Op.mult, Op.mult)
         ts(A("lt", 0, 20), A("lui", 16, 36), col(5), None, Op.add)
-
-    def within(b, e):
-        return A("cst", 2048 + 512 * b + 4 * (3 + e // 2) + e, 2048 + 512 * b + 512, 32)
 
     def consts_order_v():
         ts(A("cst", 1024, 1536), A("om", 0, 512), col(13), col(17), Op.is_equal, Op.mult)
-        for b in range(4):
-            ts(within(b, b), A("jh", 0, 16), col(3), col(17), Op.is_gt, Op.mult)
-            for e in range(b):
-                ts(within(b, e), A("ones", 0, 16), col(17), None, Op.mult)
-        quant("kc", 0, 512, "cst", 0)
         quant("kc", 512, 512, "cst", 2048)
+        quant("kc", 0, 512, "cst", 0)
 
     def consts_lists_a():
         act(A("smk", 0, 80), A("smk", 0, 80), Fn.Sign)
@@ -349,17 +343,11 @@ def rank_program(g, core, T, topo):
     def halves(q, b, i):
         k = 2560 * b + 1280 * i
         o, src = A("wv", k + 640, k + 1280), A("wv", k, k + 640)
-        for to, fr in ((0, 64), (64, 0)):
-            x, w = T.wv[to:to + 64, k + 640:k + 1280], T.wv[fr:fr + 64, k:k + 640]
-            if q == "s":
-                dma("s", x, w, [o], [src], loose=True)
-            else:
-                emit("v", lambda: g.vector.tensor_copy(x, w), [o], [src], loose=True)
+        dmas(q, [(T.wv[to:to + 64, k + 640:k + 1280], T.wv[fr:fr + 64, k:k + 640]) for to, fr in ((0, 64), (64, 0))], [o], [src])
 
-    def by_dma(d):
-        o, i, k = A("wt", TURN * d, TURN * d + 1280), A("wt", 0, 1280), 128 - 16 * d
-        dma("s", T.wt[0:k, o[1]:o[2]], T.wt[16 * d:128, 0:1280], [o], [i], loose=True)
-        dma("s", T.wt[k:128, o[1]:o[2]], T.wt[0:16 * d, 0:1280], [o], [i], loose=True)
+    def by_dma(to, fr, d, a):
+        o, i, k = A("wt", TURN * to + a, TURN * to + a + 640), A("wt", TURN * fr + a, TURN * fr + a + 640), 128 - 16 * d
+        dmas("s", [(T.wt[0:k, o[1]:o[2]], T.wt[16 * d:128, i[1]:i[2]]), (T.wt[k:128, o[1]:o[2]], T.wt[0:16 * d, i[1]:i[2]])], [o], [i])
 
     def layer(pair, tile, bank, first=None):
         for b in range(4):
@@ -441,20 +429,24 @@ def rank_program(g, core, T, topo):
     for rd in range(ROUNDS):
         dst = T.cores[rank ^ MASK[rd]]
         quant("xq", 0, C, "xin" if rd == 0 else "xn", 0)
+        def t_early():
+            for b in (0, 1):
+                t_out(b, 0, 6 + b)
+            for d in range(1, 8):
+                by_dma(d, 0, d, 0)
+
         mm(1, "us", 0, "xq", 0, C)
-        t_product(0, 0, 6)
+        if rd > 0:
+            t_product(0, 0, 6)
         mm(2, "us", 128, "xq", 0, C)
-        t_product(1, 0, 7)
-        t_product(2, 0, 0)
-        t_product(3, 0, 3)
+        if rd > 0:
+            t_product(1, 0, 7)
         mm(4, "us", 0, "xq", 0, C)
         mm(5, "us", 128, "xq", 0, C)
-        for b, bank in ((0, 6), (1, 7), (2, 0), (3, 3)):
-            t_out(b, 0, bank)
-        for d in range(T_PRODUCTS, 8):
-            by_dma(d)
-        if rd == 0:
-            consts_rank()
+        if rd > 0:
+            t_early()
+        else:
+            quant("k1", 0, 128, "cc1", 0)
         steps = (lambda gg: tt(A("pm", 320 * gg, 320 * gg + 320), P(1 + gg, C), A("tri", 0, 320), Op.min),
                  lambda gg: turn32(A("pt", 320 * gg, 320 * gg + 320), A("pm", 320 * gg, 320 * gg + 320)),
                  lambda gg: tt(A("cd", gg, 1280, 4), P(1 + gg, C), A("pt", 320 * gg, 320 * gg + 320), Op.is_le),
@@ -465,6 +457,15 @@ def rank_program(g, core, T, topo):
         steps[3](1)
         compare_v(1)
         quant("cdq", 0, C, "cd", 0)
+        if rd == 0:
+            quant("k1", 128, 128, "cc1", 512)
+            for b in range(4):
+                a = 240 * b
+                quant("er", a, 128, "est", 3 - b)
+                dma("s", T.er[:, a + 128:a + 240].bitcast(dt.uint8), T.er[:, a:a + 112].bitcast(dt.uint8), [A("er", a + 128, a + 240)], [A("er", a, a + 112)])
+                dma("s", T.ers[:, a + 128:a + 240], T.ers[:, a:a + 112], [A("ers", a + 128, a + 240)], [A("ers", a, a + 112)])
+            t_product(0, 0, 6)
+            t_product(1, 0, 7)
         mm(3, "k1", 128, "cdq", 0, C, start=True, stop=False)
         last, cut = LAST, CUT
         if rd == 0:
@@ -478,17 +479,25 @@ def rank_program(g, core, T, topo):
             compare_a(b)
             if b in (cut, NV):
                 signed(b, 10 if b == cut else cut)
+            if rd == 0 and b == 7:
+                t_early()
         if rd == 0:
+            consts_order_a()
             consts_lists_a()
         for b in range(2, NV):
             compare_v(b)
-        later = [(b, d) for d in range(1, T_PRODUCTS) for b in range(4)]
+        later = [(b, d) for d in range(4) for b in (2, 3)]
+
+        def t_late(k, bank):
+            t_out(*later[k], bank)
+            if k % 2:
+                by_dma(k // 2 + 4, k // 2, 4, 640)
+
         for k in [0] + list(range(last + 1, len(TILES))):
             add_ranks(k)
         t_product(*later[0], 6)
         t_product(*later[1], 7)
         if rd == 0:
-            consts_order_v()
             bounds(0, NV)
         for k in range(1, last):
             add_ranks(k)
@@ -497,11 +506,15 @@ def rank_program(g, core, T, topo):
         spread(NV, cut)
         mirror(NV, cut)
         tt(A("fs", 16, 336), P(3, C), A("thr", 0, 320), Op.is_lt)
-        t_out(*later[0], 6)
-        t_out(*later[1], 7)
+        if rd == 0:
+            consts_order_v()
+        t_late(0, 6)
+        t_late(1, 7)
         for k in (2, 3):
-            t_product(*later[k], 4 + k)
-            t_out(*later[k], 4 + k)
+            t_product(*later[k], 2 + k)
+            t_late(k, 2 + k)
+        t_product(*later[4], 6)
+        t_product(*later[5], 7)
         quant("fq", 0, 132, "fs", 0)
         mm(2, "kc", 384, "fq", 4, 128)
         mm(0, "kc", 0, "fq", 4, 128, True, False)
@@ -512,6 +525,7 @@ def rank_program(g, core, T, topo):
         mm(3, "kc", 768, "fq", 4, 128)
         if rd == 0:
             consts_digits()
+        t_late(4, 6)
         scan(A("st", 8, 88), P(2, 80), A("z80", 0, 80), 0.0, Op.add, Op.add)
         scan(A("su", 0, 80), P(0, 80), A("z80", 0, 80), -0.5, Op.add, Op.add)
         mm(0, "kc", 896, "fq", 4, 128)
@@ -520,9 +534,11 @@ def rank_program(g, core, T, topo):
             affine(A("r%d" % k, 80, 160), A("st", 7, 87), 1.0, col((38, 36)[k]))
         for k in (0, 1):
             affine(A("r%d" % k, 0, 80), A("r%d" % k, 80, 160), 1.0, col((39, 37)[k]))
-        for k in range(4, len(later)):
-            t_product(*later[k], 6 + k % 2)
-            t_out(*later[k], 6 + k % 2)
+        t_product(*later[6], 2)
+        t_late(5, 7)
+        t_product(*later[7], 6)
+        t_late(6, 2)
+        t_late(7, 6)
         n2, y, h2 = L(0), L(1), L(2)
         tt(A("n2f", 0, 20), A("su", 3, 80, 4), A("sg", 3, 80, 4), Op.mult)
         tt(n2, A("n2f", 0, 20), A("pl", 0, 20), Op.add)
@@ -595,28 +611,31 @@ def rank_program(g, core, T, topo):
             iota(A("wn", 0, 2560), [[0, 2560]], 0, 0)
         meanwhile(len(steps))
         for k, q in enumerate(A_OUT):
-            unpack("aq", k // 4, k % 4, k % 8, q, 0)
+            b = [int(e) for e in B_PLAN if e.isdigit()][k // 4]
+            unpack("aq", b, k % 4, k % 8, q, 0)
             if k % 4 == 3:
-                halves("s", k // 4, 0)
-        if rd == ROUNDS - 1:
-            for k in range(8):
-                a, o = k // 2, 16 * (k % 2)
-                dma("s", T.op[k:k + 1, :], T.vtr[32 * a:32 * a + 20, o:o + 16], [], [A("vtr", 0, 32)])
-        k = 0
+                halves("s", b, 0)
+        k = bank = 0
         for q in B_PLAN:
             if q in "va":
-                unpack("bl%d" % rd, k // 8, k % 8, k % 8, q, 1)
-                k += 1
+                unpack("bl%d" % rd, k // 8, k % 8, bank % 8, q, 1)
+                k, bank = k + 1, bank + 1
+            elif q == ">":
+                halves("s", k // 8, 1)
+                k += 4
             else:
                 e = int(q)
                 gather_add(A("xn", e, 1280, 4), A("wv", 2560 * e, 2560 * e + 2560), A("wl", 0, 20), A("wt", 320 * e, 320 * e + 320))
 
+    dmas("s", [(T.op[k:k + 1, :], T.vtr[32 * (k // 2):32 * (k // 2) + 20, 16 * (k % 2):16 * (k % 2) + 16]) for k in range(8)], [], [A("vtr", 0, 32)])
     quant("xq", 0, C, "xn", 0)
     dma("s", T.oc[:, :], T.xq[:, 0:C].bitcast(dt.uint8), [], [A("xq", 0, C)])
-    mm(0, "vq", 0, "xq", 0, C)
+    mm(0, "vq", 0, "xq", 0, H)
+    mm(1, "vq", 0, "xq", H, H)
     for k in range(4):
-        dma("a", T.osc[4 * k:4 * k + 4, :], T.xqs[32 * k:32 * k + 4, 0:C], [], [A("xqs", 0, C)])
-    copy(A("yo", 0, C), P(0, C))
+        dma("sa"[k % 2], T.osc[4 * k:4 * k + 4, :], T.xqs[32 * k:32 * k + 4, 0:C], [], [A("xqs", 0, C)])
+    copy(A("yo", 0, H), P(0, H))
+    act(A("yo", H, C), P(1, H), Fn.Copy)
     dma("s", T.y[:, :], T.yo[:, 0:C], [], [A("yo", 0, C)])
     for s in sorted(final):
         if known["p"].get(s, 0) < final[s]:

@@ -6,17 +6,15 @@ C, H, ROUNDS = 320, 160, 3
 MASK = [1, 2, 3]
 U8, F8, BF, F32, I32, U16 = "uint8", "float8_e4m3fn_x4", "bfloat16", "float32", "int32", "uint16"
 T_PRODUCTS = 4
-NV = 5
+NV = (6, 5)
 WIDE = H
 TURN = 2048
 FAR = 2.0 ** 90
 A_OUT = "aavaavav" + "avavavav"
-B_PLAN = "vava>" + "vavavava" + "av1aaaava" + "av2aaaava" + "03"
+B_PLAN = "vava>" + "vava>" + "vavavava" + "vav2aa0aaa" + "13"
 
-PAIRS = [("a", b, 32 * b) for b in range(9, NV - 1, -1)] + [("v", k, 32 * NV) for k in range(NV - 1)]
-TILES = [PAIRS[k:k + 2] for k in range(0, len(PAIRS), 2)]
-LAST = (9 - NV) // 2
-CUT = 10 - 2 * LAST
+SLOTS = [[("a", b, 32 * b) for b in range(9, nv - 1, -1)] + [("v", k, 32 * nv) for k in range(nv - 1)] for nv in NV]
+WIDTH = [max(s[k][2] for s in SLOTS) for k in range(0, 9, 2)]
 
 SCRATCH = {}
 
@@ -38,9 +36,9 @@ for _n, _w in (("xin", 1280), ("xn", 1280), ("ut", 512), ("vt", 512), ("ones", 5
                ("j32", 320), ("jq", 320), ("sgn", 16), ("jg", 64)):
     _sb(_n, _w, BF)
 _mx("cdq", 320)
-for _k, _t in enumerate(TILES):
-    _sb("ct%d" % _k, 4 * _t[0][2], BF)
-    _mx("cq%d" % _k, _t[0][2])
+for _k, _w in enumerate(WIDTH):
+    _sb("ct%d" % _k, 4 * _w, BF)
+    _mx("cq%d" % _k, _w)
 for _n, _w in (("pm", 640), ("pt", 640), ("acc", 24), ("aw", 48), ("sp", 320), ("thr", 320), ("su", 80), ("sg", 80), ("st", 96), ("r1", 160),
                ("r0", 160), ("dg", 80), ("n2f", 32), ("vf", 32), ("vtr", 32), ("sc", 40), ("pl", 20), ("s2", 20),
                ("smk", 80), ("z80", 80), ("yo", 320), ("lf", 200)):
@@ -183,17 +181,16 @@ def rank_program(g, core, T, topo):
         else:
             emit("a", lambda: g.scalar.activation(ap(o), ap(win).indirect(ap(lst)), Fn.Copy), [o], [win, lst])
 
-    def gather_add(o, win, lst, more):
-        emit("v", lambda: g.vector.tensor_tensor(ap(o), ap(win).indirect(ap(lst)), ap(more), Op.add), [o], [win, lst, more])
+    def gather_add(o, win, lst, more, op=Op.add):
+        emit("v", lambda: g.vector.tensor_tensor(ap(o), ap(win).indirect(ap(lst)), ap(more), op), [o], [win, lst, more])
 
     def send(dst, src, land, sem, done):
         rid, pid, _ = topo.addr(dst)
         eng = topo.engines(core, dst)
-        ec = es = eng
-        total = len(ec) + len(es)
+        total, mask = 2 * len(eng), topo.mask(core, dst)
         need("p", [r[3] for nm in (src, src + "s") for r in log[nm] if r[1]])
-        g.remote_dma(T[land][:, 0:H].bitcast(dt.uint8), T[src][:, 0:H].bitcast(dt.uint8), T.sem[sem], T.sem[done], pid, rid, sum(1 << e for e in ec))
-        g.remote_dma(T[land + "s"][:, 0:H], T[src + "s"][:, 0:H], T.sem[sem], T.sem[done], pid, rid, sum(1 << e for e in es))
+        g.remote_dma(T[land][:, 0:H].bitcast(dt.uint8), T[src][:, 0:H].bitcast(dt.uint8), T.sem[sem], T.sem[done], pid, rid, mask)
+        g.remote_dma(T[land + "s"][:, 0:H], T[src + "s"][:, 0:H], T.sem[sem], T.sem[done], pid, rid, mask)
         tok, arr = (done, total), (sem, total)
         snaps[tok], snaps[arr] = dict(known["p"]), {}
         final[done], final[sem] = total, total
@@ -228,29 +225,22 @@ def rank_program(g, core, T, topo):
     iota(A("jg", 0, 64), [[1, 8], [0, 8]], 0, 0)
     iota(A("lui", 0, 16), [[16, 2], [32, 4], [0, 2]], 0, 0)
     iota(A("j32", 0, 320), [[0, 10], [1, 32]], 0, 0)
+    iota(A("om", 0, 512), [[1, 8], [8, 16], [-8, 4]], 0, 0)
     iota(A("est", 0, 520), [[0, 520]], 0, 0)
     select(A("est", 3, 515, 4), A("ones", 0, 128), [[-1, 128]], Op.is_equal, 0, 1)
+    iota(A("zt", 0, 512), [[0, 512]], 0, 0)
     iota(A("jq", 0, 320), [[0, 40], [1, 4], [0, 2]], 0, 0)
-    for a, b in ((0, NV), (NV, CUT), (CUT, 10)):
-        iota(A("lui", 16 + 2 * a, 16 + 2 * b), [[2, 2 * (b - a)]], 4 * a % 8, 0)
-    blank = [A("fs", 0, 16), A("fs", 336, 528), A("z80", 0, 80), A("st", 0, 8), A("vf", 0, 32)]
-    for k, t in enumerate(TILES):
-        a = t[1][2] if len(t) > 1 else 0
-        if a < t[0][2]:
-            blank = [A("ct%d" % k, 4 * a + e, 4 * t[0][2], 4) for e in (2, 3)] + blank
-    for s in blank[:-5] + [None] + blank[-5:]:
-        if s is None:
-            iota(A("om", 0, 512), [[1, 8], [8, 16], [-8, 4]], 0, 0)
-        else:
-            iota(s, [[0, len(range(s[1], s[2], s[3]))]], 0, 0)
-    iota(A("smk", 0, 80), [[0, 20], [1, 4]], 0, 0)
-    iota(A("pl", 0, 20), [[128, 20]], 0, 8)
-    iota(A("s2", 0, 20), [[0, 2], [512, 5], [16, 2]], 64 * 16384, 32)
+    iota(A("lui", 16, 30), [[2, 14]], 0, 0)
+    iota(A("lui", 30, 36), [[2, 6]], 0, 0)
+    for k, n in enumerate(WIDTH[:4]):
+        for e in range(4):
+            a = SLOTS[e % 2][2 * k + e // 2][2]
+            if a < n:
+                iota(A("ct%d" % k, 4 * a + e, 4 * n, 4), [[0, n - a]], 0, 0)
 
     def affine(o, i, scale, bias):
         act(o, i, Fn.Identity, bias=bias, scale=scale)
 
-    fill(A("zt", 0, 512), 0.0)
     for k, (shift, keep) in enumerate(((0, 15), (0, 31), (4, 7), (4, 6), (0, 1), (1, 3), (3, 1), (2, 3), (0, 7))):
         ts(pcol(k + 1), pcol(0), shift, keep, Op.arith_shift_right, Op.bitwise_and)
     copy(A("sc", 0, 10), A("pi", 0, 10))
@@ -262,55 +252,61 @@ def rank_program(g, core, T, topo):
     affine(A("tri", 0, 320), A("j32", 0, 320), -FAR, col(21))
     affine(col(13), col(6), 32.0, col(3))
     affine(col(17), col(11), col(12), 0.0)
+    affine(col(14), col(2), 2.0, -31.0)
     affine(col(18), col(13), -1.0, -0.5)
-    affine(col(15), col(2), 2.0, 257.0 - 32 * (10 - NV))
     affine(col(19), col(17), 0.5, 0.0)
     affine(col(20), col(17), -0.5, 0.0)
-    affine(col(14), col(2), 2.0, -31.0)
-    affine(col(24), col(2), -2.0, 31.0)
-    affine(A("aw", 0, 4 * NV, 2), A("ones", 0, 2 * NV), col(15), 0.0)
     fill(A("sgn", 0, 16), col(17))
-    affine(A("aw", 1, 4 * NV, 2), A("aw", 0, 4 * NV, 2), -1.0, 0.0)
     for e in (0, 2, 1, 3):
         for s in range(2):
             ts(A("cc1", 4 * s + e, 512, 8), A("jg", 0, 64), col((4, 10)[e % 2]), 1.0 - 2 * s, Op.is_equal, Op.mult)
 
-    zeros = [("cst", w, 512) for w in range(2048, 4096, 512)] + [("cci", 0, 512), ("cci", 512, 128)] + [("wn", w, 512) for w in range(0, 2560, 512)]
-    for o, w, n in zeros:
-        dma("s", T[o][:, w:w + n], T.zt[:, 0:n], [A(o, w, w + n)], [A("zt", 0, n)])
     dma("s", T.wq[:, :].bitcast(dt.uint8), T.wc[:, :], [A("wq", 0, 512)], [])
     dma("s", T.wqs[:, :], T.ws[:, :], [A("wqs", 0, 512)], [])
     dma("s", T.vt[:, :], T.v[:, :], [A("vt", 0, 512)], [])
+    for o, a, b in (("ct4", 0, 4 * WIDTH[4]), ("cst", 2048, 4096), ("fs", 0, 528), ("cci", 0, 640)):
+        dmas("s", [(T[o][:, w:min(w + 512, b)], T.zt[:, 0:min(512, b - w)]) for w in range(a, b, 512)], [A(o, a, b)], [A("zt", 0, 512)])
 
     quant("uq", 0, 128, "ut", 0)
     lst = A("lu", 0, 16)
     emit("a", lambda: g.scalar.activation(T.uss[:, 0:256], T.uqs[:, 0:128].indirect(ap(lst)), Fn.Copy), [A("uss", 0, 256)], [A("uqs", 0, 128), lst])
     emit("v", lambda: g.vector.tensor_copy(T.us[:, 0:256].bitcast(dt.uint32), T.uq[:, 0:128].bitcast(dt.uint32).indirect(ap(lst))),
          [A("us", 0, 256)], [A("uq", 0, 128), lst])
+    act(A("oa", 0, 512), A("om", 0, 512), Fn.Sign, bias=col(18))
     for e in range(4):
         act(A("cc1", 512 + e, 1024, 4), A("cc1", e, 512, 4), Fn.Copy, scale=(2.0, 2.0, -2.0, -2.0)[e])
-    fill(A("cst", 1536, 2048), col(17))
+    affine(A("cst", 0, 512), A("oa", 0, 512), col(19), col(19))
     for b in range(4):
         for e in range(b + 1):
             select(A("cst", 2048 + 512 * b + 4 * (3 + e // 2) + e, 2048 + 512 * b + 512, 32), A("sgn", 0, 16), [[16, 8], [0, 2]], Op.is_gt,
                    0 if e == b else 128, -1)
+    iota(A("smk", 0, 80), [[0, 20], [1, 4]], 0, 0)
+    iota(A("pl", 0, 20), [[128, 20]], 0, 8)
+    iota(A("s2", 0, 20), [[0, 2], [512, 5], [16, 2]], 64 * 16384, 32)
+    for s in (A("z80", 0, 80), A("st", 0, 8), A("vf", 0, 32)):
+        iota(s, [[0, s[2]]], 0, 0)
 
     def consts_order_a():
-        act(A("oa", 0, 512), A("om", 0, 512), Fn.Sign, bias=col(18))
-        affine(A("cst", 0, 512), A("oa", 0, 512), col(19), col(19))
         affine(A("cst", 512, 1024), A("oa", 0, 512), col(20), col(19))
+        fill(A("cst", 1536, 2048), col(17))
 
     def consts_flags():
-        ts(A("row", 0, 320), A("jq", 0, 320), col(8), -FAR, Op.not_equal, Op.mult)
         ts(A("lt", 0, 20), A("lui", 16, 36), col(5), None, Op.add)
+        affine(col(26), col(8), -FAR, 0.0)
+        affine(col(24), col(2), -2.0, 31.0)
+        for gg in range(2):
+            affine(A("aw", 2 * gg, 24, 4), A("ones", 0, 6), col(14), 288.0 - 32 * (10 - NV[gg]))
+        act(A("row", 0, 320), A("jq", 0, 320), Fn.Abs, bias=col(26), scale=FAR)
+        affine(A("aw", 1, 24, 2), A("aw", 0, 24, 2), -1.0, 0.0)
 
     def consts_order_v():
-        ts(A("cst", 1024, 1536), A("om", 0, 512), col(13), col(17), Op.is_equal, Op.mult)
         quant("kc", 512, 512, "cst", 2048)
         quant("kc", 0, 512, "cst", 0)
 
     def consts_lists_a():
+        affine(col(32), col(29), 32.0, col(31))
         act(A("smk", 0, 80), A("smk", 0, 80), Fn.Sign)
+        affine(col(38), col(30), 16.0, col(32))
         affine(col(23), col(3), -127.0, 0.5)
         affine(col(22), col(7), 16383.0, 1.0)
         affine(col(34), col(7), -16383.0, -1.0)
@@ -325,12 +321,9 @@ def rank_program(g, core, T, topo):
         ts(col(29), col(1), 0.0, 1.5 * 2.0 ** 30, Op.is_equal, Op.mult)
         ts(col(30), col(1), 1.0, 1.5 * 2.0 ** 26, Op.is_equal, Op.mult)
         ts(col(31), col(9), 2.0, 1.5 * 2.0 ** 26, Op.is_equal, Op.mult)
-        quant("ki", 0, 160, "cci", 0)
+        quant("k1", 0, 128, "cc1", 0)
         tt(col(36), col(29), col(30), Op.add)
-        ts(col(32), col(29), 32.0, col(31), Op.mult, Op.add)
-        ts(col(38), col(30), 16.0, col(32), Op.mult, Op.add)
-        affine(col(37), col(36), -1.0, 0.0)
-        affine(col(39), col(38), -1.0, 0.0)
+
 
     def unpack(pair, b, d, bank, q, i):
         mm(bank, "er", 240 * b + 16 * d, pair, 0, H)
@@ -380,17 +373,18 @@ def rank_program(g, core, T, topo):
         act(A("wt", TURN * d + 320 * b, TURN * d + 320 * b + 320), P(bank, C), Fn.Copy)
 
     def where(kind, k, gg):
-        i = [p[:2] for p in PAIRS].index((kind, k))
+        i = [p[:2] for p in SLOTS[gg]].index((kind, k))
         return "ct%d" % (i // 2), 2 * (i % 2) + gg
 
     def compare_v(b):
         for gg in range(2):
-            if b > 0:
+            nv = NV[gg]
+            if 0 < b < nv:
                 t, e = where("v", b - 1, gg)
                 ts(A(t, e, 128 * b, 4), P(1 + gg, 32 * b), own(gg, b), 2.0, Op.is_lt, Op.mult)
-            if b < NV - 1:
+            if b < nv - 1:
                 t, e = where("v", b, gg)
-                ts(A(t, 128 * b + 128 + e, 128 * NV, 4), P(1 + gg, 32 * NV, 32 * b + 32), own(gg, b), 2.0, Op.is_le, Op.mult)
+                ts(A(t, 128 * b + 128 + e, 128 * nv, 4), P(1 + gg, 32 * nv, 32 * b + 32), own(gg, b), 2.0, Op.is_le, Op.mult)
 
     def zs(b, gg):
         return A("zs", 288 * (2 * (b % 2) + gg), 288 * (2 * (b % 2) + gg) + 32 * b)
@@ -405,26 +399,28 @@ def rank_program(g, core, T, topo):
     def compare_a(b):
         for step in (signs, sums):
             for gg in range(2):
-                step(b, gg)
+                if b >= NV[gg]:
+                    step(b, gg)
 
     def add_ranks(k, stop=False):
-        n = TILES[k][0][2]
+        n = WIDTH[k]
         quant("cq%d" % k, 0, n, "ct%d" % k, 0)
         mm(3, "k1", 0, "cq%d" % k, 0, n, start=False, stop=stop)
 
     def signed(a, b):
-        affine(A("aw", 4 * a, 4 * b, 2), A("acc", 2 * a, 2 * b), 1.0, col(14))
-        affine(A("aw", 4 * a + 1, 4 * b, 2), A("acc", 2 * a, 2 * b), -1.0, col(24))
+        affine(A("aw", 2 * a, 2 * b, 2), A("acc", a, b), 1.0, col(14))
+        affine(A("aw", 2 * a + 1, 2 * b, 2), A("acc", a, b), -1.0, col(24))
+
+    def signed_high():
+        ts(A("aw", 32, 44, 2), A("acc", 14, 20), col(14), None, Op.add)
+        ts(A("aw", 33, 44, 2), A("acc", 14, 20), col(14), -1.0, Op.add, Op.mult)
 
     def spread(a, b):
-        gather_add(A("sp", 32 * a, 32 * b), A("aw", 4 * a // 8 * 8, 4 * b), A("lt", 2 * a, 2 * b), A("row", 32 * a, 32 * b))
+        win = A("aw", 32, 44) if a == 7 else A("aw", 0, 28)
+        gather_add(A("sp", 32 * a, 32 * b), win, A("lt", 2 * a, 2 * b), A("row", 32 * a, 32 * b), Op.subtract)
 
     def mirror(a, b):
         turn32(A("thr", 32 * a, 32 * b), A("sp", 32 * a, 32 * b))
-
-    def bounds(a, b):
-        spread(a, b)
-        mirror(a, b)
 
     for rd in range(ROUNDS):
         dst = T.cores[rank ^ MASK[rd]]
@@ -446,7 +442,7 @@ def rank_program(g, core, T, topo):
         if rd > 0:
             t_early()
         else:
-            quant("k1", 0, 128, "cc1", 0)
+            consts_digits()
         steps = (lambda gg: tt(A("pm", 320 * gg, 320 * gg + 320), P(1 + gg, C), A("tri", 0, 320), Op.min),
                  lambda gg: turn32(A("pt", 320 * gg, 320 * gg + 320), A("pm", 320 * gg, 320 * gg + 320)),
                  lambda gg: tt(A("cd", gg, 1280, 4), P(1 + gg, C), A("pt", 320 * gg, 320 * gg + 320), Op.is_le),
@@ -464,27 +460,28 @@ def rank_program(g, core, T, topo):
                 quant("er", a, 128, "est", 3 - b)
                 dma("s", T.er[:, a + 128:a + 240].bitcast(dt.uint8), T.er[:, a:a + 112].bitcast(dt.uint8), [A("er", a + 128, a + 240)], [A("er", a, a + 112)])
                 dma("s", T.ers[:, a + 128:a + 240], T.ers[:, a:a + 112], [A("ers", a + 128, a + 240)], [A("ers", a, a + 112)])
+            dmas("s", [(T.wn[:, w:w + 512], T.zt[:, 0:512]) for w in range(0, 2560, 512)], [A("wn", 0, 2560)], [A("zt", 0, 512)])
             t_product(0, 0, 6)
             t_product(1, 0, 7)
         mm(3, "k1", 128, "cdq", 0, C, start=True, stop=False)
-        last, cut = LAST, CUT
-        if rd == 0:
-            consts_flags()
         for gg in range(2):
             for b in (9, 8):
                 signs(b, gg)
             for b in (9, 8):
                 sums(b, gg)
-        for b in range(7, NV - 1, -1):
-            compare_a(b)
-            if b in (cut, NV):
-                signed(b, 10 if b == cut else cut)
-            if rd == 0 and b == 7:
-                t_early()
+        if rd == 0:
+            consts_flags()
+        compare_a(7)
+        for step in (signs, sums):
+            for b, gg in ((6, 0), (6, 1), (5, 0), (5, 1)):
+                if b >= NV[gg]:
+                    step(b, gg)
+        signed(sum(NV), 14)
         if rd == 0:
             consts_order_a()
+            t_early()
             consts_lists_a()
-        for b in range(2, NV):
+        for b in range(2, max(NV)):
             compare_v(b)
         later = [(b, d) for d in range(4) for b in (2, 3)]
 
@@ -493,28 +490,38 @@ def rank_program(g, core, T, topo):
             if k % 2:
                 by_dma(k // 2 + 4, k // 2, 4, 640)
 
-        for k in [0] + list(range(last + 1, len(TILES))):
-            add_ranks(k)
-        t_product(*later[0], 6)
-        t_product(*later[1], 7)
+        add_ranks(0)
+        if rd > 0:
+            t_product(*later[0], 6)
+            t_product(*later[1], 7)
+        add_ranks(3)
+        signed_high()
+        add_ranks(4)
         if rd == 0:
-            bounds(0, NV)
-        for k in range(1, last):
-            add_ranks(k)
-        bounds(cut, 10)
-        add_ranks(last, True)
-        spread(NV, cut)
-        mirror(NV, cut)
+            ts(A("cst", 1024, 1536), A("om", 0, 512), col(13), col(17), Op.is_equal, Op.mult)
+        spread(7, 10)
+        add_ranks(1)
+        if rd == 0:
+            spread(0, 7)
+            add_ranks(2, True)
+            mirror(0, 10)
+        else:
+            add_ranks(2, True)
+            spread(min(NV), 7)
+            mirror(min(NV), 10)
         tt(A("fs", 16, 336), P(3, C), A("thr", 0, 320), Op.is_lt)
         if rd == 0:
             consts_order_v()
+            t_product(*later[0], 6)
+            t_product(*later[1], 7)
         t_late(0, 6)
-        t_late(1, 7)
-        for k in (2, 3):
-            t_product(*later[k], 2 + k)
-            t_late(k, 2 + k)
-        t_product(*later[4], 6)
-        t_product(*later[5], 7)
+        if rd > 0:
+            t_late(1, 7)
+            for k in (2, 3):
+                t_product(*later[k], 2 + k)
+                t_late(k, 2 + k)
+            t_product(*later[4], 6)
+            t_product(*later[5], 7)
         quant("fq", 0, 132, "fs", 0)
         mm(2, "kc", 384, "fq", 4, 128)
         mm(0, "kc", 0, "fq", 4, 128, True, False)
@@ -523,24 +530,20 @@ def rank_program(g, core, T, topo):
         mm(4, "kc", 512, "fq", 4, 128)
         mm(5, "kc", 640, "fq", 4, 128)
         mm(3, "kc", 768, "fq", 4, 128)
-        if rd == 0:
-            consts_digits()
-        t_late(4, 6)
+        if rd > 0:
+            t_late(4, 6)
         scan(A("st", 8, 88), P(2, 80), A("z80", 0, 80), 0.0, Op.add, Op.add)
         scan(A("su", 0, 80), P(0, 80), A("z80", 0, 80), -0.5, Op.add, Op.add)
         mm(0, "kc", 896, "fq", 4, 128)
         scan(A("sg", 0, 80), A("smk", 0, 80), P(1, 80), 0.0, Op.mult, Op.add)
-        for k in (0, 1):
-            affine(A("r%d" % k, 80, 160), A("st", 7, 87), 1.0, col((38, 36)[k]))
-        for k in (0, 1):
-            affine(A("r%d" % k, 0, 80), A("r%d" % k, 80, 160), 1.0, col((39, 37)[k]))
-        t_product(*later[6], 2)
-        t_late(5, 7)
-        t_product(*later[7], 6)
-        t_late(6, 2)
-        t_late(7, 6)
+        ts(A("r0", 0, 80), A("st", 7, 87), col(38), col(38), Op.add, Op.subtract)
+        t_late(*((5, 7) if rd > 0 else (1, 7)))
+        for k in range(6 if rd > 0 else 2, 8):
+            t_product(*later[k], (2, 6, 7)[k % 3])
+            t_late(k, (2, 6, 7)[k % 3])
         n2, y, h2 = L(0), L(1), L(2)
         tt(A("n2f", 0, 20), A("su", 3, 80, 4), A("sg", 3, 80, 4), Op.mult)
+        ts(A("r1", 0, 80), A("st", 7, 87), col(36), col(36), Op.add, Op.subtract)
         tt(n2, A("n2f", 0, 20), A("pl", 0, 20), Op.add)
         tt(A("dg", 0, 80), A("r1", 0, 80), A("r0", 0, 80), Op.subtract)
         ts(y, n2, 4, 31, Op.arith_shift_right, Op.bitwise_and)
@@ -556,6 +559,8 @@ def rank_program(g, core, T, topo):
         copy(A("pos", 0, 20), L(6))
         slots, lst = A("wn", 0, 2560), A("pos", 0, 20)
         emit("v", lambda: g.vector.tensor_copy(ap(slots).indirect(ap(lst)), T.dat[:, 0:320]), [slots], [lst, A("dat", 0, 320)])
+        if rd == 0:
+            quant("ki", 0, 160, "cci", 0)
         for a, n in ((0, 256), (256, 256), (512, 128)):
             quant("nq", a, n, "wn", 4 * a)
             for s in range(a // 128, (a + n) // 128):
@@ -633,10 +638,11 @@ def rank_program(g, core, T, topo):
     mm(0, "vq", 0, "xq", 0, H)
     mm(1, "vq", 0, "xq", H, H)
     for k in range(4):
-        dma("sa"[k % 2], T.osc[4 * k:4 * k + 4, :], T.xqs[32 * k:32 * k + 4, 0:C], [], [A("xqs", 0, C)])
-    copy(A("yo", 0, H), P(0, H))
-    act(A("yo", H, C), P(1, H), Fn.Copy)
-    dma("s", T.y[:, :], T.yo[:, 0:C], [], [A("yo", 0, C)])
+        dma("s", T.osc[4 * k:4 * k + 4, :], T.xqs[32 * k:32 * k + 4, 0:C], [], [A("xqs", 0, C)])
+    act(A("yo", 0, H), P(0, H), Fn.Copy)
+    copy(A("yo", H, C), P(1, H))
+    dma("a", T.y[:, 0:H], T.yo[:, 0:H], [], [A("yo", 0, H)])
+    dma("s", T.y[:, H:C], T.yo[:, H:C], [], [A("yo", H, C)])
     for s in sorted(final):
         if known["p"].get(s, 0) < final[s]:
             g.wait_ge(T.sem[s], final[s])

@@ -30,10 +30,10 @@ def _mx(name, cols):
 
 for _k in range(8):
     SCRATCH["ps%d" % _k] = ("psum", [128, 512], F32)
-for _n, _w in (("xin", 1280), ("xn", 1280), ("ut", 512), ("vt", 512), ("ones", 512), ("zt", 512), ("zs", 1152), ("cd", 1280),
-               ("fs", 528), ("dat", 320), ("wn", 2560), ("wt", 7 * TURN + 1280), ("wv", 10240), ("gt", 640), ("ft", 640), ("at", 640),
+for _n, _w in (("xin", 1280), ("xn", 1280), ("ut", 512), ("vt", 512), ("ones", 128), ("zt", 512), ("zs", 1152), ("cd", 1280),
+               ("fs", 528), ("dat", 320), ("wn", 3072), ("wt", 7 * TURN + 1280), ("wv", 10240), ("gt", 640), ("ft", 640), ("at", 640),
                ("bt", 640), ("tri", 320), ("row", 320), ("est", 520), ("cst", 4096), ("cc1", 1024), ("cci", 640), ("om", 512), ("oa", 512),
-               ("j32", 320), ("jq", 320), ("sgn", 16), ("jg", 64)):
+               ("j32", 320), ("jq", 320), ("smk", 80), ("sgn", 64), ("jg", 64)):
     _sb(_n, _w, BF)
 _mx("cdq", 320)
 for _k, _w in enumerate(WIDTH):
@@ -41,14 +41,14 @@ for _k, _w in enumerate(WIDTH):
     _mx("cq%d" % _k, _w)
 for _n, _w in (("pm", 640), ("pt", 640), ("acc", 24), ("aw", 48), ("sp", 320), ("thr", 320), ("su", 80), ("sg", 80), ("st", 96), ("r1", 160),
                ("r0", 160), ("dg", 80), ("n2f", 32), ("vf", 32), ("vtr", 32), ("sc", 40), ("pl", 20), ("s2", 20),
-               ("smk", 80), ("z80", 80), ("yo", 320), ("lf", 200)):
+               ("z80", 80), ("yo", 320), ("lf", 200)):
     _sb(_n, _w, F32)
 for _n, _w in (("pi", 16), ("lui", 40), ("li", 400)):
     _sb(_n, _w, I32)
 for _n, _w in (("lu", 16), ("lt", 20), ("pos", 32), ("off", 32), ("wl", 32)):
     _sb(_n, _w, U16)
 for _n, _w in (("xq", 320), ("uq", 128), ("us", 256), ("vq", 128), ("wq", 512), ("er", 960), ("kc", 1024), ("k1", 256),
-               ("ki", 160), ("fq", 132), ("nq", 640), ("gq", WIDE), ("fqq", 160), ("aq", 160), ("bq", WIDE)):
+               ("ki", 160), ("fq", 132), ("nq", 768), ("gq", WIDE), ("fqq", 160), ("aq", 160), ("bq", WIDE)):
     _mx(_n, _w)
 for _k in range(ROUNDS):
     _mx("gl%d" % _k, WIDE)
@@ -220,16 +220,19 @@ def rank_program(g, core, T, topo):
     dma("a", T.ut[:, :], T.u[:, :], [A("ut", 0, 512)], [])
     dma("s", T.xin[:, :], T.x[:, :], [A("xin", 0, 1280)], [])
 
+    memset(A("zt", 0, 512), 0.0)
     iota(A("pi", 0, 1), [[0, 1]], 0, 1)
-    memset(A("ones", 0, 512), 1.0)
+    for k, (shift, keep) in enumerate(((0, 15), (0, 31), (4, 7), (4, 6), (0, 1), (1, 3), (3, 1), (2, 3), (0, 7))):
+        ts(pcol(k + 1), pcol(0), shift, keep, Op.arith_shift_right, Op.bitwise_and)
+    memset(A("ones", 0, 128), 1.0)
+    copy(A("sc", 0, 10), A("pi", 0, 10))
     iota(A("jg", 0, 64), [[1, 8], [0, 8]], 0, 0)
     iota(A("lui", 0, 16), [[16, 2], [32, 4], [0, 2]], 0, 0)
     iota(A("j32", 0, 320), [[0, 10], [1, 32]], 0, 0)
+    dmas("s", [(T.est[:, 0:512], T.zt[:, 0:512]), (T.est[:, 512:520], T.zt[:, 0:8])], [A("est", 0, 520)], [A("zt", 0, 512)])
     iota(A("om", 0, 512), [[1, 8], [8, 16], [-8, 4]], 0, 0)
-    iota(A("est", 0, 520), [[0, 520]], 0, 0)
-    select(A("est", 3, 515, 4), A("ones", 0, 128), [[-1, 128]], Op.is_equal, 0, 1)
-    iota(A("zt", 0, 512), [[0, 512]], 0, 0)
     iota(A("jq", 0, 320), [[0, 40], [1, 4], [0, 2]], 0, 0)
+    select(A("est", 3, 515, 4), A("ones", 0, 128), [[-1, 128]], Op.is_equal, 0, 1)
     iota(A("lui", 16, 30), [[2, 14]], 0, 0)
     iota(A("lui", 30, 36), [[2, 6]], 0, 0)
     for k, n in enumerate(WIDTH[:4]):
@@ -241,9 +244,6 @@ def rank_program(g, core, T, topo):
     def affine(o, i, scale, bias):
         act(o, i, Fn.Identity, bias=bias, scale=scale)
 
-    for k, (shift, keep) in enumerate(((0, 15), (0, 31), (4, 7), (4, 6), (0, 1), (1, 3), (3, 1), (2, 3), (0, 7))):
-        ts(pcol(k + 1), pcol(0), shift, keep, Op.arith_shift_right, Op.bitwise_and)
-    copy(A("sc", 0, 10), A("pi", 0, 10))
     copy(A("lu", 0, 16), A("lui", 0, 16))
     ts(col(10), col(4), 1.0, None, Op.add)
     affine(col(21), col(2), FAR, 0.5 * FAR)
@@ -253,76 +253,77 @@ def rank_program(g, core, T, topo):
     affine(col(13), col(6), 32.0, col(3))
     affine(col(17), col(11), col(12), 0.0)
     affine(col(14), col(2), 2.0, -31.0)
+    affine(col(24), col(2), -2.0, 31.0)
     affine(col(18), col(13), -1.0, -0.5)
-    affine(col(19), col(17), 0.5, 0.0)
-    affine(col(20), col(17), -0.5, 0.0)
-    fill(A("sgn", 0, 16), col(17))
+    affine(col(19), col(17), 16.0, 0.0)
+    affine(col(20), col(17), -16.0, 0.0)
+    fill(A("sgn", 0, 32), col(17))
     for e in (0, 2, 1, 3):
         for s in range(2):
             ts(A("cc1", 4 * s + e, 512, 8), A("jg", 0, 64), col((4, 10)[e % 2]), 1.0 - 2 * s, Op.is_equal, Op.mult)
+    ts(col(23), col(3), 32.0 - 4096, None, Op.mult)
+    ts(col(27), col(3), -64.0, 512.0, Op.mult, Op.add)
 
+    for o, a, b in (("ct4", 0, 4 * WIDTH[4]), ("cst", 1024, 1536), ("cst", 2048, 4096), ("fs", 0, 528), ("cci", 0, 640), ("wn", 0, 3072)):
+        dmas("s", [(T[o][:, w:min(w + 512, b)], T.zt[:, 0:min(512, b - w)]) for w in range(a, b, 512)], [A(o, a, b)], [A("zt", 0, 512)])
     dma("s", T.wq[:, :].bitcast(dt.uint8), T.wc[:, :], [A("wq", 0, 512)], [])
     dma("s", T.wqs[:, :], T.ws[:, :], [A("wqs", 0, 512)], [])
     dma("s", T.vt[:, :], T.v[:, :], [A("vt", 0, 512)], [])
-    for o, a, b in (("ct4", 0, 4 * WIDTH[4]), ("cst", 2048, 4096), ("fs", 0, 528), ("cci", 0, 640)):
-        dmas("s", [(T[o][:, w:min(w + 512, b)], T.zt[:, 0:min(512, b - w)]) for w in range(a, b, 512)], [A(o, a, b)], [A("zt", 0, 512)])
+
+    def unpacker(b):
+        a = 240 * b
+        quant("er", a, 128, "est", 3 - b)
+        dma("s", T.er[:, a + 128:a + 240].bitcast(dt.uint8), T.er[:, a:a + 112].bitcast(dt.uint8), [A("er", a + 128, a + 240)], [A("er", a, a + 112)])
+        dma("s", T.ers[:, a + 128:a + 240], T.ers[:, a:a + 112], [A("ers", a + 128, a + 240)], [A("ers", a, a + 112)])
 
     quant("uq", 0, 128, "ut", 0)
     lst = A("lu", 0, 16)
     emit("a", lambda: g.scalar.activation(T.uss[:, 0:256], T.uqs[:, 0:128].indirect(ap(lst)), Fn.Copy), [A("uss", 0, 256)], [A("uqs", 0, 128), lst])
     emit("v", lambda: g.vector.tensor_copy(T.us[:, 0:256].bitcast(dt.uint32), T.uq[:, 0:128].bitcast(dt.uint32).indirect(ap(lst))),
          [A("us", 0, 256)], [A("uq", 0, 128), lst])
-    act(A("oa", 0, 512), A("om", 0, 512), Fn.Sign, bias=col(18))
     for e in range(4):
         act(A("cc1", 512 + e, 1024, 4), A("cc1", e, 512, 4), Fn.Copy, scale=(2.0, 2.0, -2.0, -2.0)[e])
+    act(A("oa", 0, 512), A("om", 0, 512), Fn.Sign, bias=col(18))
     affine(A("cst", 0, 512), A("oa", 0, 512), col(19), col(19))
+    select(A("smk", 0, 80), A("ones", 0, 80), [[0, 20], [1, 4]], Op.is_gt, 0, 0)
+    iota(A("pl", 0, 20), [[4096, 20]], 64 * 768, 256)
+    iota(A("s2", 0, 10), [[256, 10]], 64 * 16384, 16)
+    for s in (A("z80", 0, 80), A("st", 0, 8), A("vf", 0, 32)):
+        iota(s, [[0, s[2]]], 0, 0)
+    select(A("sgn", 32, 64), A("sgn", 0, 32), [[16, 8], [2, 4]], Op.is_ge, 1, -1)
+    for e in range(4):
+        select(A("cst", 1024 + 5 * e, 1536, 16), A("sgn", 32, 64), [[-16, 8], [-2, 4]], Op.is_ge, 0, 1)
     for b in range(4):
         for e in range(b + 1):
             select(A("cst", 2048 + 512 * b + 4 * (3 + e // 2) + e, 2048 + 512 * b + 512, 32), A("sgn", 0, 16), [[16, 8], [0, 2]], Op.is_gt,
                    0 if e == b else 128, -1)
-    iota(A("smk", 0, 80), [[0, 20], [1, 4]], 0, 0)
-    iota(A("pl", 0, 20), [[128, 20]], 0, 8)
-    iota(A("s2", 0, 20), [[0, 2], [512, 5], [16, 2]], 64 * 16384, 32)
-    for s in (A("z80", 0, 80), A("st", 0, 8), A("vf", 0, 32)):
-        iota(s, [[0, s[2]]], 0, 0)
 
     def consts_order_a():
         affine(A("cst", 512, 1024), A("oa", 0, 512), col(20), col(19))
-        fill(A("cst", 1536, 2048), col(17))
+        affine(A("cst", 1536, 2048), A("oa", 0, 512), 0.0, col(17))
 
     def consts_flags():
         ts(A("lt", 0, 20), A("lui", 16, 36), col(5), None, Op.add)
-        affine(col(26), col(8), -FAR, 0.0)
-        affine(col(24), col(2), -2.0, 31.0)
+        ts(col(38), col(29), 32.0, col(33), Op.mult, Op.add)
         for gg in range(2):
-            affine(A("aw", 2 * gg, 24, 4), A("ones", 0, 6), col(14), 288.0 - 32 * (10 - NV[gg]))
-        act(A("row", 0, 320), A("jq", 0, 320), Fn.Abs, bias=col(26), scale=FAR)
-        affine(A("aw", 1, 24, 2), A("aw", 0, 24, 2), -1.0, 0.0)
+            ts(A("aw", 2 * gg, 24, 4), A("ones", 0, 6), col(14), 288.0 - 32 * (10 - NV[gg]), Op.mult, Op.add)
+        ts(A("row", 0, 320), A("jq", 0, 320), col(8), FAR, Op.not_equal, Op.mult)
+        ts(A("aw", 1, 24, 2), A("aw", 0, 24, 2), -1.0, None, Op.mult)
 
-    def consts_order_v():
-        quant("kc", 512, 512, "cst", 2048)
-        quant("kc", 0, 512, "cst", 0)
-
-    def consts_lists_a():
-        affine(col(32), col(29), 32.0, col(31))
-        act(A("smk", 0, 80), A("smk", 0, 80), Fn.Sign)
-        affine(col(38), col(30), 16.0, col(32))
-        affine(col(23), col(3), -127.0, 0.5)
+    def consts_places_a():
         affine(col(22), col(7), 16383.0, 1.0)
         affine(col(34), col(7), -16383.0, -1.0)
-        affine(col(25), col(3), 16386.0 - 512, 0.0)
-        affine(A("pl", 0, 20), A("pl", 0, 20), 1.0, col(23))
-        for e, c in ((80, 34), (86, 34), (121, 22), (127, 22)):
-            fill(A("cci", e, e + 1), col(c))
-        affine(A("s2", 0, 20), A("s2", 0, 20), 1.0, col(25))
-        affine(col(27), col(3), -2.0, 16.0)
+        affine(col(25), col(3), 16386.0 - 256, 0.0)
+        fill(A("cci", 48, 64, 5), col(22))
+        fill(A("cci", 128, 144, 5), col(34))
+        affine(A("s2", 0, 10), A("s2", 0, 10), 1.0, col(25))
 
     def consts_digits():
         ts(col(29), col(1), 0.0, 1.5 * 2.0 ** 30, Op.is_equal, Op.mult)
         ts(col(30), col(1), 1.0, 1.5 * 2.0 ** 26, Op.is_equal, Op.mult)
         ts(col(31), col(9), 2.0, 1.5 * 2.0 ** 26, Op.is_equal, Op.mult)
-        quant("k1", 0, 128, "cc1", 0)
         tt(col(36), col(29), col(30), Op.add)
+        ts(col(33), col(30), 16.0, col(31), Op.mult, Op.add)
 
 
     def unpack(pair, b, d, bank, q, i):
@@ -424,30 +425,38 @@ def rank_program(g, core, T, topo):
 
     for rd in range(ROUNDS):
         dst = T.cores[rank ^ MASK[rd]]
-        quant("xq", 0, C, "xin" if rd == 0 else "xn", 0)
+
         def t_early():
             for b in (0, 1):
                 t_out(b, 0, 6 + b)
             for d in range(1, 8):
                 by_dma(d, 0, d, 0)
 
-        mm(1, "us", 0, "xq", 0, C)
+        for a in (H, 0):
+            quant("xq", a, H, "xin" if rd == 0 else "xn", 4 * a)
+            mm(3 * a // H, "us", 0, "xq", a, H)
         if rd > 0:
             t_product(0, 0, 6)
         mm(2, "us", 128, "xq", 0, C)
         if rd > 0:
             t_product(1, 0, 7)
         mm(4, "us", 0, "xq", 0, C)
+        mm(1, "us", 0, "xq", 0, C)
         mm(5, "us", 128, "xq", 0, C)
         if rd > 0:
             t_early()
         else:
             consts_digits()
+            quant("k1", 0, 128, "cc1", 0)
         steps = (lambda gg: tt(A("pm", 320 * gg, 320 * gg + 320), P(1 + gg, C), A("tri", 0, 320), Op.min),
                  lambda gg: turn32(A("pt", 320 * gg, 320 * gg + 320), A("pm", 320 * gg, 320 * gg + 320)),
                  lambda gg: tt(A("cd", gg, 1280, 4), P(1 + gg, C), A("pt", 320 * gg, 320 * gg + 320), Op.is_le),
                  lambda gg: turn32(A("cd", 2 + gg, 1280, 4), A("cd", gg, 1280, 4)))
-        for k, gg in ((0, 0), (1, 0), (0, 1), (2, 0), (1, 1), (3, 0), (2, 1)):
+        for a in (H, 0):
+            tt(A("pm", a, a + H), P(3 * a // H, H), A("tri", 0, H), Op.min)
+        for a in (H, 0):
+            turn32(A("pt", a, a + H), A("pm", a, a + H))
+        for k, gg in ((0, 1), (2, 0), (1, 1), (3, 0), (2, 1)):
             steps[k](gg)
         compare_v(0)
         steps[3](1)
@@ -456,11 +465,7 @@ def rank_program(g, core, T, topo):
         if rd == 0:
             quant("k1", 128, 128, "cc1", 512)
             for b in range(4):
-                a = 240 * b
-                quant("er", a, 128, "est", 3 - b)
-                dma("s", T.er[:, a + 128:a + 240].bitcast(dt.uint8), T.er[:, a:a + 112].bitcast(dt.uint8), [A("er", a + 128, a + 240)], [A("er", a, a + 112)])
-                dma("s", T.ers[:, a + 128:a + 240], T.ers[:, a:a + 112], [A("ers", a + 128, a + 240)], [A("ers", a, a + 112)])
-            dmas("s", [(T.wn[:, w:w + 512], T.zt[:, 0:512]) for w in range(0, 2560, 512)], [A("wn", 0, 2560)], [A("zt", 0, 512)])
+                unpacker(b)
             t_product(0, 0, 6)
             t_product(1, 0, 7)
         mm(3, "k1", 128, "cdq", 0, C, start=True, stop=False)
@@ -478,9 +483,8 @@ def rank_program(g, core, T, topo):
                     step(b, gg)
         signed(sum(NV), 14)
         if rd == 0:
-            consts_order_a()
             t_early()
-            consts_lists_a()
+            consts_order_a()
         for b in range(2, max(NV)):
             compare_v(b)
         later = [(b, d) for d in range(4) for b in (2, 3)]
@@ -497,25 +501,28 @@ def rank_program(g, core, T, topo):
         add_ranks(3)
         signed_high()
         add_ranks(4)
-        if rd == 0:
-            ts(A("cst", 1024, 1536), A("om", 0, 512), col(13), col(17), Op.is_equal, Op.mult)
         spread(7, 10)
         add_ranks(1)
         if rd == 0:
             spread(0, 7)
             add_ranks(2, True)
             mirror(0, 10)
+            quant("kc", 0, 256, "cst", 0)
         else:
             add_ranks(2, True)
             spread(min(NV), 7)
-            mirror(min(NV), 10)
-        tt(A("fs", 16, 336), P(3, C), A("thr", 0, 320), Op.is_lt)
+            mirror(7, 10)
+            mirror(min(NV), 7)
+        for a, b in ((224, C), (0, 224)) if rd > 0 else ((0, C),):
+            tt(A("fs", 16 + a, 16 + b), P(3, b, a), A("thr", a, b), Op.is_lt)
         if rd == 0:
-            consts_order_v()
-            t_product(*later[0], 6)
-            t_product(*later[1], 7)
-        t_late(0, 6)
-        if rd > 0:
+            quant("kc", 256, 256, "cst", 1024)
+            for k in range(4):
+                t_product(*later[k], 4 + k)
+                t_late(k, 4 + k)
+            affine(A("pl", 0, 20), A("pl", 0, 20), 1.0, col(23))
+        else:
+            t_late(0, 6)
             t_late(1, 7)
             for k in (2, 3):
                 t_product(*later[k], 2 + k)
@@ -527,63 +534,57 @@ def rank_program(g, core, T, topo):
         mm(0, "kc", 0, "fq", 4, 128, True, False)
         mm(0, "kc", 128, "fq", 0, 128, False, True)
         mm(1, "kc", 256, "fq", 4, 128)
+        if rd == 0:
+            quant("kc", 512, 512, "cst", 2048)
         mm(4, "kc", 512, "fq", 4, 128)
         mm(5, "kc", 640, "fq", 4, 128)
         mm(3, "kc", 768, "fq", 4, 128)
         if rd > 0:
             t_late(4, 6)
         scan(A("st", 8, 88), P(2, 80), A("z80", 0, 80), 0.0, Op.add, Op.add)
-        scan(A("su", 0, 80), P(0, 80), A("z80", 0, 80), -0.5, Op.add, Op.add)
+        scan(A("su", 0, 80), P(0, 80), A("z80", 0, 80), 64.0 * 768, Op.add, Op.add)
         mm(0, "kc", 896, "fq", 4, 128)
         scan(A("sg", 0, 80), A("smk", 0, 80), P(1, 80), 0.0, Op.mult, Op.add)
         ts(A("r0", 0, 80), A("st", 7, 87), col(38), col(38), Op.add, Op.subtract)
-        t_late(*((5, 7) if rd > 0 else (1, 7)))
-        for k in range(6 if rd > 0 else 2, 8):
+        if rd > 0:
+            t_late(5, 7)
+        for k in range(6 if rd > 0 else 4, 8):
             t_product(*later[k], (2, 6, 7)[k % 3])
             t_late(k, (2, 6, 7)[k % 3])
-        n2, y, h2 = L(0), L(1), L(2)
-        tt(A("n2f", 0, 20), A("su", 3, 80, 4), A("sg", 3, 80, 4), Op.mult)
-        ts(A("r1", 0, 80), A("st", 7, 87), col(36), col(36), Op.add, Op.subtract)
-        tt(n2, A("n2f", 0, 20), A("pl", 0, 20), Op.add)
-        tt(A("dg", 0, 80), A("r1", 0, 80), A("r0", 0, 80), Op.subtract)
-        ts(y, n2, 4, 31, Op.arith_shift_right, Op.bitwise_and)
-        ts(h2, n2, 14, None, Op.bitwise_and)
-        tt(A("dat", 0, 320, 4), P(4, 80), A("dg", 0, 80), Op.add)
-        ts(L(3), y, -14, None, Op.mult)
-        ts(L(4), h2, 31, None, Op.mult)
-        tt(A("dat", 1, 320, 4), P(5, 80), A("dg", 0, 80), Op.add)
-        tt(L(5), L(3), n2, Op.add)
-        tt(A("dat", 2, 320, 4), P(3, 80), A("dg", 0, 80), Op.add)
-        tt(L(6), L(5), L(4), Op.add)
-        tt(A("dat", 3, 320, 4), P(0, 80), A("dg", 0, 80), Op.add)
-        copy(A("pos", 0, 20), L(6))
-        slots, lst = A("wn", 0, 2560), A("pos", 0, 20)
-        emit("v", lambda: g.vector.tensor_copy(ap(slots).indirect(ap(lst)), T.dat[:, 0:320]), [slots], [lst, A("dat", 0, 320)])
         if rd == 0:
-            quant("ki", 0, 160, "cci", 0)
-        for a, n in ((0, 256), (256, 256), (512, 128)):
-            quant("nq", a, n, "wn", 4 * a)
-            for s in range(a // 128, (a + n) // 128):
-                mm(1, "nq", 128 * s, "ki", 20 - 2 * s, 128, s == 0, s == 4)
-        steps = [lambda: ts(L(13), n2, 4, None, Op.arith_shift_right),
-                 lambda: ts(L(14), n2, 16, None, Op.bitwise_and),
-                 lambda: ts(L(15), n2, 1, None, Op.bitwise_and),
-                 lambda: ts(L(16), n2, col(27), None, Op.add),
-                 lambda: ts(LF(0), y, -0.5, None, Op.mult),
-                 lambda: ts(LF(1), L(14), 0.96875, None, Op.mult),
-                 lambda: ts(LF(2), L(15), 1280.0, None, Op.mult),
-                 lambda: ts(L(17), L(16), 14, None, Op.bitwise_and),
-                 lambda: tt(LF(3), LF(0), L(13), Op.add),
-                 lambda: tt(LF(4), LF(1), LF(2), Op.add),
-                 lambda: ts(LF(5), L(17), 80.0, None, Op.mult),
-                 lambda: tt(LF(6), LF(3), LF(4), Op.add),
-                 lambda: tt(LF(7), LF(6), LF(5), Op.add),
-                 lambda: copy(A("wl", 0, 20), LF(7))]
+            consts_places_a()
+        num, sign = L(0), A("sg", 3, 80, 4)
+        tt(A("n2f", 0, 20), A("su", 3, 80, 4), sign, Op.mult)
+        ts(A("r1", 0, 80), A("st", 7, 87), col(36), col(36), Op.add, Op.subtract)
+        tt(num, A("n2f", 0, 20), A("pl", 0, 20), Op.add)
+        tt(A("dg", 0, 80), A("r1", 0, 80), A("r0", 0, 80), Op.subtract)
+        ts(L(1), num, 6, 7 * 512, Op.arith_shift_right, Op.bitwise_and)
+        ts(L(2), num, 13, 3, Op.arith_shift_right, Op.bitwise_and)
+        ts(L(3), num, 7 * 64, None, Op.bitwise_and)
+        ts(L(4), num, 7, 15 * 4, Op.arith_shift_right, Op.bitwise_and)
+        tt(L(5), L(1), L(2), Op.add)
+        tt(A("dat", 0, 320, 4), P(4, 80), A("dg", 0, 80), Op.add)
+        tt(L(6), L(3), L(4), Op.add)
+        tt(A("dat", 1, 320, 4), P(5, 80), A("dg", 0, 80), Op.add)
+        tt(L(9), L(5), L(6), Op.add)
+        tt(A("dat", 2, 320, 4), P(3, 80), A("dg", 0, 80), Op.add)
+        copy(A("pos", 0, 20), L(9))
+        tt(A("dat", 3, 320, 4), P(0, 80), A("dg", 0, 80), Op.add)
+        slots, lst = A("wn", 0, 3072), A("pos", 0, 20)
+        steps = [lambda: ts(L(16), num, col(27), None, Op.add),
+                 lambda: ts(L(13), num, 9, None, Op.arith_shift_right),
+                 lambda: ts(LF(0), sign, -736.0, 544.0, Op.mult, Op.add),
+                 lambda: ts(L(17), L(16), 6, 7, Op.arith_shift_right, Op.bitwise_and),
+                 lambda: tt(LF(1), LF(0), L(13), Op.add),
+                 lambda: ts(LF(2), L(17), 160.0, None, Op.mult),
+                 lambda: tt(LF(3), LF(1), LF(2), Op.add),
+                 lambda: copy(A("wl", 0, 20), LF(3))]
         if rd == 0:
             steps.append(lambda: quant("vq", 0, 128, "vt", 0))
         if rd == ROUNDS - 1:
-            steps += [lambda: ts(L(18), n2, 1, None, Op.arith_shift_right),
-                      lambda: tt(A("vf", 0, 20), L(18), LF(2), Op.add),
+            steps += [lambda: ts(L(18), num, 6, None, Op.arith_shift_right),
+                      lambda: ts(LF(4), sign, -1408.0, -128.0, Op.mult, Op.add),
+                      lambda: tt(A("vf", 0, 20), L(18), LF(4), Op.add),
                       lambda: turn32(A("vtr", 0, 32), A("vf", 0, 32))]
 
         def meanwhile(k):
@@ -591,35 +592,59 @@ def rank_program(g, core, T, topo):
                 step()
             del steps[:k]
 
-        meanwhile(4)
-        tt(L(7), P(1, 20), A("s2", 0, 20), Op.add)
+        def places(i, a, n):
+            quant("nq", 384 * i + 128 * a, 128 * n, "wn", 1536 * i + 512 * a)
+            for s in range(a, a + n):
+                mm(1 + 2 * i, "nq", 384 * i + 128 * s, "ki", 12 + 20 * i - 4 * s, 128, s == 0, s == 2)
+
+        def half(s, i):
+            return A(s[0], s[1] + 10 * i, s[1] + 10 * i + 10)
+
+        listing = [lambda i: tt(half(L(7), i), P(1 + 2 * i, 10), A("s2", 0, 10), Op.add),
+                   lambda i: ts(half(L(8), i), half(L(7), i), 3, 7 * TURN + 511, Op.arith_shift_right, Op.bitwise_and),
+                   lambda i: copy(A("off", 10 * i, 10 * i + 10), half(L(8), i))]
         meanwhile(1)
-        ts(L(8), L(7), 3, 7 * TURN + 511, Op.arith_shift_right, Op.bitwise_and)
+        emit("v", lambda: g.vector.tensor_copy(ap(slots).indirect(ap(lst)), T.dat[:, 0:320]), [slots], [lst, A("dat", 0, 320)])
+        if rd == 0:
+            quant("ki", 0, 160, "cci", 0)
+        else:
+            meanwhile(1)
+        places(0, 0, 2)
+        places(0, 2, 1)
+        places(1, 0, 2)
+        listing[0](0)
+        places(1, 2, 1)
+        listing[1](0)
         meanwhile(1)
-        copy(A("off", 0, 20), L(8))
-        meanwhile(1)
+        listing[2](0)
+        listing[0](1)
         for b in range(4):
-            gather("va"[b % 2], A("gt", b, 640, 4), TW(b), A("off", 10, 20))
-        meanwhile(1)
+            gather("va"[b % 2], A("gt", b, 640, 4), TW(b), A("off", 0, 10))
+            if b % 2 == 0:
+                listing[1 + b // 2](1)
         quant("gq", 0, H, "gt", 0)
         send(dst, "gq", "gl%d" % rd, "ga%d" % rd, "gs%d" % rd)
         for b in range(4):
-            gather("aava"[b], A("ft", b, 640, 4), TW(b), A("off", 0, 10))
-        meanwhile(3)
+            gather("avav"[b], A("ft", b, 640, 4), TW(b), A("off", 10, 20))
+        meanwhile(1)
         quant("fqq", 0, H, "ft", 0)
         meanwhile(3)
         layer("fqq", "at", 0)
+
+        def unpack_a(ks, banks):
+            for k in ks:
+                b = [int(e) for e in B_PLAN if e.isdigit()][k // 4]
+                unpack("aq", b, k % 4, k % banks, A_OUT[k], 0)
+                if k % 4 == 3:
+                    halves("s", b, 0)
+
         layer("gl%d" % rd, "bt", 4, lambda: quant("aq", 0, H, "at", 0))
         quant("bq", 0, H, "bt", 0)
         send(dst, "bq", "bl%d" % rd, "ba%d" % rd, "bs%d" % rd)
         if rd < ROUNDS - 1:
-            iota(A("wn", 0, 2560), [[0, 2560]], 0, 0)
+            iota(A("wn", 0, 3072), [[0, 3072]], 0, 0)
         meanwhile(len(steps))
-        for k, q in enumerate(A_OUT):
-            b = [int(e) for e in B_PLAN if e.isdigit()][k // 4]
-            unpack("aq", b, k % 4, k % 8, q, 0)
-            if k % 4 == 3:
-                halves("s", b, 0)
+        unpack_a(range(16), 8)
         k = bank = 0
         for q in B_PLAN:
             if q in "va":
@@ -630,19 +655,21 @@ def rank_program(g, core, T, topo):
                 k += 4
             else:
                 e = int(q)
-                gather_add(A("xn", e, 1280, 4), A("wv", 2560 * e, 2560 * e + 2560), A("wl", 0, 20), A("wt", 320 * e, 320 * e + 320))
+                for a, n in ((H, H), (0, H)) if q == B_PLAN[-1] else ((0, C),):
+                    gather_add(A("xn", 4 * a + e, 4 * (a + n), 4), A("wv", 2560 * e, 2560 * e + 2560), A("wl", a // 16, (a + n) // 16),
+                               A("wt", 320 * e + a, 320 * e + a + n))
 
     dmas("s", [(T.op[k:k + 1, :], T.vtr[32 * (k // 2):32 * (k // 2) + 20, 16 * (k % 2):16 * (k % 2) + 16]) for k in range(8)], [], [A("vtr", 0, 32)])
-    quant("xq", 0, C, "xn", 0)
+    for a in (H, 0):
+        quant("xq", a, H, "xn", 4 * a)
+        mm(a // H, "vq", 0, "xq", a, H)
     dma("s", T.oc[:, :], T.xq[:, 0:C].bitcast(dt.uint8), [], [A("xq", 0, C)])
-    mm(0, "vq", 0, "xq", 0, H)
-    mm(1, "vq", 0, "xq", H, H)
+    act(A("yo", H, C), P(1, H), Fn.Copy)
+    copy(A("yo", 0, H), P(0, H))
+    dma("a", T.y[:, H:C], T.yo[:, H:C], [], [A("yo", H, C)])
     for k in range(4):
-        dma("s", T.osc[4 * k:4 * k + 4, :], T.xqs[32 * k:32 * k + 4, 0:C], [], [A("xqs", 0, C)])
-    act(A("yo", 0, H), P(0, H), Fn.Copy)
-    copy(A("yo", H, C), P(1, H))
-    dma("a", T.y[:, 0:H], T.yo[:, 0:H], [], [A("yo", 0, H)])
-    dma("s", T.y[:, H:C], T.yo[:, H:C], [], [A("yo", H, C)])
+        dma("sa"[k % 2], T.osc[4 * k:4 * k + 4, :], T.xqs[32 * k:32 * k + 4, 0:C], [], [A("xqs", 0, C)])
+    dma("s", T.y[:, 0:H], T.yo[:, 0:H], [], [A("yo", 0, H)])
     for s in sorted(final):
         if known["p"].get(s, 0) < final[s]:
             g.wait_ge(T.sem[s], final[s])

@@ -1,20 +1,18 @@
 import math
-from concourse.bass import DstId, RemoteDMATransfer
 from concourse.mybir import dt, AluOpType as Op, ActivationFunctionType as Fn
 
 C, H, ROUNDS = 320, 160, 3
 MASK = [1, 2, 3]
 U8, F8, BF, F32, I32, U16 = "uint8", "float8_e4m3fn_x4", "bfloat16", "float32", "int32", "uint16"
-T_PRODUCTS = 4
-NV = (6, 5)
-WIDE = H
+NV = (6, 6)
+T_TURNS = {0: (4, 5), 1: (6, 7), 2: (), 3: ()}
 TURN = 2048
 FAR = 2.0 ** 90
 A_OUT = "aavaavav" + "avavavav"
-B_PLAN = "vava>" + "vava>" + "vavavava" + "vav2aa0aaa" + "13"
+B_PLAN = "vava>" + "vava>" + "vavavava" + "vav2aa0aaa"
+LAST = (3, 1)
 
-SLOTS = [[("a", b, 32 * b) for b in range(9, nv - 1, -1)] + [("v", k, 32 * nv) for k in range(nv - 1)] for nv in NV]
-WIDTH = [max(s[k][2] for s in SLOTS) for k in range(0, 9, 2)]
+WIDTH = [max(32 * b, 128) for b in (9, 7, 5, 3, 1)]
 
 SCRATCH = {}
 
@@ -32,27 +30,26 @@ for _k in range(8):
     SCRATCH["ps%d" % _k] = ("psum", [128, 512], F32)
 for _n, _w in (("xin", 1280), ("xn", 1280), ("ut", 512), ("vt", 512), ("ones", 128), ("zt", 512), ("zs", 1152), ("cd", 1280),
                ("fs", 528), ("dat", 320), ("wn", 3072), ("wt", 7 * TURN + 1280), ("wv", 10240), ("gt", 640), ("ft", 640), ("at", 640),
-               ("bt", 640), ("tri", 320), ("row", 320), ("est", 520), ("cst", 4096), ("cc1", 1024), ("cci", 640), ("om", 512), ("oa", 512),
-               ("j32", 320), ("jq", 320), ("smk", 80), ("sgn", 64), ("jg", 64)):
+               ("bt", 640), ("tri", 320), ("row", 160), ("est", 520), ("cst", 4096), ("cc1", 512), ("cci", 640), ("om", 512),
+               ("j32", 160), ("jq", 160), ("smk", 80), ("sgn", 64), ("jg", 64), ("dd", 640), ("sv", 320), ("rs", 192 * sum(NV))):
     _sb(_n, _w, BF)
 _mx("cdq", 320)
 for _k, _w in enumerate(WIDTH):
     _sb("ct%d" % _k, 4 * _w, BF)
     _mx("cq%d" % _k, _w)
-for _n, _w in (("pm", 640), ("pt", 640), ("acc", 24), ("aw", 48), ("sp", 320), ("thr", 320), ("su", 80), ("sg", 80), ("st", 96), ("r1", 160),
-               ("r0", 160), ("dg", 80), ("n2f", 32), ("vf", 32), ("vtr", 32), ("sc", 40), ("pl", 20), ("s2", 20),
-               ("z80", 80), ("yo", 320), ("lf", 200)):
+for _n, _w in (("pt", 640), ("aw", 40), ("sp", 320), ("thr", 320), ("su", 80), ("sg", 80), ("st", 96),
+               ("n2f", 32), ("vf", 32), ("vtr", 32), ("sc", 40), ("pl", 20), ("s2", 20), ("yo", 320), ("lf", 200)):
     _sb(_n, _w, F32)
-for _n, _w in (("pi", 16), ("lui", 40), ("li", 400)):
+for _n, _w in (("pi", 16), ("lui", 40), ("li", 400), ("r1", 80), ("dg", 80)):
     _sb(_n, _w, I32)
 for _n, _w in (("lu", 16), ("lt", 20), ("pos", 32), ("off", 32), ("wl", 32)):
     _sb(_n, _w, U16)
-for _n, _w in (("xq", 320), ("uq", 128), ("us", 256), ("vq", 128), ("wq", 512), ("er", 960), ("kc", 1024), ("k1", 256),
-               ("ki", 160), ("fq", 132), ("nq", 768), ("gq", WIDE), ("fqq", 160), ("aq", 160), ("bq", WIDE)):
+for _n, _w in (("xq", 320), ("uq", 128), ("us", 256), ("vq", 128), ("wq", 512), ("er", 960), ("kc", 1024), ("k1", 128),
+               ("ki", 160), ("fq", 132), ("nq", 768), ("gq", H), ("fqq", H), ("aq", H), ("bq", H)):
     _mx(_n, _w)
 for _k in range(ROUNDS):
-    _mx("gl%d" % _k, WIDE)
-    _mx("bl%d" % _k, WIDE)
+    _mx("gl%d" % _k, H)
+    _mx("bl%d" % _k, H)
 
 SEMAPHORES = ["ev", "ea", "et", "ep"] + ["d%d" % _k for _k in range(130)]
 for _k in range(ROUNDS):
@@ -91,10 +88,10 @@ def rank_program(g, core, T, topo):
             inside = s[1] <= x[1] and x[2] <= s[2] and (s[3] == 1 or (s[3] == x[3] and (s[1] - x[1]) % s[3] == 0))
             if loose or not (inside and (w or (r[2] == q and not r[1]))):
                 keep.append(r)
-        keep.append((s, w, q, token, loose))
+        keep.append((s, w, q, token))
         log[s[0]] = keep
 
-    def emit(q, fn, outs, ins, token=None, acc=False, loose=False):
+    def emit(q, fn, outs, ins, token=None, acc=False):
         tokens = []
         for lst, w in ((ins, False), (outs, True)):
             for s in lst:
@@ -103,8 +100,6 @@ def rank_program(g, core, T, topo):
                     if bank:
                         if not (r[2] == q and (acc or not (w or r[1]))):
                             tokens.append(r[3])
-                    elif loose and w and r[1] and r[2] == q and r[4]:
-                        continue
                     elif (w or r[1]) and hit(s, r[0]):
                         tokens.append(r[3])
         need(q, tokens)
@@ -119,7 +114,7 @@ def rank_program(g, core, T, topo):
         for s in ins:
             note(s, False, q, token, q == "s")
         for s in outs:
-            note(s, True, q, token, loose)
+            note(s, True, q, token)
 
     def dmas(q, sides, outs, ins):
         tok = ("d%d" % ndma[0], 16 * len(sides))
@@ -175,6 +170,12 @@ def rank_program(g, core, T, topo):
     def P(bank, n, a=0):
         return A("ps%d" % bank, a, n)
 
+    def take(q, o, i):
+        if q == "v":
+            copy(o, i)
+        else:
+            act(o, i, Fn.Copy)
+
     def gather(q, o, win, lst):
         if q == "v":
             emit("v", lambda: g.vector.tensor_copy(ap(o), ap(win).indirect(ap(lst))), [o], [win, lst])
@@ -195,9 +196,9 @@ def rank_program(g, core, T, topo):
         snaps[tok], snaps[arr] = dict(known["p"]), {}
         final[done], final[sem] = total, total
         for nm in (src, src + "s"):
-            note(A(nm, 0, WIDE), False, "p", tok)
+            note(A(nm, 0, H), False, "p", tok)
         for nm in (land, land + "s"):
-            log[nm] = [(A(nm, 0, WIDE), True, "r", arr, False)]
+            log[nm] = [(A(nm, 0, H), True, "r", arr)]
 
     def iota(o, pattern, base, cm):
         if o[0] in ("pi", "lui"):
@@ -217,137 +218,149 @@ def rank_program(g, core, T, topo):
     def fill(s, c):
         act(s, A("ones", 0, len(range(s[1], s[2], s[3]))), Fn.Copy, scale=c)
 
-    dma("a", T.ut[:, :], T.u[:, :], [A("ut", 0, 512)], [])
-    dma("s", T.xin[:, :], T.x[:, :], [A("xin", 0, 1280)], [])
-
-    memset(A("zt", 0, 512), 0.0)
-    iota(A("pi", 0, 1), [[0, 1]], 0, 1)
-    for k, (shift, keep) in enumerate(((0, 15), (0, 31), (4, 7), (4, 6), (0, 1), (1, 3), (3, 1), (2, 3), (0, 7))):
-        ts(pcol(k + 1), pcol(0), shift, keep, Op.arith_shift_right, Op.bitwise_and)
-    memset(A("ones", 0, 128), 1.0)
-    copy(A("sc", 0, 10), A("pi", 0, 10))
-    iota(A("jg", 0, 64), [[1, 8], [0, 8]], 0, 0)
-    iota(A("lui", 0, 16), [[16, 2], [32, 4], [0, 2]], 0, 0)
-    iota(A("j32", 0, 320), [[0, 10], [1, 32]], 0, 0)
-    dmas("s", [(T.est[:, 0:512], T.zt[:, 0:512]), (T.est[:, 512:520], T.zt[:, 0:8])], [A("est", 0, 520)], [A("zt", 0, 512)])
-    iota(A("om", 0, 512), [[1, 8], [8, 16], [-8, 4]], 0, 0)
-    iota(A("jq", 0, 320), [[0, 40], [1, 4], [0, 2]], 0, 0)
-    select(A("est", 3, 515, 4), A("ones", 0, 128), [[-1, 128]], Op.is_equal, 0, 1)
-    iota(A("lui", 16, 30), [[2, 14]], 0, 0)
-    iota(A("lui", 30, 36), [[2, 6]], 0, 0)
-    for k, n in enumerate(WIDTH[:4]):
-        for e in range(4):
-            a = SLOTS[e % 2][2 * k + e // 2][2]
-            if a < n:
-                iota(A("ct%d" % k, 4 * a + e, 4 * n, 4), [[0, n - a]], 0, 0)
-
     def affine(o, i, scale, bias):
         act(o, i, Fn.Identity, bias=bias, scale=scale)
 
+    dma("s", T.ut[:, :], T.u[:, :], [A("ut", 0, 512)], [])
+    dma("s", T.xin[:, 640:1280], T.x[:, 640:1280], [A("xin", 640, 1280)], [])
+    dma("s", T.xin[:, 0:640], T.x[:, 0:640], [A("xin", 0, 640)], [])
+
+    memset(A("est", 0, 520), 0.0)
+    memset(A("ones", 0, 128), 1.0)
+    memset(A("zt", 0, 512), 0.0)
+    for o, a, b in (("cc1", 0, 512), ("ct2", 512, 640), ("ct1", 768, 896), ("ct0", 1024, 1152)):
+        act(A(o, a, b), A("zt", 0, b - a), Fn.Copy)
+    iota(A("pi", 0, 1), [[0, 1]], 0, 8)
+    iota(A("lui", 0, 16), [[16, 2], [32, 4], [0, 2]], 0, 0)
+    select(A("est", 3, 515, 4), A("ones", 0, 128), [[-1, 128]], Op.is_equal, 0, 1)
+    for k, (shift, keep) in enumerate(((3, 15), (2, 62), (7, 7), (7, 6), (3, 1), (4, 1), (5, 2), (0, 96), (3, 7))):
+        ts(pcol(k + 1), pcol(0), shift, keep, Op.arith_shift_right, Op.bitwise_and)
     copy(A("lu", 0, 16), A("lui", 0, 16))
-    ts(col(10), col(4), 1.0, None, Op.add)
-    affine(col(21), col(2), FAR, 0.5 * FAR)
-    affine(col(11), col(5), -2.0, 1.0)
-    affine(col(12), col(7), -1.0, 1.0)
-    affine(A("tri", 0, 320), A("j32", 0, 320), -FAR, col(21))
-    affine(col(13), col(6), 32.0, col(3))
-    affine(col(17), col(11), col(12), 0.0)
-    affine(col(14), col(2), 2.0, -31.0)
-    affine(col(24), col(2), -2.0, 31.0)
-    affine(col(18), col(13), -1.0, -0.5)
-    affine(col(19), col(17), 16.0, 0.0)
-    affine(col(20), col(17), -16.0, 0.0)
+    quant("er", 0, 128, "est", 3)
+    copy(A("sc", 0, 10), A("pi", 0, 10))
+    iota(A("jg", 0, 64), [[-1, 2], [1, 8], [0, 4]], 0, 0)
+    iota(A("j32", 0, 160), [[0, 5], [2, 32]], 1, 0)
+    iota(A("jq", 0, 160), [[0, 20], [32, 4], [0, 2]], 0, 0)
+    iota(A("lui", 24, 26), [[5, 2]], 0, 0)
+    iota(A("lui", 16, 24), [[8, 4], [5, 2]], 0, 0)
+    iota(A("om", 0, 512), [[1, 8], [8, 16], [-8, 4]], 0, 0)
+    iota(A("sp", 1, 320, 2), [[0, 160]], -4096, 0)
+
+    affine(col(17), col(6), -2.0, 1.0)
+    affine(col(19), col(6), -64.0, 32.0)
+    affine(col(13), col(8), 1.0, col(3))
+    affine(col(23), col(3), 32.0 - 4096, 0.0)
     fill(A("sgn", 0, 32), col(17))
-    for e in (0, 2, 1, 3):
-        for s in range(2):
-            ts(A("cc1", 4 * s + e, 512, 8), A("jg", 0, 64), col((4, 10)[e % 2]), 1.0 - 2 * s, Op.is_equal, Op.mult)
-    ts(col(23), col(3), 32.0 - 4096, None, Op.mult)
-    ts(col(27), col(3), -64.0, 512.0, Op.mult, Op.add)
-
-    for o, a, b in (("ct4", 0, 4 * WIDTH[4]), ("cst", 1024, 1536), ("cst", 2048, 4096), ("fs", 0, 528), ("cci", 0, 640), ("wn", 0, 3072)):
-        dmas("s", [(T[o][:, w:min(w + 512, b)], T.zt[:, 0:min(512, b - w)]) for w in range(a, b, 512)], [A(o, a, b)], [A("zt", 0, 512)])
-    dma("s", T.wq[:, :].bitcast(dt.uint8), T.wc[:, :], [A("wq", 0, 512)], [])
-    dma("s", T.wqs[:, :], T.ws[:, :], [A("wqs", 0, 512)], [])
-    dma("s", T.vt[:, :], T.v[:, :], [A("vt", 0, 512)], [])
-
-    def unpacker(b):
-        a = 240 * b
-        quant("er", a, 128, "est", 3 - b)
-        dma("s", T.er[:, a + 128:a + 240].bitcast(dt.uint8), T.er[:, a:a + 112].bitcast(dt.uint8), [A("er", a + 128, a + 240)], [A("er", a, a + 112)])
-        dma("s", T.ers[:, a + 128:a + 240], T.ers[:, a:a + 112], [A("ers", a + 128, a + 240)], [A("ers", a, a + 112)])
-
+    for b in range(1, 3):
+        quant("er", 240 * b, 128, "est", 3 - b)
     quant("uq", 0, 128, "ut", 0)
-    lst = A("lu", 0, 16)
-    emit("a", lambda: g.scalar.activation(T.uss[:, 0:256], T.uqs[:, 0:128].indirect(ap(lst)), Fn.Copy), [A("uss", 0, 256)], [A("uqs", 0, 128), lst])
-    emit("v", lambda: g.vector.tensor_copy(T.us[:, 0:256].bitcast(dt.uint32), T.uq[:, 0:128].bitcast(dt.uint32).indirect(ap(lst))),
-         [A("us", 0, 256)], [A("uq", 0, 128), lst])
-    for e in range(4):
-        act(A("cc1", 512 + e, 1024, 4), A("cc1", e, 512, 4), Fn.Copy, scale=(2.0, 2.0, -2.0, -2.0)[e])
-    act(A("oa", 0, 512), A("om", 0, 512), Fn.Sign, bias=col(18))
-    affine(A("cst", 0, 512), A("oa", 0, 512), col(19), col(19))
+    for e in range(2):
+        for s in range(2):
+            ts(A("cc1", 8 * s + e, 512, 16), A("jg", 32 * e, 32 * e + 32), col(4), 2.0 * s - 1, Op.is_equal, Op.mult)
+
+    def zeros(*runs):
+        for o, a, b in runs:
+            dmas("s", [(T[o][:, w:min(w + 512, b)], T.zt[:, 0:min(512, b - w)]) for w in range(a, b, 512)], [A(o, a, b)], [A("zt", 0, 512)])
+
+    zeros(("ct3", 256, 512), ("ct4", 0, 512), ("cst", 1536, 4096))
+
+    def later_dmas():
+        for a in range(0, 960, 240):
+            dma("s", T.er[:, a + 128:a + 240].bitcast(dt.uint8), T.er[:, a:a + 112].bitcast(dt.uint8), [A("er", a + 128, a + 240)], [A("er", a, a + 112)])
+            dma("s", T.ers[:, a + 128:a + 240], T.ers[:, a:a + 112], [A("ers", a + 128, a + 240)], [A("ers", a, a + 112)])
+        zeros(("fs", 0, 16), ("fs", 336, 528), ("cci", 0, 640), ("wn", 0, 3072))
+
+    def scoring(gg):
+        a, lst = 128 * gg, A("lu", 8 * gg, 8 * gg + 8)
+        emit("a", lambda: g.scalar.activation(T.uss[:, a:a + 128], T.uqs[:, 0:128].indirect(ap(lst)), Fn.Copy),
+             [A("uss", a, a + 128)], [A("uqs", 0, 128), lst])
+        emit("v", lambda: g.vector.tensor_copy(T.us[:, a:a + 128].bitcast(dt.uint32), T.uq[:, 0:128].bitcast(dt.uint32).indirect(ap(lst))),
+             [A("us", a, a + 128)], [A("uq", 0, 128), lst])
+
+    scoring(0)
     select(A("smk", 0, 80), A("ones", 0, 80), [[0, 20], [1, 4]], Op.is_gt, 0, 0)
     iota(A("pl", 0, 20), [[4096, 20]], 64 * 768, 256)
-    iota(A("s2", 0, 10), [[256, 10]], 64 * 16384, 16)
-    for s in (A("z80", 0, 80), A("st", 0, 8), A("vf", 0, 32)):
-        iota(s, [[0, s[2]]], 0, 0)
-    select(A("sgn", 32, 64), A("sgn", 0, 32), [[16, 8], [2, 4]], Op.is_ge, 1, -1)
+    iota(A("s2", 0, 20), [[2560, 2], [256, 10]], 64 * 16384 - 1280, 16)
+    for gg in range(2):
+        iota(A("aw", 2 * gg, 2 * gg + 2), [[64 - 64 * NV[gg], 2]], 32 * NV[gg] - 32, 0)
+    iota(A("vf", 20, 32), [[0, 12]], 0, 0)
+    iota(A("st", 0, 8), [[0, 8]], 0, 0)
+    select(A("sgn", 32, 64), A("sgn", 0, 32), [[16, 8], [4, 4]], Op.is_ge, 3, -1)
     for e in range(4):
-        select(A("cst", 1024 + 5 * e, 1536, 16), A("sgn", 32, 64), [[-16, 8], [-2, 4]], Op.is_ge, 0, 1)
+        select(A("cst", 1536 + 5 * e, 2048, 16), A("sgn", 32, 64), [[-16, 8], [-4, 4]], Op.is_ge, 0, 1)
     for b in range(4):
         for e in range(b + 1):
             select(A("cst", 2048 + 512 * b + 4 * (3 + e // 2) + e, 2048 + 512 * b + 512, 32), A("sgn", 0, 16), [[16, 8], [0, 2]], Op.is_gt,
                    0 if e == b else 128, -1)
 
-    def consts_order_a():
-        affine(A("cst", 512, 1024), A("oa", 0, 512), col(20), col(19))
-        affine(A("cst", 1536, 2048), A("oa", 0, 512), 0.0, col(17))
+    def consts_ranks():
+        act(A("row", 0, 160), A("j32", 0, 160), Fn.Sign, bias=col(2), scale=-1.0)
+        affine(col(26), col(8), -FAR, 0.0)
+        affine(col(14), col(2), 1.0, -31.0)
+        affine(col(24), col(2), -1.0, 31.0)
+        for a in (0, H):
+            affine(A("tri", a, a + H), A("row", 0, 160), 1.0, -1.0)
+
+    def consts_signs():
+        for e in range(2):
+            act(A("cc1", 2 + e, 512, 4), A("cc1", e, 512, 4), Fn.Copy, scale=-1.0)
+        act(A("row", 0, 160), A("jq", 0, 160), Fn.Abs, bias=col(26), scale=FAR)
 
     def consts_flags():
-        ts(A("lt", 0, 20), A("lui", 16, 36), col(5), None, Op.add)
-        ts(col(38), col(29), 32.0, col(33), Op.mult, Op.add)
-        for gg in range(2):
-            ts(A("aw", 2 * gg, 24, 4), A("ones", 0, 6), col(14), 288.0 - 32 * (10 - NV[gg]), Op.mult, Op.add)
-        ts(A("row", 0, 320), A("jq", 0, 320), col(8), FAR, Op.not_equal, Op.mult)
-        ts(A("aw", 1, 24, 2), A("aw", 0, 24, 2), -1.0, None, Op.mult)
+        ts(A("lt", 0, 10, 2), A("lui", 16, 26, 2), col(7), col(5), Op.add, Op.add)
+        ts(A("lt", 1, 10, 2), A("lui", 17, 26, 2), col(7), col(5), Op.add, Op.subtract)
+        affine(A("row", 0, 160, 2), A("row", 0, 160, 2), 1.0, col(24))
+        affine(A("row", 1, 160, 2), A("row", 1, 160, 2), 1.0, col(14))
 
-    def consts_places_a():
-        affine(col(22), col(7), 16383.0, 1.0)
-        affine(col(34), col(7), -16383.0, -1.0)
+    def consts_order():
+        ts(A("cst", 512, 1024), A("om", 0, 512), col(13), col(19), Op.is_gt, Op.mult)
+        affine(A("cst", 1024, 1536), A("cst", 512, 1024), -1.0, col(19))
+
+    small = [lambda: ts(col(30), col(1), 1.0, 16.0, Op.is_equal, Op.mult),
+             lambda: ts(col(31), col(9), 2.0, 256.0, Op.is_equal, Op.mult),
+             lambda: ts(col(33), col(1), 0.0, col(30), Op.is_equal, Op.add),
+             lambda: ts(col(36), col(33), col(31), None, Op.add),
+             lambda: ts(A("pl", 0, 20), A("pl", 0, 20), col(23), None, Op.add),
+             lambda: ts(col(38), col(36), 1280.0, None, Op.mult)]
+
+    def once(k):
+        for step in small[:k]:
+            step()
+        del small[:k]
+
+    def consts_places():
+        affine(col(21), col(7), 16383.0 / 2, 1.0)
+        affine(col(12), col(30), -15.0 / 256, 1.0)
         affine(col(25), col(3), 16386.0 - 256, 0.0)
+        affine(col(27), col(3), -64.0, 512.0)
+        affine(col(15), col(31), -255.0 / 65536, col(12))
+        affine(A("s2", 0, 20), A("s2", 0, 20), 1.0, col(25))
+        affine(col(22), col(15), col(21), 0.0)
+        affine(col(34), col(22), -1.0, 0.0)
         fill(A("cci", 48, 64, 5), col(22))
         fill(A("cci", 128, 144, 5), col(34))
-        affine(A("s2", 0, 10), A("s2", 0, 10), 1.0, col(25))
-
-    def consts_digits():
-        ts(col(29), col(1), 0.0, 1.5 * 2.0 ** 30, Op.is_equal, Op.mult)
-        ts(col(30), col(1), 1.0, 1.5 * 2.0 ** 26, Op.is_equal, Op.mult)
-        ts(col(31), col(9), 2.0, 1.5 * 2.0 ** 26, Op.is_equal, Op.mult)
-        tt(col(36), col(29), col(30), Op.add)
-        ts(col(33), col(30), 16.0, col(31), Op.mult, Op.add)
-
 
     def unpack(pair, b, d, bank, q, i):
         mm(bank, "er", 240 * b + 16 * d, pair, 0, H)
         k = 2560 * b + 1280 * i + 160 * d
-        if q == "v":
-            copy(A("wv", k, k + H), P(bank, H))
-        else:
-            act(A("wv", k, k + H), P(bank, H), Fn.Copy)
+        take(q, A("wv", k, k + H), P(bank, H))
+
+    def splice(e, a, n):
+        gather_add(A("xn", 4 * a + e, 4 * (a + n), 4), A("wv", 2560 * e, 2560 * e + 2560), A("wl", a // 16, (a + n) // 16),
+                   A("wt", 320 * e + a, 320 * e + a + n))
 
     def halves(q, b, i):
         k = 2560 * b + 1280 * i
         o, src = A("wv", k + 640, k + 1280), A("wv", k, k + 640)
         dmas(q, [(T.wv[to:to + 64, k + 640:k + 1280], T.wv[fr:fr + 64, k:k + 640]) for to, fr in ((0, 64), (64, 0))], [o], [src])
 
-    def by_dma(to, fr, d, a):
-        o, i, k = A("wt", TURN * to + a, TURN * to + a + 640), A("wt", TURN * fr + a, TURN * fr + a + 640), 128 - 16 * d
-        dmas("s", [(T.wt[0:k, o[1]:o[2]], T.wt[16 * d:128, i[1]:i[2]]), (T.wt[k:128, o[1]:o[2]], T.wt[0:16 * d, i[1]:i[2]])], [o], [i])
+    def t_copy(to, fr):
+        o, i, d = A("wt", TURN * to, TURN * to + 1280), A("wt", TURN * fr, TURN * fr + 1280), 16 * ((to - fr) % 8)
+        dmas("s", [(T.wt[0:128 - d, o[1]:o[2]], T.wt[d:128, i[1]:i[2]]), (T.wt[128 - d:128, o[1]:o[2]], T.wt[0:d, i[1]:i[2]])], [o], [i])
 
-    def layer(pair, tile, bank, first=None):
+    def layer(pair, tile, bank):
         for b in range(4):
             mm(bank + b, "wq", 128 * b, pair, 0, H)
-        if first:
-            first()
         for b in range(4):
             o = A(tile, b, 4 * H, 4)
             if b % 2 == 1:
@@ -365,27 +378,26 @@ def rank_program(g, core, T, topo):
         return A("wt", 320 * b, 320 * b + 7 * TURN + 320)
 
     def own(gg, b):
-        return A("pt", 320 * gg + 32 * b + 31, 320 * gg + 32 * b + 32)
+        return A("pt", 320 * gg + 32 * b, 320 * gg + 32 * b + 1)
 
     def t_product(b, d, bank):
         mm(bank, "er", 240 * b + 16 * d, "xq", 0, C)
 
-    def t_out(b, d, bank):
-        act(A("wt", TURN * d + 320 * b, TURN * d + 320 * b + 320), P(bank, C), Fn.Copy)
+    def t_out(b, d, bank, q="a"):
+        take(q, A("wt", TURN * d + 320 * b, TURN * d + 320 * b + 320), P(bank, C))
 
-    def where(kind, k, gg):
-        i = [p[:2] for p in SLOTS[gg]].index((kind, k))
-        return "ct%d" % (i // 2), 2 * (i % 2) + gg
+    def lane(b, gg):
+        return A("ct%d" % ((9 - b) // 2), 2 * ((9 - b) % 2) + gg, 128 * b, 4)
 
-    def compare_v(b):
-        for gg in range(2):
-            nv = NV[gg]
-            if 0 < b < nv:
-                t, e = where("v", b - 1, gg)
-                ts(A(t, e, 128 * b, 4), P(1 + gg, 32 * b), own(gg, b), 2.0, Op.is_lt, Op.mult)
-            if b < nv - 1:
-                t, e = where("v", b, gg)
-                ts(A(t, 128 * b + 128 + e, 128 * nv, 4), P(1 + gg, 32 * nv, 32 * b + 32), own(gg, b), 2.0, Op.is_le, Op.mult)
+    def sense(b):
+        return -1.0 if b % 2 else 1.0
+
+    def compare_v(b, gg):
+        ts(lane(b, gg), P(1 + gg, 32 * b), own(gg, b), 2.0 * sense(b), Op.is_lt, Op.mult)
+
+    def sums_v(b, gg):
+        end = 192 * (2 * b + gg + 1)
+        scan(A("rs", end - 32 * b, end), lane(b, gg), A("zt", 0, 32 * b), (32.0 * NV[gg] - 32 - 64 * b) * sense(b), Op.add, Op.add)
 
     def zs(b, gg):
         return A("zs", 288 * (2 * (b % 2) + gg), 288 * (2 * (b % 2) + gg) + 32 * b)
@@ -394,197 +406,148 @@ def rank_program(g, core, T, topo):
         act(zs(b, gg), P(4 + gg, 32 * b), Fn.Sign, bias=own(gg, b), scale=-1.0)
 
     def sums(b, gg):
-        t, e = where("a", b, gg)
-        act(A(t, e, 128 * b, 4), zs(b, gg), Fn.Sign, bias=-0.5, total=A("acc", 2 * b + gg, 2 * b + gg + 1))
+        act(lane(b, gg), zs(b, gg), Fn.Sign, bias=-0.5 * sense(b), scale=sense(b), total=A("aw", 4 * b + 2 * gg, 4 * b + 2 * gg + 1))
 
-    def compare_a(b):
+    def compare_a(pairs):
         for step in (signs, sums):
-            for gg in range(2):
-                if b >= NV[gg]:
-                    step(b, gg)
+            for b, gg in pairs:
+                step(b, gg)
 
     def add_ranks(k, stop=False):
         n = WIDTH[k]
         quant("cq%d" % k, 0, n, "ct%d" % k, 0)
         mm(3, "k1", 0, "cq%d" % k, 0, n, start=False, stop=stop)
 
-    def signed(a, b):
-        affine(A("aw", 2 * a, 2 * b, 2), A("acc", a, b), 1.0, col(14))
-        affine(A("aw", 2 * a + 1, 2 * b, 2), A("acc", a, b), -1.0, col(24))
+    def bounds(a, b):
+        gather_add(A("sp", 32 * a, 32 * b, 2), A("aw", 4 * a, 4 * b), A("lt", a, b), A("row", 16 * a, 16 * b), Op.subtract)
 
-    def signed_high():
-        ts(A("aw", 32, 44, 2), A("acc", 14, 20), col(14), None, Op.add)
-        ts(A("aw", 33, 44, 2), A("acc", 14, 20), col(14), -1.0, Op.add, Op.mult)
-
-    def spread(a, b):
-        win = A("aw", 32, 44) if a == 7 else A("aw", 0, 28)
-        gather_add(A("sp", 32 * a, 32 * b), win, A("lt", 2 * a, 2 * b), A("row", 32 * a, 32 * b), Op.subtract)
-
-    def mirror(a, b):
-        turn32(A("thr", 32 * a, 32 * b), A("sp", 32 * a, 32 * b))
+    def turn_high(tile):
+        quant("xq", H, H, tile, 4 * H)
+        mm(3, "us", 0, "xq", H, H)
+        if tile == "xin":
+            scoring(1)
+        mm(0, "us", 128, "xq", H, H)
 
     for rd in range(ROUNDS):
         dst = T.cores[rank ^ MASK[rd]]
+        if rd == 0:
+            turn_high("xin")
+        quant("xq", 0, H, "xin" if rd == 0 else "xn", 0)
+        mm(1, "us", 0, "xq", 0, max(H, 32 * NV[0] - 32))
+        mm(4, "us", 0, "xq", 0, 288)
+        mm(2, "us", 128, "xq", 0, max(H, 32 * NV[1] - 32))
+        mm(5, "us", 128, "xq", 0, 288)
+        turns, ahead = [(b, d) for d in T_TURNS for b in range(4)], []
 
-        def t_early():
-            for b in (0, 1):
-                t_out(b, 0, 6 + b)
-            for d in range(1, 8):
-                by_dma(d, 0, d, 0)
+        def t_products(banks):
+            for bank in banks:
+                t_product(*turns[0], bank)
+                ahead.append(turns.pop(0) + (bank,))
 
-        for a in (H, 0):
-            quant("xq", a, H, "xin" if rd == 0 else "xn", 4 * a)
-            mm(3 * a // H, "us", 0, "xq", a, H)
-        if rd > 0:
-            t_product(0, 0, 6)
-        mm(2, "us", 128, "xq", 0, C)
-        if rd > 0:
-            t_product(1, 0, 7)
-        mm(4, "us", 0, "xq", 0, C)
-        mm(1, "us", 0, "xq", 0, C)
-        mm(5, "us", 128, "xq", 0, C)
-        if rd > 0:
-            t_early()
-        else:
-            consts_digits()
-            quant("k1", 0, 128, "cc1", 0)
-        steps = (lambda gg: tt(A("pm", 320 * gg, 320 * gg + 320), P(1 + gg, C), A("tri", 0, 320), Op.min),
-                 lambda gg: turn32(A("pt", 320 * gg, 320 * gg + 320), A("pm", 320 * gg, 320 * gg + 320)),
-                 lambda gg: tt(A("cd", gg, 1280, 4), P(1 + gg, C), A("pt", 320 * gg, 320 * gg + 320), Op.is_le),
-                 lambda gg: turn32(A("cd", 2 + gg, 1280, 4), A("cd", gg, 1280, 4)))
-        for a in (H, 0):
-            tt(A("pm", a, a + H), P(3 * a // H, H), A("tri", 0, H), Op.min)
-        for a in (H, 0):
-            turn32(A("pt", a, a + H), A("pm", a, a + H))
-        for k, gg in ((0, 1), (2, 0), (1, 1), (3, 0), (2, 1)):
-            steps[k](gg)
-        compare_v(0)
-        steps[3](1)
-        compare_v(1)
+        def t_outs(qs):
+            for q in qs:
+                b, d, bank = ahead.pop(0)
+                t_out(b, d, bank, q)
+                for to in T_TURNS[d] if b == 3 else ():
+                    t_copy(to, d)
+
+        t_products((6, 7))
+        if rd == 0:
+            quant("er", 720, 128, "est", 0)
+            later_dmas()
+            consts_ranks()
+        for a, banks in ((H, (3, 0)), (0, (1, 2))):
+            for gg in range(2):
+                turn32(A("pt", 320 * gg + a, 320 * gg + a + H), P(banks[gg], H))
+            once(1)
+            for gg in range(2):
+                tt(A("dd", 320 * gg + a, 320 * gg + a + H), P(banks[gg], H), A("pt", 320 * gg + a, 320 * gg + a + H), Op.is_le)
+        compare_a([(7, 0), (6, 0)])
+        if rd == 0:
+            consts_signs()
+        for gg in range(2):
+            scan(A("cd", gg, 1280, 4), A("dd", 320 * gg, 320 * gg + 320), A("tri", 0, 320), 0.0, Op.max, Op.mult)
+        once(1)
+        low = [(b, gg) for b in range(max(NV) - 1, 0, -1) for gg in range(2) if b < NV[gg]]
+        compare_v(*low[0])
+        for gg in range(2):
+            turn32(A("cd", 2 + gg, 1280, 4), A("cd", gg, 1280, 4))
+        compare_v(*low[1])
+        compare_v(*low[2])
         quant("cdq", 0, C, "cd", 0)
         if rd == 0:
-            quant("k1", 128, 128, "cc1", 512)
-            for b in range(4):
-                unpacker(b)
-            t_product(0, 0, 6)
-            t_product(1, 0, 7)
-        mm(3, "k1", 128, "cdq", 0, C, start=True, stop=False)
-        for gg in range(2):
-            for b in (9, 8):
-                signs(b, gg)
-            for b in (9, 8):
-                sums(b, gg)
+            quant("k1", 0, 128, "cc1", 0)
+        mm(3, "k1", 0, "cdq", 0, C, start=True, stop=False)
+        compare_a([(7, 1), (6, 1)])
         if rd == 0:
             consts_flags()
-        compare_a(7)
-        for step in (signs, sums):
-            for b, gg in ((6, 0), (6, 1), (5, 0), (5, 1)):
-                if b >= NV[gg]:
-                    step(b, gg)
-        signed(sum(NV), 14)
+        for b in (9, 8):
+            compare_a([(b, 0), (b, 1)])
+        for pair in low[3:]:
+            compare_v(*pair)
+        for pair in low:
+            sums_v(*pair)
         if rd == 0:
-            t_early()
-            consts_order_a()
-        for b in range(2, max(NV)):
-            compare_v(b)
-        later = [(b, d) for d in range(4) for b in (2, 3)]
-
-        def t_late(k, bank):
-            t_out(*later[k], bank)
-            if k % 2:
-                by_dma(k // 2 + 4, k // 2, 4, 640)
-
-        add_ranks(0)
-        if rd > 0:
-            t_product(*later[0], 6)
-            t_product(*later[1], 7)
-        add_ranks(3)
-        signed_high()
-        add_ranks(4)
-        spread(7, 10)
+            affine(A("cst", 0, 512), A("zt", 0, 512), 1.0, col(17))
+            consts_order()
+        t_products((0, 1, 2))
         add_ranks(1)
+        last = A("rs", 3 * 192 - 1, 192 * sum(NV), 192)
+        copy(A("aw", 4, 2 * sum(NV), 2), last)
+        ts(A("aw", 5, 2 * sum(NV), 2), last, -1.0, None, Op.mult)
+        ts(A("aw", 25, 32, 2), A("aw", 24, 32, 2), -1.0, None, Op.mult)
+        add_ranks(2)
+        bounds(0, 8)
+        t_products((4, 5))
+        t_outs("aaaaaaa")
+        add_ranks(3)
+        add_ranks(4)
+        ts(A("aw", 33, 40, 2), A("aw", 32, 40, 2), -1.0, None, Op.mult)
+        add_ranks(0, True)
+        bounds(8, 10)
+        turn32(A("thr", 0, 256), A("sp", 0, 256))
+        turn32(A("thr", 256, C), A("sp", 256, C))
         if rd == 0:
-            spread(0, 7)
-            add_ranks(2, True)
-            mirror(0, 10)
-            quant("kc", 0, 256, "cst", 0)
-        else:
-            add_ranks(2, True)
-            spread(min(NV), 7)
-            mirror(7, 10)
-            mirror(min(NV), 7)
-        for a, b in ((224, C), (0, 224)) if rd > 0 else ((0, C),):
-            tt(A("fs", 16 + a, 16 + b), P(3, b, a), A("thr", a, b), Op.is_lt)
-        if rd == 0:
-            quant("kc", 256, 256, "cst", 1024)
-            for k in range(4):
-                t_product(*later[k], 4 + k)
-                t_late(k, 4 + k)
-            affine(A("pl", 0, 20), A("pl", 0, 20), 1.0, col(23))
-        else:
-            t_late(0, 6)
-            t_late(1, 7)
-            for k in (2, 3):
-                t_product(*later[k], 2 + k)
-                t_late(k, 2 + k)
-            t_product(*later[4], 6)
-            t_product(*later[5], 7)
+            quant("kc", 0, 512, "cst", 0)
+        tt(A("fs", 16, 16 + C), P(3, C), A("thr", 0, C), Op.is_lt)
+        t_products((6, 7))
+        once(2)
         quant("fq", 0, 132, "fs", 0)
-        mm(2, "kc", 384, "fq", 4, 128)
-        mm(0, "kc", 0, "fq", 4, 128, True, False)
-        mm(0, "kc", 128, "fq", 0, 128, False, True)
-        mm(1, "kc", 256, "fq", 4, 128)
+        t_outs("av" if rd else "aa")
+        if rd == 0:
+            consts_places()
+        mm(0, "kc", 128, "fq", 4, 128, True, False)
+        mm(0, "kc", 256, "fq", 0, 128, False, True)
+        mm(1, "kc", 384, "fq", 4, 128)
+        mm(2, "kc", 0, "fq", 4, 128)
         if rd == 0:
             quant("kc", 512, 512, "cst", 2048)
-        mm(4, "kc", 512, "fq", 4, 128)
-        mm(5, "kc", 640, "fq", 4, 128)
-        mm(3, "kc", 768, "fq", 4, 128)
-        if rd > 0:
-            t_late(4, 6)
-        scan(A("st", 8, 88), P(2, 80), A("z80", 0, 80), 0.0, Op.add, Op.add)
-        scan(A("su", 0, 80), P(0, 80), A("z80", 0, 80), 64.0 * 768, Op.add, Op.add)
+        for k, bank in enumerate((4, 5, 3)):
+            mm(bank, "kc", 512 + 128 * k, "fq", 4, 128)
+        scan(A("su", 0, 80), P(0, 80), A("zt", 0, 80), 64.0 * 768, Op.add, Op.add)
         mm(0, "kc", 896, "fq", 4, 128)
         scan(A("sg", 0, 80), A("smk", 0, 80), P(1, 80), 0.0, Op.mult, Op.add)
-        ts(A("r0", 0, 80), A("st", 7, 87), col(38), col(38), Op.add, Op.subtract)
-        if rd > 0:
-            t_late(5, 7)
-        for k in range(6 if rd > 0 else 4, 8):
-            t_product(*later[k], (2, 6, 7)[k % 3])
-            t_late(k, (2, 6, 7)[k % 3])
+        scan(A("st", 8, 88), P(2, 80), A("zt", 0, 80), 0.0, Op.add, Op.add)
+        for bank in ((6, 1, 7, 2) * 3)[:len(turns)]:
+            t_products((bank,))
+            t_outs("a")
         if rd == 0:
-            consts_places_a()
+            dma("s", T.wq[:, :].bitcast(dt.uint8), T.wc[:, :], [A("wq", 0, 512)], [])
+            dma("s", T.wqs[:, :], T.ws[:, :], [A("wqs", 0, 512)], [])
+        if rd == 1:
+            dma("s", T.vt[:, :], T.v[:, :], [A("vt", 0, 512)], [])
         num, sign = L(0), A("sg", 3, 80, 4)
-        tt(A("n2f", 0, 20), A("su", 3, 80, 4), sign, Op.mult)
-        ts(A("r1", 0, 80), A("st", 7, 87), col(36), col(36), Op.add, Op.subtract)
-        tt(num, A("n2f", 0, 20), A("pl", 0, 20), Op.add)
-        tt(A("dg", 0, 80), A("r1", 0, 80), A("r0", 0, 80), Op.subtract)
-        ts(L(1), num, 6, 7 * 512, Op.arith_shift_right, Op.bitwise_and)
-        ts(L(2), num, 13, 3, Op.arith_shift_right, Op.bitwise_and)
-        ts(L(3), num, 7 * 64, None, Op.bitwise_and)
-        ts(L(4), num, 7, 15 * 4, Op.arith_shift_right, Op.bitwise_and)
-        tt(L(5), L(1), L(2), Op.add)
-        tt(A("dat", 0, 320, 4), P(4, 80), A("dg", 0, 80), Op.add)
-        tt(L(6), L(3), L(4), Op.add)
-        tt(A("dat", 1, 320, 4), P(5, 80), A("dg", 0, 80), Op.add)
-        tt(L(9), L(5), L(6), Op.add)
-        tt(A("dat", 2, 320, 4), P(3, 80), A("dg", 0, 80), Op.add)
-        copy(A("pos", 0, 20), L(9))
-        tt(A("dat", 3, 320, 4), P(0, 80), A("dg", 0, 80), Op.add)
-        slots, lst = A("wn", 0, 3072), A("pos", 0, 20)
         steps = [lambda: ts(L(16), num, col(27), None, Op.add),
                  lambda: ts(L(13), num, 9, None, Op.arith_shift_right),
-                 lambda: ts(LF(0), sign, -736.0, 544.0, Op.mult, Op.add),
                  lambda: ts(L(17), L(16), 6, 7, Op.arith_shift_right, Op.bitwise_and),
                  lambda: tt(LF(1), LF(0), L(13), Op.add),
                  lambda: ts(LF(2), L(17), 160.0, None, Op.mult),
                  lambda: tt(LF(3), LF(1), LF(2), Op.add),
                  lambda: copy(A("wl", 0, 20), LF(3))]
-        if rd == 0:
-            steps.append(lambda: quant("vq", 0, 128, "vt", 0))
         if rd == ROUNDS - 1:
-            steps += [lambda: ts(L(18), num, 6, None, Op.arith_shift_right),
-                      lambda: ts(LF(4), sign, -1408.0, -128.0, Op.mult, Op.add),
-                      lambda: tt(A("vf", 0, 20), L(18), LF(4), Op.add),
+            steps[2:2] = [lambda: ts(L(18), num, 6, None, Op.arith_shift_right),
+                          lambda: ts(LF(4), sign, -1408.0, -128.0, Op.mult, Op.add)]
+            steps += [lambda: tt(A("vf", 0, 20), L(18), LF(4), Op.add),
                       lambda: turn32(A("vtr", 0, 32), A("vf", 0, 32))]
 
         def meanwhile(k):
@@ -592,18 +555,40 @@ def rank_program(g, core, T, topo):
                 step()
             del steps[:k]
 
+        once(1)
+        tt(A("n2f", 0, 20), A("su", 3, 80, 4), sign, Op.mult)
+        ts(A("r1", 0, 80), A("st", 7, 87), col(36), col(38), Op.mult, Op.add)
+        ts(LF(0), sign, -736.0, 544.0, Op.mult, Op.add)
+        tt(num, A("n2f", 0, 20), A("pl", 0, 20), Op.add)
+        ts(A("dg", 0, 80), A("r1", 0, 80), 15 * 256, None, Op.bitwise_and)
+        ts(L(1), num, 6, 7 * 512, Op.arith_shift_right, Op.bitwise_and)
+        ts(L(2), num, 13, 3, Op.arith_shift_right, Op.bitwise_and)
+        ts(L(3), num, 7 * 64, None, Op.bitwise_and)
+        ts(L(4), num, 7, 15 * 4, Op.arith_shift_right, Op.bitwise_and)
+        tt(A("dat", 0, 320, 4), P(4, 80), A("dg", 0, 80), Op.add)
+        tt(L(5), L(1), L(2), Op.add)
+        tt(A("dat", 1, 320, 4), P(5, 80), A("dg", 0, 80), Op.add)
+        tt(L(6), L(3), L(4), Op.add)
+        tt(A("dat", 2, 320, 4), P(3, 80), A("dg", 0, 80), Op.add)
+        tt(A("dat", 3, 320, 4), P(0, 80), A("dg", 0, 80), Op.add)
+        meanwhile(1)
+        tt(L(9), L(5), L(6), Op.add)
+        meanwhile(1)
+        copy(A("pos", 0, 20), L(9))
+        meanwhile(2)
+        slots, lst = A("wn", 0, 3072), A("pos", 0, 20)
+
         def places(i, a, n):
             quant("nq", 384 * i + 128 * a, 128 * n, "wn", 1536 * i + 512 * a)
             for s in range(a, a + n):
-                mm(1 + 2 * i, "nq", 384 * i + 128 * s, "ki", 12 + 20 * i - 4 * s, 128, s == 0, s == 2)
+                mm(3 + i, "nq", 384 * i + 128 * s, "ki", 12 + 20 * i - 4 * s, 128, s == 0, s == 2)
 
         def half(s, i):
             return A(s[0], s[1] + 10 * i, s[1] + 10 * i + 10)
 
-        listing = [lambda i: tt(half(L(7), i), P(1 + 2 * i, 10), A("s2", 0, 10), Op.add),
+        listing = [lambda i: tt(half(L(7), i), P(3 + i, 10), A("s2", 10 * i, 10 * i + 10), Op.add),
                    lambda i: ts(half(L(8), i), half(L(7), i), 3, 7 * TURN + 511, Op.arith_shift_right, Op.bitwise_and),
                    lambda i: copy(A("off", 10 * i, 10 * i + 10), half(L(8), i))]
-        meanwhile(1)
         emit("v", lambda: g.vector.tensor_copy(ap(slots).indirect(ap(lst)), T.dat[:, 0:320]), [slots], [lst, A("dat", 0, 320)])
         if rd == 0:
             quant("ki", 0, 160, "cci", 0)
@@ -612,6 +597,7 @@ def rank_program(g, core, T, topo):
         places(0, 0, 2)
         places(0, 2, 1)
         places(1, 0, 2)
+        meanwhile(1)
         listing[0](0)
         places(1, 2, 1)
         listing[1](0)
@@ -626,25 +612,22 @@ def rank_program(g, core, T, topo):
         send(dst, "gq", "gl%d" % rd, "ga%d" % rd, "gs%d" % rd)
         for b in range(4):
             gather("avav"[b], A("ft", b, 640, 4), TW(b), A("off", 10, 20))
-        meanwhile(1)
         quant("fqq", 0, H, "ft", 0)
-        meanwhile(3)
+        if rd == 1:
+            quant("vq", 0, 128, "vt", 0)
         layer("fqq", "at", 0)
-
-        def unpack_a(ks, banks):
-            for k in ks:
-                b = [int(e) for e in B_PLAN if e.isdigit()][k // 4]
-                unpack("aq", b, k % 4, k % banks, A_OUT[k], 0)
-                if k % 4 == 3:
-                    halves("s", b, 0)
-
-        layer("gl%d" % rd, "bt", 4, lambda: quant("aq", 0, H, "at", 0))
+        quant("aq", 0, H, "at", 0)
+        layer("gl%d" % rd, "bt", 4)
         quant("bq", 0, H, "bt", 0)
         send(dst, "bq", "bl%d" % rd, "ba%d" % rd, "bs%d" % rd)
         if rd < ROUNDS - 1:
             iota(A("wn", 0, 3072), [[0, 3072]], 0, 0)
         meanwhile(len(steps))
-        unpack_a(range(16), 8)
+        for k in range(16):
+            b = ([int(e) for e in B_PLAN if e.isdigit()] + list(LAST))[k // 4]
+            unpack("aq", b, k % 4, k % 8, A_OUT[k], 0)
+            if k % 4 == 3:
+                halves("s", b, 0)
         k = bank = 0
         for q in B_PLAN:
             if q in "va":
@@ -654,19 +637,29 @@ def rank_program(g, core, T, topo):
                 halves("s", k // 8, 1)
                 k += 4
             else:
-                e = int(q)
-                for a, n in ((H, H), (0, H)) if q == B_PLAN[-1] else ((0, C),):
-                    gather_add(A("xn", 4 * a + e, 4 * (a + n), 4), A("wv", 2560 * e, 2560 * e + 2560), A("wl", a // 16, (a + n) // 16),
-                               A("wt", 320 * e + a, 320 * e + a + n))
+                splice(int(q), 0, C)
+        e, f = LAST
+        for a in (H, 0):
+            mm(6 + a // H, "er", 240 * f, "xq", a, H)
+            gather("a", A("sv", a, a + H), A("wv", 2560 * f, 2560 * f + 2560), A("wl", a // 16, (a + H) // 16))
+        splice(e, H, H)
+        tt(A("xn", 4 * H + f, 4 * C, 4), P(7, H), A("sv", H, C), Op.add)
+        splice(e, 0, H)
+        if rd < ROUNDS - 1:
+            turn_high("xn")
+        else:
+            quant("xq", H, H, "xn", 4 * H)
+            mm(1, "vq", 0, "xq", H, H)
+        tt(A("xn", f, 4 * H, 4), P(6, H), A("sv", 0, H), Op.add)
 
     dmas("s", [(T.op[k:k + 1, :], T.vtr[32 * (k // 2):32 * (k // 2) + 20, 16 * (k % 2):16 * (k % 2) + 16]) for k in range(8)], [], [A("vtr", 0, 32)])
-    for a in (H, 0):
-        quant("xq", a, H, "xn", 4 * a)
-        mm(a // H, "vq", 0, "xq", a, H)
-    dma("s", T.oc[:, :], T.xq[:, 0:C].bitcast(dt.uint8), [], [A("xq", 0, C)])
+    dma("s", T.oc[:, 4 * H:4 * C], T.xq[:, H:C].bitcast(dt.uint8), [], [A("xq", H, C)])
     act(A("yo", H, C), P(1, H), Fn.Copy)
-    copy(A("yo", 0, H), P(0, H))
     dma("a", T.y[:, H:C], T.yo[:, H:C], [], [A("yo", H, C)])
+    quant("xq", 0, H, "xn", 0)
+    mm(0, "vq", 0, "xq", 0, H)
+    dma("s", T.oc[:, 0:4 * H], T.xq[:, 0:H].bitcast(dt.uint8), [], [A("xq", 0, H)])
+    copy(A("yo", 0, H), P(0, H))
     for k in range(4):
         dma("sa"[k % 2], T.osc[4 * k:4 * k + 4, :], T.xqs[32 * k:32 * k + 4, 0:C], [], [A("xqs", 0, C)])
     dma("s", T.y[:, 0:H], T.yo[:, 0:H], [], [A("yo", 0, H)])

import math
from concourse.mybir import dt, AluOpType as Op, ActivationFunctionType as Fn

C, H, ROUNDS = 320, 160, 3
MASK = [1, 2, 3]
U8, F8, BF, F32, I32, U16 = "uint8", "float8_e4m3fn_x4", "bfloat16", "float32", "int32", "uint16"
NV = (6, 6)
T_TURNS = {0: (4, 5), 1: (6, 7), 2: (), 3: ()}
TURN = 2048
FAR = 2.0 ** 90
A_OUT = "aavaavav" + "avavavav"
B_PLAN = "vava>" + "vava>" + "vavavava" + "vav2aa0aaa"
LAST = (3, 1)

WIDTH = [max(32 * b, 128) for b in (9, 7, 5, 3, 1)]

SCRATCH = {}


def _sb(name, cols, dtype):
    SCRATCH[name] = ("sbuf", [128, cols], dtype)


def _mx(name, cols):
    _sb(name, cols, F8)
    _sb(name + "s", cols, U8)


for _k in range(8):
    SCRATCH["ps%d" % _k] = ("psum", [128, 512], F32)
for _n, _w in (("xin", 1280), ("xn", 1280), ("ut", 512), ("vt", 512), ("ones", 128), ("zt", 512), ("zs", 1152), ("cd", 1280),
               ("fs", 528), ("dat", 320), ("wn", 3072), ("wt", 7 * TURN + 1280), ("wv", 10240), ("gt", 640), ("ft", 640), ("at", 640),
               ("bt", 640), ("tri", 320), ("row", 160), ("est", 520), ("cst", 4096), ("cc1", 512), ("cci", 640), ("om", 512),
               ("j32", 160), ("jq", 160), ("smk", 80), ("sgn", 64), ("jg", 64), ("dd", 640), ("sv", 320), ("rs", 192 * sum(NV))):
    _sb(_n, _w, BF)
_mx("cdq", 320)
for _k, _w in enumerate(WIDTH):
    _sb("ct%d" % _k, 4 * _w, BF)
    _mx("cq%d" % _k, _w)
for _n, _w in (("pt", 640), ("aw", 40), ("sp", 320), ("thr", 320), ("su", 80), ("sg", 80), ("st", 96),
               ("n2f", 32), ("vf", 32), ("vtr", 32), ("sc", 40), ("pl", 20), ("s2", 20), ("yo", 320), ("lf", 200)):
    _sb(_n, _w, F32)
for _n, _w in (("pi", 16), ("lui", 40), ("li", 400), ("r1", 80), ("dg", 80)):
    _sb(_n, _w, I32)
for _n, _w in (("lu", 16), ("lt", 20), ("pos", 32), ("off", 32), ("wl", 32)):
    _sb(_n, _w, U16)
for _n, _w in (("xq", 320), ("uq", 128), ("us", 256), ("vq", 128), ("wq", 512), ("er", 960), ("kc", 1024), ("k1", 128),
               ("ki", 160), ("fq", 132), ("nq", 768), ("gq", H), ("fqq", H), ("aq", H), ("bq", H)):
    _mx(_n, _w)
for _k in range(ROUNDS):
    _mx("gl%d" % _k, H)
    _mx("bl%d" % _k, H)

SEMAPHORES = ["ev", "ea", "et", "ep"] + ["d%d" % _k for _k in range(130)]
for _k in range(ROUNDS):
    SEMAPHORES += ["ga%d" % _k, "ba%d" % _k, "gs%d" % _k, "bs%d" % _k]


def rank_program(g, core, T, topo):
    rank = T.rank_of(core)
    if rank is None:
        return
    queue = {"v": g.vector, "a": g.scalar, "t": g.tensor, "p": g, "s": g.sync}
    known = {q: {} for q in queue}
    count, snaps, log, ndma, final = {}, {}, {}, [0], {}

    def A(name, a, b, step=1):
        return (name, a, b, step)

    def ap(s):
        return T[s[0]][:, s[1]:s[2]] if s[3] == 1 else T[s[0]][:, s[1]:s[2]:s[3]]

    def hit(x, y):
        return x[1] < y[2] and y[1] < x[2] and (x[1] - y[1]) % math.gcd(x[3], y[3]) == 0

    def need(q, tokens):
        for tok in sorted(set(tokens), key=lambda k: (k[0], -k[1])):
            if known[q].get(tok[0], 0) < tok[1]:
                queue[q].wait_ge(T.sem[tok[0]], tok[1])
                known[q][tok[0]] = tok[1]
                for s, n in snaps[tok].items():
                    known[q][s] = max(known[q].get(s, 0), n)

    def note(s, w, q, token, loose=False):
        keep = []
        for r in log.get(s[0], []):
            x = r[0]
            inside = s[1] <= x[1] and x[2] <= s[2] and (s[3] == 1 or (s[3] == x[3] and (s[1] - x[1]) % s[3] == 0))
            if loose or not (inside and (w or (r[2] == q and not r[1]))):
                keep.append(r)
        keep.append((s, w, q, token))
        log[s[0]] = keep

    def emit(q, fn, outs, ins, token=None, acc=False):
        tokens = []
        for lst, w in ((ins, False), (outs, True)):
            for s in lst:
                bank = s[0][:2] == "ps"
                for r in log.get(s[0], ()):
                    if bank:
                        if not (r[2] == q and (acc or not (w or r[1]))):
                            tokens.append(r[3])
                    elif (w or r[1]) and hit(s, r[0]):
                        tokens.append(r[3])
        need(q, tokens)
        inst = fn()
        if token is None:
            name = "e" + q
            count[name] = count.get(name, 0) + 1
            token = (name, count[name])
            inst.then_inc(T.sem[name], 1)
        final[token[0]] = token[1]
        snaps[token] = dict(known[q])
        for s in ins:
            note(s, False, q, token, q == "s")
        for s in outs:
            note(s, True, q, token)

    def dmas(q, sides, outs, ins):
        tok = ("d%d" % ndma[0], 16 * len(sides))
        ndma[0] += 1
        emit(q, lambda: [queue[q].dma_start(o, i).then_inc(T.sem[tok[0]], 16) for o, i in sides], outs, ins, tok)

    def dma(q, out_ap, in_ap, outs, ins):
        dmas(q, [(out_ap, in_ap)], outs, ins)

    def memset(s, c):
        emit("v", lambda: g.vector.memset(ap(s), c), [s], [])

    def copy(o, i):
        emit("v", lambda: g.vector.tensor_copy(ap(o), ap(i)), [o], [i])

    def turn32(o, i):
        emit("v", lambda: g.vector.transpose(ap(o), ap(i)), [o], [i])

    def tt(o, a, b, op):
        emit("v", lambda: g.vector.tensor_tensor(ap(o), ap(a), ap(b), op), [o], [a, b])

    def ts(o, a, c1, c2, op0, op1=None):
        ins = [a] + [c for c in (c1, c2) if isinstance(c, tuple)]
        x1 = ap(c1) if isinstance(c1, tuple) else c1
        x2 = ap(c2) if isinstance(c2, tuple) else c2
        if op1 is None:
            emit("v", lambda: g.vector.tensor_scalar(ap(o), ap(a), x1, None, op0), [o], ins)
        else:
            emit("v", lambda: g.vector.tensor_scalar(ap(o), ap(a), x1, x2, op0, op1), [o], ins)

    def scan(o, a, b, init, op0, op1):
        emit("v", lambda: g.vector.tensor_tensor_scan(ap(o), ap(a), ap(b), init, op0, op1), [o], [a, b])

    def act(o, i, fn, bias=None, scale=1.0, total=None):
        kw = {"scale": ap(scale) if isinstance(scale, tuple) else scale}
        if bias is not None:
            kw["bias"] = ap(bias) if isinstance(bias, tuple) else bias
        if total is not None:
            kw["accum_out"] = ap(total)
        emit("a", lambda: g.scalar.activation(ap(o), ap(i), fn, **kw), [o] + ([total] if total else []),
             [i] + [c for c in (bias, scale) if isinstance(c, tuple)])

    def quant(o, c, n, i, c2):
        src = A(i, c2, c2 + 4 * n)
        emit("v", lambda: g.vector.quantize_mx(T[o][:, c:c + n], T[o + "s"][:, c:c + n], ap(src)), [A(o, c, c + n), A(o + "s", c, c + n)], [src])

    def mm(bank, w, wc, x, xc, n, start=True, stop=True):
        o = A("ps%d" % bank, 0, 512)
        emit("t", lambda: g.tensor.matmul_mx(T["ps%d" % bank][:, 0:n], T[w][:, wc:wc + 128], T[w + "s"][:, wc:wc + 128],
                                             T[x][:, xc:xc + n], T[x + "s"][:, xc:xc + n], start, stop),
             [o], [A(w, wc, wc + 128), A(w + "s", wc, wc + 128), A(x, xc, xc + n), A(x + "s", xc, xc + n)], acc=not start)

    def P(bank, n, a=0):
        return A("ps%d" % bank, a, n)

    def take(q, o, i):
        if q == "v":
            copy(o, i)
        else:
            act(o, i, Fn.Copy)

    def gather(q, o, win, lst):
        if q == "v":
            emit("v", lambda: g.vector.tensor_copy(ap(o), ap(win).indirect(ap(lst))), [o], [win, lst])
        else:
            emit("a", lambda: g.scalar.activation(ap(o), ap(win).indirect(ap(lst)), Fn.Copy), [o], [win, lst])

    def gather_add(o, win, lst, more, op=Op.add):
        emit("v", lambda: g.vector.tensor_tensor(ap(o), ap(win).indirect(ap(lst)), ap(more), op), [o], [win, lst, more])

    def send(dst, src, land, sem, done):
        rid, pid, _ = topo.addr(dst)
        eng = topo.engines(core, dst)
        total, mask = 2 * len(eng), topo.mask(core, dst)
        need("p", [r[3] for nm in (src, src + "s") for r in log[nm] if r[1]])
        g.remote_dma(T[land][:, 0:H].bitcast(dt.uint8), T[src][:, 0:H].bitcast(dt.uint8), T.sem[sem], T.sem[done], pid, rid, mask)
        g.remote_dma(T[land + "s"][:, 0:H], T[src + "s"][:, 0:H], T.sem[sem], T.sem[done], pid, rid, mask)
        tok, arr = (done, total), (sem, total)
        snaps[tok], snaps[arr] = dict(known["p"]), {}
        final[done], final[sem] = total, total
        for nm in (src, src + "s"):
            note(A(nm, 0, H), False, "p", tok)
        for nm in (land, land + "s"):
            log[nm] = [(A(nm, 0, H), True, "r", arr)]

    def iota(o, pattern, base, cm):
        if o[0] in ("pi", "lui"):
            emit("p", lambda: g.iota(ap(o), pattern, base, cm), [o], [])
        else:
            emit("p", lambda: g.iota(ap(o), pattern, base, cm, allow_small_or_imprecise_dtypes=True), [o], [])

    def select(o, i, pattern, cmp, base, cm):
        emit("p", lambda: g.affine_select(ap(o), ap(i), pattern, cmp, 0.0, base, cm), [o], [i])

    def pcol(k):
        return A("pi", k, k + 1)

    def col(k):
        return A("sc", k, k + 1)

    def fill(s, c):
        act(s, A("ones", 0, len(range(s[1], s[2], s[3]))), Fn.Copy, scale=c)

    def affine(o, i, scale, bias):
        act(o, i, Fn.Identity, bias=bias, scale=scale)

    dma("s", T.ut[:, :], T.u[:, :], [A("ut", 0, 512)], [])
    dma("s", T.xin[:, 640:1280], T.x[:, 640:1280], [A("xin", 640, 1280)], [])
    dma("s", T.xin[:, 0:640], T.x[:, 0:640], [A("xin", 0, 640)], [])

    memset(A("est", 0, 520), 0.0)
    memset(A("ones", 0, 128), 1.0)
    memset(A("zt", 0, 512), 0.0)
    for o, a, b in (("cc1", 0, 512), ("ct2", 512, 640), ("ct1", 768, 896), ("ct0", 1024, 1152)):
        act(A(o, a, b), A("zt", 0, b - a), Fn.Copy)
    iota(A("pi", 0, 1), [[0, 1]], 0, 8)
    iota(A("lui", 0, 16), [[16, 2], [32, 4], [0, 2]], 0, 0)
    select(A("est", 3, 515, 4), A("ones", 0, 128), [[-1, 128]], Op.is_equal, 0, 1)
    for k, (shift, keep) in enumerate(((3, 15), (2, 62), (7, 7), (7, 6), (3, 1), (4, 1), (5, 2), (0, 96), (3, 7))):
        ts(pcol(k + 1), pcol(0), shift, keep, Op.arith_shift_right, Op.bitwise_and)
    copy(A("lu", 0, 16), A("lui", 0, 16))
    quant("er", 0, 128, "est", 3)
    copy(A("sc", 0, 10), A("pi", 0, 10))
    iota(A("jg", 0, 64), [[-1, 2], [1, 8], [0, 4]], 0, 0)
    iota(A("j32", 0, 160), [[0, 5], [2, 32]], 1, 0)
    iota(A("jq", 0, 160), [[0, 20], [32, 4], [0, 2]], 0, 0)
    iota(A("lui", 24, 26), [[5, 2]], 0, 0)
    iota(A("lui", 16, 24), [[8, 4], [5, 2]], 0, 0)
    iota(A("om", 0, 512), [[1, 8], [8, 16], [-8, 4]], 0, 0)
    iota(A("sp", 1, 320, 2), [[0, 160]], -4096, 0)

    affine(col(17), col(6), -2.0, 1.0)
    affine(col(19), col(6), -64.0, 32.0)
    affine(col(13), col(8), 1.0, col(3))
    affine(col(23), col(3), 32.0 - 4096, 0.0)
    fill(A("sgn", 0, 32), col(17))
    for b in range(1, 3):
        quant("er", 240 * b, 128, "est", 3 - b)
    quant("uq", 0, 128, "ut", 0)
    for e in range(2):
        for s in range(2):
            ts(A("cc1", 8 * s + e, 512, 16), A("jg", 32 * e, 32 * e + 32), col(4), 2.0 * s - 1, Op.is_equal, Op.mult)

    def zeros(*runs):
        for o, a, b in runs:
            dmas("s", [(T[o][:, w:min(w + 512, b)], T.zt[:, 0:min(512, b - w)]) for w in range(a, b, 512)], [A(o, a, b)], [A("zt", 0, 512)])

    zeros(("ct3", 256, 512), ("ct4", 0, 512), ("cst", 1536, 4096))

    def later_dmas():
        for a in range(0, 960, 240):
            dma("s", T.er[:, a + 128:a + 240].bitcast(dt.uint8), T.er[:, a:a + 112].bitcast(dt.uint8), [A("er", a + 128, a + 240)], [A("er", a, a + 112)])
            dma("s", T.ers[:, a + 128:a + 240], T.ers[:, a:a + 112], [A("ers", a + 128, a + 240)], [A("ers", a, a + 112)])
        zeros(("fs", 0, 16), ("fs", 336, 528), ("cci", 0, 640), ("wn", 0, 3072))

    def scoring(gg):
        a, lst = 128 * gg, A("lu", 8 * gg, 8 * gg + 8)
        emit("a", lambda: g.scalar.activation(T.uss[:, a:a + 128], T.uqs[:, 0:128].indirect(ap(lst)), Fn.Copy),
             [A("uss", a, a + 128)], [A("uqs", 0, 128), lst])
        emit("v", lambda: g.vector.tensor_copy(T.us[:, a:a + 128].bitcast(dt.uint32), T.uq[:, 0:128].bitcast(dt.uint32).indirect(ap(lst))),
             [A("us", a, a + 128)], [A("uq", 0, 128), lst])

    scoring(0)
    select(A("smk", 0, 80), A("ones", 0, 80), [[0, 20], [1, 4]], Op.is_gt, 0, 0)
    iota(A("pl", 0, 20), [[4096, 20]], 64 * 768, 256)
    iota(A("s2", 0, 20), [[2560, 2], [256, 10]], 64 * 16384 - 1280, 16)
    for gg in range(2):
        iota(A("aw", 2 * gg, 2 * gg + 2), [[64 - 64 * NV[gg], 2]], 32 * NV[gg] - 32, 0)
    iota(A("vf", 20, 32), [[0, 12]], 0, 0)
    iota(A("st", 0, 8), [[0, 8]], 0, 0)
    select(A("sgn", 32, 64), A("sgn", 0, 32), [[16, 8], [4, 4]], Op.is_ge, 3, -1)
    for e in range(4):
        select(A("cst", 1536 + 5 * e, 2048, 16), A("sgn", 32, 64), [[-16, 8], [-4, 4]], Op.is_ge, 0, 1)
    for b in range(4):
        for e in range(b + 1):
            select(A("cst", 2048 + 512 * b + 4 * (3 + e // 2) + e, 2048 + 512 * b + 512, 32), A("sgn", 0, 16), [[16, 8], [0, 2]], Op.is_gt,
                   0 if e == b else 128, -1)

    def consts_ranks():
        act(A("row", 0, 160), A("j32", 0, 160), Fn.Sign, bias=col(2), scale=-1.0)
        affine(col(26), col(8), -FAR, 0.0)
        affine(col(14), col(2), 1.0, -31.0)
        affine(col(24), col(2), -1.0, 31.0)
        for a in (0, H):
            affine(A("tri", a, a + H), A("row", 0, 160), 1.0, -1.0)

    def consts_signs():
        for e in range(2):
            act(A("cc1", 2 + e, 512, 4), A("cc1", e, 512, 4), Fn.Copy, scale=-1.0)
        act(A("row", 0, 160), A("jq", 0, 160), Fn.Abs, bias=col(26), scale=FAR)

    def consts_flags():
        ts(A("lt", 0, 10, 2), A("lui", 16, 26, 2), col(7), col(5), Op.add, Op.add)
        ts(A("lt", 1, 10, 2), A("lui", 17, 26, 2), col(7), col(5), Op.add, Op.subtract)
        affine(A("row", 0, 160, 2), A("row", 0, 160, 2), 1.0, col(24))
        affine(A("row", 1, 160, 2), A("row", 1, 160, 2), 1.0, col(14))

    def consts_order():
        ts(A("cst", 512, 1024), A("om", 0, 512), col(13), col(19), Op.is_gt, Op.mult)
        affine(A("cst", 1024, 1536), A("cst", 512, 1024), -1.0, col(19))

    small = [lambda: ts(col(30), col(1), 1.0, 16.0, Op.is_equal, Op.mult),
             lambda: ts(col(31), col(9), 2.0, 256.0, Op.is_equal, Op.mult),
             lambda: ts(col(33), col(1), 0.0, col(30), Op.is_equal, Op.add),
             lambda: ts(col(36), col(33), col(31), None, Op.add),
             lambda: ts(A("pl", 0, 20), A("pl", 0, 20), col(23), None, Op.add),
             lambda: ts(col(38), col(36), 1280.0, None, Op.mult)]

    def once(k):
        for step in small[:k]:
            step()
        del small[:k]

    def consts_places():
        affine(col(21), col(7), 16383.0 / 2, 1.0)
        affine(col(12), col(30), -15.0 / 256, 1.0)
        affine(col(25), col(3), 16386.0 - 256, 0.0)
        affine(col(27), col(3), -64.0, 512.0)
        affine(col(15), col(31), -255.0 / 65536, col(12))
        affine(A("s2", 0, 20), A("s2", 0, 20), 1.0, col(25))
        affine(col(22), col(15), col(21), 0.0)
        affine(col(34), col(22), -1.0, 0.0)
        fill(A("cci", 48, 64, 5), col(22))
        fill(A("cci", 128, 144, 5), col(34))

    def unpack(pair, b, d, bank, q, i):
        mm(bank, "er", 240 * b + 16 * d, pair, 0, H)
        k = 2560 * b + 1280 * i + 160 * d
        take(q, A("wv", k, k + H), P(bank, H))

    def splice(e, a, n):
        gather_add(A("xn", 4 * a + e, 4 * (a + n), 4), A("wv", 2560 * e, 2560 * e + 2560), A("wl", a // 16, (a + n) // 16),
                   A("wt", 320 * e + a, 320 * e + a + n))

    def halves(q, b, i):
        k = 2560 * b + 1280 * i
        o, src = A("wv", k + 640, k + 1280), A("wv", k, k + 640)
        dmas(q, [(T.wv[to:to + 64, k + 640:k + 1280], T.wv[fr:fr + 64, k:k + 640]) for to, fr in ((0, 64), (64, 0))], [o], [src])

    def t_copy(to, fr):
        o, i, d = A("wt", TURN * to, TURN * to + 1280), A("wt", TURN * fr, TURN * fr + 1280), 16 * ((to - fr) % 8)
        dmas("s", [(T.wt[0:128 - d, o[1]:o[2]], T.wt[d:128, i[1]:i[2]]), (T.wt[128 - d:128, o[1]:o[2]], T.wt[0:d, i[1]:i[2]])], [o], [i])

    def layer(pair, tile, bank):
        for b in range(4):
            mm(bank + b, "wq", 128 * b, pair, 0, H)
        for b in range(4):
            o = A(tile, b, 4 * H, 4)
            if b % 2 == 1:
                ts(o, P(bank + b, H), 0.0, 0.03125, Op.max, Op.mult)
            else:
                act(o, P(bank + b, H), Fn.Relu, scale=0.03125)

    def L(k):
        return A("li", 20 * k, 20 * k + 20)

    def LF(k):
        return A("lf", 20 * k, 20 * k + 20)

    def TW(b):
        return A("wt", 320 * b, 320 * b + 7 * TURN + 320)

    def own(gg, b):
        return A("pt", 320 * gg + 32 * b, 320 * gg + 32 * b + 1)

    def t_product(b, d, bank):
        mm(bank, "er", 240 * b + 16 * d, "xq", 0, C)

    def t_out(b, d, bank, q="a"):
        take(q, A("wt", TURN * d + 320 * b, TURN * d + 320 * b + 320), P(bank, C))

    def lane(b, gg):
        return A("ct%d" % ((9 - b) // 2), 2 * ((9 - b) % 2) + gg, 128 * b, 4)

    def sense(b):
        return -1.0 if b % 2 else 1.0

    def compare_v(b, gg):
        ts(lane(b, gg), P(1 + gg, 32 * b), own(gg, b), 2.0 * sense(b), Op.is_lt, Op.mult)

    def sums_v(b, gg):
        end = 192 * (2 * b + gg + 1)
        scan(A("rs", end - 32 * b, end), lane(b, gg), A("zt", 0, 32 * b), (32.0 * NV[gg] - 32 - 64 * b) * sense(b), Op.add, Op.add)

    def zs(b, gg):
        return A("zs", 288 * (2 * (b % 2) + gg), 288 * (2 * (b % 2) + gg) + 32 * b)

    def signs(b, gg):
        act(zs(b, gg), P(4 + gg, 32 * b), Fn.Sign, bias=own(gg, b), scale=-1.0)

    def sums(b, gg):
        act(lane(b, gg), zs(b, gg), Fn.Sign, bias=-0.5 * sense(b), scale=sense(b), total=A("aw", 4 * b + 2 * gg, 4 * b + 2 * gg + 1))

    def compare_a(pairs):
        for step in (signs, sums):
            for b, gg in pairs:
                step(b, gg)

    def add_ranks(k, stop=False):
        n = WIDTH[k]
        quant("cq%d" % k, 0, n, "ct%d" % k, 0)
        mm(3, "k1", 0, "cq%d" % k, 0, n, start=False, stop=stop)

    def bounds(a, b):
        gather_add(A("sp", 32 * a, 32 * b, 2), A("aw", 4 * a, 4 * b), A("lt", a, b), A("row", 16 * a, 16 * b), Op.subtract)

    def turn_high(tile):
        quant("xq", H, H, tile, 4 * H)
        mm(3, "us", 0, "xq", H, H)
        if tile == "xin":
            scoring(1)
        mm(0, "us", 128, "xq", H, H)

    for rd in range(ROUNDS):
        dst = T.cores[rank ^ MASK[rd]]
        if rd == 0:
            turn_high("xin")
        quant("xq", 0, H, "xin" if rd == 0 else "xn", 0)
        mm(1, "us", 0, "xq", 0, max(H, 32 * NV[0] - 32))
        mm(4, "us", 0, "xq", 0, 288)
        mm(2, "us", 128, "xq", 0, max(H, 32 * NV[1] - 32))
        mm(5, "us", 128, "xq", 0, 288)
        turns, ahead = [(b, d) for d in T_TURNS for b in range(4)], []

        def t_products(banks):
            for bank in banks:
                t_product(*turns[0], bank)
                ahead.append(turns.pop(0) + (bank,))

        def t_outs(qs):
            for q in qs:
                b, d, bank = ahead.pop(0)
                t_out(b, d, bank, q)
                for to in T_TURNS[d] if b == 3 else ():
                    t_copy(to, d)

        t_products((6, 7))
        if rd == 0:
            quant("er", 720, 128, "est", 0)
            later_dmas()
            consts_ranks()
        for a, banks in ((H, (3, 0)), (0, (1, 2))):
            for gg in range(2):
                turn32(A("pt", 320 * gg + a, 320 * gg + a + H), P(banks[gg], H))
            once(1)
            for gg in range(2):
                tt(A("dd", 320 * gg + a, 320 * gg + a + H), P(banks[gg], H), A("pt", 320 * gg + a, 320 * gg + a + H), Op.is_le)
        compare_a([(7, 0), (6, 0)])
        if rd == 0:
            consts_signs()
        for gg in range(2):
            scan(A("cd", gg, 1280, 4), A("dd", 320 * gg, 320 * gg + 320), A("tri", 0, 320), 0.0, Op.max, Op.mult)
        once(1)
        low = [(b, gg) for b in range(max(NV) - 1, 0, -1) for gg in range(2) if b < NV[gg]]
        compare_v(*low[0])
        for gg in range(2):
            turn32(A("cd", 2 + gg, 1280, 4), A("cd", gg, 1280, 4))
        compare_v(*low[1])
        compare_v(*low[2])
        quant("cdq", 0, C, "cd", 0)
        if rd == 0:
            quant("k1", 0, 128, "cc1", 0)
        mm(3, "k1", 0, "cdq", 0, C, start=True, stop=False)
        compare_a([(7, 1), (6, 1)])
        if rd == 0:
            consts_flags()
        for b in (9, 8):
            compare_a([(b, 0), (b, 1)])
        for pair in low[3:]:
            compare_v(*pair)
        for pair in low:
            sums_v(*pair)
        if rd == 0:
            affine(A("cst", 0, 512), A("zt", 0, 512), 1.0, col(17))
            consts_order()
        t_products((0, 1, 2))
        add_ranks(1)
        last = A("rs", 3 * 192 - 1, 192 * sum(NV), 192)
        copy(A("aw", 4, 2 * sum(NV), 2), last)
        ts(A("aw", 5, 2 * sum(NV), 2), last, -1.0, None, Op.mult)
        ts(A("aw", 25, 32, 2), A("aw", 24, 32, 2), -1.0, None, Op.mult)
        add_ranks(2)
        bounds(0, 8)
        t_products((4, 5))
        t_outs("aaaaaaa")
        add_ranks(3)
        add_ranks(4)
        ts(A("aw", 33, 40, 2), A("aw", 32, 40, 2), -1.0, None, Op.mult)
        add_ranks(0, True)
        bounds(8, 10)
        turn32(A("thr", 0, 256), A("sp", 0, 256))
        turn32(A("thr", 256, C), A("sp", 256, C))
        if rd == 0:
            quant("kc", 0, 512, "cst", 0)
        tt(A("fs", 16, 16 + C), P(3, C), A("thr", 0, C), Op.is_lt)
        t_products((6, 7))
        once(2)
        quant("fq", 0, 132, "fs", 0)
        t_outs("av" if rd else "aa")
        if rd == 0:
            consts_places()
        mm(0, "kc", 128, "fq", 4, 128, True, False)
        mm(0, "kc", 256, "fq", 0, 128, False, True)
        mm(1, "kc", 384, "fq", 4, 128)
        mm(2, "kc", 0, "fq", 4, 128)
        if rd == 0:
            quant("kc", 512, 512, "cst", 2048)
        for k, bank in enumerate((4, 5, 3)):
            mm(bank, "kc", 512 + 128 * k, "fq", 4, 128)
        scan(A("su", 0, 80), P(0, 80), A("zt", 0, 80), 64.0 * 768, Op.add, Op.add)
        mm(0, "kc", 896, "fq", 4, 128)
        scan(A("sg", 0, 80), A("smk", 0, 80), P(1, 80), 0.0, Op.mult, Op.add)
        scan(A("st", 8, 88), P(2, 80), A("zt", 0, 80), 0.0, Op.add, Op.add)
        for bank in ((6, 1, 7, 2) * 3)[:len(turns)]:
            t_products((bank,))
            t_outs("a")
        if rd == 0:
            dma("s", T.wq[:, :].bitcast(dt.uint8), T.wc[:, :], [A("wq", 0, 512)], [])
            dma("s", T.wqs[:, :], T.ws[:, :], [A("wqs", 0, 512)], [])
        if rd == 1:
            dma("s", T.vt[:, :], T.v[:, :], [A("vt", 0, 512)], [])
        num, sign = L(0), A("sg", 3, 80, 4)
        steps = [lambda: ts(L(16), num, col(27), None, Op.add),
                 lambda: ts(L(13), num, 9, None, Op.arith_shift_right),
                 lambda: ts(L(17), L(16), 6, 7, Op.arith_shift_right, Op.bitwise_and),
                 lambda: tt(LF(1), LF(0), L(13), Op.add),
                 lambda: ts(LF(2), L(17), 160.0, None, Op.mult),
                 lambda: tt(LF(3), LF(1), LF(2), Op.add),
                 lambda: copy(A("wl", 0, 20), LF(3))]
        if rd == ROUNDS - 1:
            steps[2:2] = [lambda: ts(L(18), num, 6, None, Op.arith_shift_right),
                          lambda: ts(LF(4), sign, -1408.0, -128.0, Op.mult, Op.add)]
            steps += [lambda: tt(A("vf", 0, 20), L(18), LF(4), Op.add),
                      lambda: turn32(A("vtr", 0, 32), A("vf", 0, 32))]

        def meanwhile(k):
            for step in steps[:k]:
                step()
            del steps[:k]

        once(1)
        tt(A("n2f", 0, 20), A("su", 3, 80, 4), sign, Op.mult)
        ts(A("r1", 0, 80), A("st", 7, 87), col(36), col(38), Op.mult, Op.add)
        ts(LF(0), sign, -736.0, 544.0, Op.mult, Op.add)
        tt(num, A("n2f", 0, 20), A("pl", 0, 20), Op.add)
        ts(A("dg", 0, 80), A("r1", 0, 80), 15 * 256, None, Op.bitwise_and)
        ts(L(1), num, 6, 7 * 512, Op.arith_shift_right, Op.bitwise_and)
        ts(L(2), num, 13, 3, Op.arith_shift_right, Op.bitwise_and)
        ts(L(3), num, 7 * 64, None, Op.bitwise_and)
        ts(L(4), num, 7, 15 * 4, Op.arith_shift_right, Op.bitwise_and)
        tt(A("dat", 0, 320, 4), P(4, 80), A("dg", 0, 80), Op.add)
        tt(L(5), L(1), L(2), Op.add)
        tt(A("dat", 1, 320, 4), P(5, 80), A("dg", 0, 80), Op.add)
        tt(L(6), L(3), L(4), Op.add)
        tt(A("dat", 2, 320, 4), P(3, 80), A("dg", 0, 80), Op.add)
        tt(A("dat", 3, 320, 4), P(0, 80), A("dg", 0, 80), Op.add)
        meanwhile(1)
        tt(L(9), L(5), L(6), Op.add)
        meanwhile(1)
        copy(A("pos", 0, 20), L(9))
        meanwhile(2)
        slots, lst = A("wn", 0, 3072), A("pos", 0, 20)

        def places(i, a, n):
            quant("nq", 384 * i + 128 * a, 128 * n, "wn", 1536 * i + 512 * a)
            for s in range(a, a + n):
                mm(3 + i, "nq", 384 * i + 128 * s, "ki", 12 + 20 * i - 4 * s, 128, s == 0, s == 2)

        def half(s, i):
            return A(s[0], s[1] + 10 * i, s[1] + 10 * i + 10)

        listing = [lambda i: tt(half(L(7), i), P(3 + i, 10), A("s2", 10 * i, 10 * i + 10), Op.add),
                   lambda i: ts(half(L(8), i), half(L(7), i), 3, 7 * TURN + 511, Op.arith_shift_right, Op.bitwise_and),
                   lambda i: copy(A("off", 10 * i, 10 * i + 10), half(L(8), i))]
        emit("v", lambda: g.vector.tensor_copy(ap(slots).indirect(ap(lst)), T.dat[:, 0:320]), [slots], [lst, A("dat", 0, 320)])
        if rd == 0:
            quant("ki", 0, 160, "cci", 0)
        else:
            meanwhile(1)
        places(0, 0, 2)
        places(0, 2, 1)
        places(1, 0, 2)
        meanwhile(1)
        listing[0](0)
        places(1, 2, 1)
        listing[1](0)
        meanwhile(1)
        listing[2](0)
        listing[0](1)
        for b in range(4):
            gather("va"[b % 2], A("gt", b, 640, 4), TW(b), A("off", 0, 10))
            if b % 2 == 0:
                listing[1 + b // 2](1)
        quant("gq", 0, H, "gt", 0)
        send(dst, "gq", "gl%d" % rd, "ga%d" % rd, "gs%d" % rd)
        for b in range(4):
            gather("avav"[b], A("ft", b, 640, 4), TW(b), A("off", 10, 20))
        quant("fqq", 0, H, "ft", 0)
        if rd == 1:
            quant("vq", 0, 128, "vt", 0)
        layer("fqq", "at", 0)
        quant("aq", 0, H, "at", 0)
        layer("gl%d" % rd, "bt", 4)
        quant("bq", 0, H, "bt", 0)
        send(dst, "bq", "bl%d" % rd, "ba%d" % rd, "bs%d" % rd)
        if rd < ROUNDS - 1:
            iota(A("wn", 0, 3072), [[0, 3072]], 0, 0)
        meanwhile(len(steps))
        for k in range(16):
            b = ([int(e) for e in B_PLAN if e.isdigit()] + list(LAST))[k // 4]
            unpack("aq", b, k % 4, k % 8, A_OUT[k], 0)
            if k % 4 == 3:
                halves("s", b, 0)
        k = bank = 0
        for q in B_PLAN:
            if q in "va":
                unpack("bl%d" % rd, k // 8, k % 8, bank % 8, q, 1)
                k, bank = k + 1, bank + 1
            elif q == ">":
                halves("s", k // 8, 1)
                k += 4
            else:
                splice(int(q), 0, C)
        e, f = LAST
        for a in (H, 0):
            mm(6 + a // H, "er", 240 * f, "xq", a, H)
            gather("a", A("sv", a, a + H), A("wv", 2560 * f, 2560 * f + 2560), A("wl", a // 16, (a + H) // 16))
        splice(e, H, H)
        tt(A("xn", 4 * H + f, 4 * C, 4), P(7, H), A("sv", H, C), Op.add)
        splice(e, 0, H)
        if rd < ROUNDS - 1:
            turn_high("xn")
        else:
            quant("xq", H, H, "xn", 4 * H)
            mm(1, "vq", 0, "xq", H, H)
        tt(A("xn", f, 4 * H, 4), P(6, H), A("sv", 0, H), Op.add)

    dmas("s", [(T.op[k:k + 1, :], T.vtr[32 * (k // 2):32 * (k // 2) + 20, 16 * (k % 2):16 * (k % 2) + 16]) for k in range(8)], [], [A("vtr", 0, 32)])
    dma("s", T.oc[:, 4 * H:4 * C], T.xq[:, H:C].bitcast(dt.uint8), [], [A("xq", H, C)])
    act(A("yo", H, C), P(1, H), Fn.Copy)
    dma("a", T.y[:, H:C], T.yo[:, H:C], [], [A("yo", H, C)])
    quant("xq", 0, H, "xn", 0)
    mm(0, "vq", 0, "xq", 0, H)
    dma("s", T.oc[:, 0:4 * H], T.xq[:, 0:H].bitcast(dt.uint8), [], [A("xq", 0, H)])
    copy(A("yo", 0, H), P(0, H))
    for k in range(4):
        dma("sa"[k % 2], T.osc[4 * k:4 * k + 4, :], T.xqs[32 * k:32 * k + 4, 0:C], [], [A("xqs", 0, C)])
    dma("s", T.y[:, 0:H], T.yo[:, 0:H], [], [A("yo", 0, H)])
    for s in sorted(final):
        if known["p"].get(s, 0) < final[s]:
            g.wait_ge(T.sem[s], final[s])
